import numpy as np
import ml_dtypes


def mxq(x, axis, fmt="e4m3"):
    dtype, down = {"e4m3": (ml_dtypes.float8_e4m3fn, 7), "e5m2": (ml_dtypes.float8_e5m2, 14)}[fmt]
    v = np.moveaxis(np.asarray(x, np.float32).astype(ml_dtypes.bfloat16).astype(np.float64), axis, -1)
    blocks = v.reshape(v.shape[:-1] + (-1, 32))
    amax = np.abs(blocks).max(-1, keepdims=True)
    byte = np.maximum(np.where(amax > 0, np.frexp(amax)[1] - 1 + 127, 0) - down, 1)
    scale = np.exp2(byte - 127.0)
    codes = (blocks / scale).astype(np.float32).astype(dtype).astype(np.float64)
    return np.moveaxis((codes * scale).reshape(v.shape), -1, axis)


WIDE = False


def mx_kscale(k):
    if not WIDE:
        return np.ones(k)
    levels = np.array([10, -10, 5, -5, 0])
    if k % 512:
        return np.exp2(np.random.permutation(np.resize(levels, k // 32))).repeat(32)
    a = np.empty((k // 512, 16))
    for p in range(k // 512):
        a[p, :8] = np.random.permutation(np.resize(levels, 8))
        for g in range(8):
            far = levels[np.abs(levels - a[p, g]) >= 10]
            a[p, g + 8] = far[np.random.randint(len(far))]
    return np.exp2(a.ravel()).repeat(32)


def f64(x):
    return np.asarray(x).astype(np.float64)


def striped(idx):
    return np.tile(idx.reshape(-1, 16).T, (8, 1)).astype(np.uint16)


def unstriped(offs):
    return offs[:16].T.reshape(-1).astype(np.int64)


def striped8(idx):
    return np.concatenate([x.reshape(-1, 16).T for x in idx]).astype(np.uint16)


def runs(offs, k):
    lists = np.stack([offs[16 * r : 16 * r + 16].T.reshape(-1) for r in range(8)]).astype(np.int64)
    return lists[np.arange(k) % 512 // 64]


def pack_weight(w):
    k, n = w.shape
    w = f64(np.asarray(w, np.float32).astype(ml_dtypes.bfloat16)).reshape(k // 32, 32, n)
    amax = np.abs(w).max(1)
    byte = np.clip(np.where(amax > 0, np.frexp(amax)[1] - 1 + 127 - 7, 1), 1, 254)
    scaled = (w * np.exp2(127.0 - byte)[:, None, :]).reshape(k, n).astype(np.float32)
    words = np.ascontiguousarray(scaled.reshape(k // 512, 128, 4, n).transpose(0, 1, 3, 2)).astype(ml_dtypes.float8_e4m3fn).view(np.uint8)
    return words, np.ascontiguousarray(byte.astype(np.uint8).reshape(k // 512, 16, n))


def unpack_weight(words, scales):
    g, p, n, _ = words.shape
    vals = np.ascontiguousarray(words).view(ml_dtypes.float8_e4m3fn).astype(np.float64) * np.repeat(np.exp2(scales.astype(np.float64) - 127.0), 8, axis=1)[..., None]
    return vals.transpose(0, 1, 3, 2).reshape(g * 512, n)

def planes(y):
    n, m = y.shape
    v = y.astype(np.float32).astype(ml_dtypes.bfloat16).astype(np.float64).reshape(n // 32, 32, m)
    top = np.abs(v).max(1)
    byte = np.clip(np.where(top > 0, np.frexp(top)[1] - 1 + 127 - 7, 1), 1, 254)
    codes = (v * np.exp2(127.0 - byte)[:, None, :]).reshape(n, m).astype(np.float32).astype(ml_dtypes.float8_e4m3fn).view(np.uint8)
    words = codes.reshape(n // 512, 128, 4, m).transpose(0, 1, 3, 2)
    return np.ascontiguousarray(words), np.ascontiguousarray(byte.astype(np.uint8).reshape(n // 512, 16, m))


K, T, S, N, U = 512, 2048, 512, 512, 1024


def setup_inputs():
    n = np.random.standard_normal
    s = mx_kscale(K)[:, None]
    packed_xT = pack_weight(n((K, T)) * s)
    return {
        "x_words": packed_xT[0],
        "x_scales": packed_xT[1],
        "w1": (n((K, N)) / np.sqrt(K) / s).astype(np.float32),
        "st": n((N, U)).astype(np.float32),
        "va": np.random.uniform(0.2, 2.0, (N, U)).astype(np.float32),
        "offs": striped(np.random.permutation(T)[:S]),
        "trk": striped8(np.stack([np.random.permutation(U)[:S] for _ in range(8)])),
    }


def reference(x_words, x_scales, w1, st, va, offs, trk):
    so = f64(st)[np.arange(N)[:, None], runs(trk, N)]
    po = f64(va)[np.arange(N)[:, None], runs(trk, N)]
    kg = po / (po + 0.5)
    xq = unpack_weight(x_words, x_scales)[:, unstriped(offs)]
    y = mxq(f64(w1), 0, "e4m3").T @ xq
    sn = so + kg * (y - so)
    out = f64(st).copy()
    out[np.arange(N)[:, None], runs(trk, N)] = sn
    return (out,) + planes(out)

@@ -1,0 +1,147 @@
+from contextlib import ExitStack
+
+import concourse.mybir as mybir
+
+K, T, S, N, U = 512, 2048, 512, 512, 1024
+FLOPS = 2 * K * S * N
+
+F32 = mybir.dt.float32
+BF16 = mybir.dt.bfloat16
+I32 = mybir.dt.int32
+U32 = mybir.dt.uint32
+U16 = mybir.dt.uint16
+U8 = mybir.dt.uint8
+FP8X4 = mybir.dt.float8_e4m3fn_x4
+ALU = mybir.AluOpType
+ACT = mybir.ActivationFunctionType
+
+P = 128
+PACK = 4
+HALF = U // 2
+
+
+def tile_picked_kalman8_none_po_kernel(
+    tc, x_words, x_scales, w1, st, va, offs, trk, out_0, out_1, out_2
+):
+    nc = tc.nc
+    st_rows = st.rearrange("(p t) u -> p t u", t=PACK)
+    va_rows = va.rearrange("(p t) u -> p t u", t=PACK)
+    out_rows = out_0.rearrange("(p t) u -> p t u", t=PACK)
+
+    with ExitStack() as ctx:
+        keep = ctx.enter_context(tc.tile_pool(name="keep", bufs=1))
+        psum = ctx.enter_context(tc.psum_pool(name="psum", bufs=1))
+
+        trk_sb = keep.tile([P, S // 16], U16, name="trk_sb")
+        offs_sb = keep.tile([P, S // 16], U16, name="offs_sb")
+        x_table = keep.tile([P, T], I32, name="x_table", align_bytes=64)
+        scale_table = keep.tile([P, T], U8, name="scale_table", align_bytes=64)
+        w_raw = keep.tile([P, PACK, N], F32, name="w_raw")
+        state = [keep.tile([P, U], F32, name=f"state{t}") for t in range(PACK)]
+        var = [keep.tile([P, U], F32, name=f"var{t}", tag=f"var{t}") for t in range(PACK)]
+
+        nc.vector.memset(scale_table[:].bitcast(I32), 0)
+        nc.sync.dma_start(trk_sb[:], trk)
+        nc.sync.dma_start(offs_sb[:], offs)
+        nc.sync.dma_start(var[0][:], va_rows[:, 0, :])
+        nc.sync.dma_start(var[1][:], va_rows[:, 1, :])
+        for q in range(4):
+            nc.sync.dma_start(
+                scale_table[32 * q : 32 * q + 4, :].bitcast(I32),
+                x_scales[0, 4 * q : 4 * q + 4, :].bitcast(I32),
+            )
+        nc.sync.dma_start(w_raw[:], w1.rearrange("(p j) c -> p j c", j=PACK))
+        nc.sync.dma_start(x_table[:], x_words[0].rearrange("p c r -> p (c r)").bitcast(I32))
+        nc.sync.dma_start(state[0][:], st_rows[:, 0, :])
+        nc.sync.dma_start(state[1][:], st_rows[:, 1, :])
+        nc.sync.dma_start(var[2][:], va_rows[:, 2, :])
+        nc.sync.dma_start(var[3][:], va_rows[:, 3, :])
+        nc.sync.dma_start(state[2][:], st_rows[:, 2, :])
+        nc.sync.dma_start(state[3][:], st_rows[:, 3, :])
+
+        keepfrac = {}
+
+        def gains(pair):
+            logs = []
+            for i, t in enumerate(pair):
+                lg = keep.tile([P, U], F32, name=f"log{t}", tag=f"log{(i + t // 2) % 2}", align_bytes=64)
+                nc.scalar.activation(lg[:], var[t][:], ACT.Ln, bias=1.0, scale=2.0)
+                logs.append(lg)
+            for i, t in enumerate(pair):
+                r = keep.tile([P, S], F32, name=f"keepfrac{t}", tag=f"var{pair[1 - i]}")
+                nc.scalar.activation(r[:], logs[i][:].indirect(trk_sb[:]), ACT.Exp, scale=-1.0)
+                keepfrac[t] = r
+
+        gains((0, 1))
+
+        x_scale = keep.tile([P, S], U8, name="x_scale", align_bytes=64)
+        nc.vector.tensor_copy(x_scale[:], scale_table[:].indirect(offs_sb[:]))
+
+        w_bf = keep.tile([P, N * PACK], BF16, name="w_bf", align_bytes=64)
+        nc.vector.tensor_scalar(
+            w_bf[:].rearrange("p (t m j) -> p m t j", t=PACK, j=PACK),
+            w_raw[:].rearrange("p j (m t) -> p m t j", t=PACK),
+            -1.0,
+            None,
+            ALU.mult,
+        )
+        w_codes = keep.tile([P, N], U32, name="w_codes", align_bytes=64)
+        w_scale = keep.tile([P, N], U8, name="w_scale", align_bytes=64)
+        nc.vector.quantize_mx(out=w_codes[:].bitcast(FP8X4), scales=w_scale[:], in_=w_bf[:])
+
+        x_codes = keep.tile([P, S], U32, name="x_codes", align_bytes=64)
+        nc.vector.tensor_copy(x_codes[:], x_table[:].bitcast(U32).indirect(offs_sb[:]))
+
+        neg_y = []
+        for t in range(PACK):
+            bank = psum.tile([P, S], F32, name=f"neg_y{t}")
+            cols = slice(t * P, (t + 1) * P)
+            nc.tensor.matmul_mx(
+                out=bank[:],
+                lhsT=w_codes[:, cols].bitcast(FP8X4),
+                lhsT_scale=w_scale[:, cols],
+                rhs=x_codes[:].bitcast(FP8X4),
+                rhs_scale=x_scale[:],
+                start=True,
+                stop=True,
+            )
+            neg_y.append(bank)
+
+        gains((2, 3))
+
+        woven = [keep.tile([P, HALF, PACK], BF16, name=f"woven{h}", tag=f"log{h}", align_bytes=64) for h in range(2)]
+        for t in range(PACK):
+            old_part = keep.tile([P, S], F32, name=f"old_part{t}")
+            new_part = keep.tile([P, S], F32, name=f"new_part{t}")
+            nc.vector.tensor_tensor(old_part[:], state[t][:].indirect(trk_sb[:]), keepfrac[t][:], ALU.mult)
+            nc.vector.scalar_tensor_tensor(
+                new_part[:], keepfrac[t][:], 1.0, neg_y[t][:], ALU.subtract, ALU.mult
+            )
+            nc.vector.tensor_tensor(state[t][:].indirect(trk_sb[:]), old_part[:], new_part[:], ALU.add)
+            nc.sync.dma_start(out_rows[:, t, :], state[t][:])
+            for h in range(2):
+                src = state[t][:, h * HALF : (h + 1) * HALF]
+                if t < PACK - 2:
+                    nc.scalar.copy(woven[h][:, :, t], src)
+                elif t == PACK - 2:
+                    nc.scalar.copy(woven[h][:, :, t:], src.unsqueeze(2).to_broadcast([P, HALF, 2]))
+
+        out_scale = keep.tile([P, U], U8, name="out_scale", align_bytes=64)
+        out_words = out_1[0].rearrange("p c r -> p (c r)").bitcast(I32)
+        for h in range(2):
+            nc.vector.tensor_copy(woven[h][:, :, PACK - 1], state[PACK - 1][:, h * HALF : (h + 1) * HALF])
+        for h in range(2):
+            cols = slice(h * HALF, (h + 1) * HALF)
+            codes = keep.tile([P, HALF], I32, name=f"out_codes{h}", align_bytes=64)
+            nc.vector.quantize_mx(
+                out=codes[:].bitcast(FP8X4),
+                scales=out_scale[:, cols],
+                in_=woven[h][:].rearrange("p c t -> p (c t)"),
+            )
+            nc.sync.dma_start(out_words[:, cols], codes[:])
+        for q in range(4):
+            queue = nc.sync if q % 2 == 0 else nc.scalar
+            queue.dma_start(
+                out_2[0, 4 * q : 4 * q + 4, :].bitcast(I32),
+                out_scale[32 * q : 32 * q + 4, :].bitcast(I32),
+            )

@@ -18,6 +18,7 @@ ACT = mybir.ActivationFunctionType
 P = 128
 PACK = 4
 HALF = U // 2
+QUARTER = U // 4
 
 
 def tile_picked_kalman8_none_po_kernel(
@@ -67,10 +68,10 @@ def tile_picked_kalman8_none_po_kernel(
                 lg = keep.tile([P, U], F32, name=f"log{t}", tag=f"log{(i + t // 2) % 2}", align_bytes=64)
                 nc.scalar.activation(lg[:], var[t][:], ACT.Ln, bias=1.0, scale=2.0)
                 logs.append(lg)
+            both = keep.tile([P, 2 * S], F32, name=f"keepfrac{pair[0]}", tag=f"var{pair[1]}")
             for i, t in enumerate(pair):
-                r = keep.tile([P, S], F32, name=f"keepfrac{t}", tag=f"var{pair[1 - i]}")
-                nc.scalar.activation(r[:], logs[i][:].indirect(trk_sb[:]), ACT.Exp, scale=-1.0)
-                keepfrac[t] = r
+                keepfrac[t] = both[:, i * S : (i + 1) * S]
+                nc.scalar.activation(keepfrac[t], logs[i][:].indirect(trk_sb[:]), ACT.Exp, scale=-1.0)
 
         gains((0, 1))
 
@@ -109,36 +110,50 @@ def tile_picked_kalman8_none_po_kernel(
 
         gains((2, 3))
 
-        woven = [keep.tile([P, HALF, PACK], BF16, name=f"woven{h}", tag=f"log{h}", align_bytes=64) for h in range(2)]
-        for t in range(PACK):
-            old_part = keep.tile([P, S], F32, name=f"old_part{t}")
-            new_part = keep.tile([P, S], F32, name=f"new_part{t}")
-            nc.vector.tensor_tensor(old_part[:], state[t][:].indirect(trk_sb[:]), keepfrac[t][:], ALU.mult)
-            nc.vector.scalar_tensor_tensor(
-                new_part[:], keepfrac[t][:], 1.0, neg_y[t][:], ALU.subtract, ALU.mult
-            )
-            nc.vector.tensor_tensor(state[t][:].indirect(trk_sb[:]), old_part[:], new_part[:], ALU.add)
+        woven_all = keep.tile([P, U, PACK], BF16, name="woven", tag="log0", align_bytes=64)
+        woven = [woven_all[:, h * HALF : (h + 1) * HALF, :] for h in range(2)]
+        old_part = {}
+
+        def weigh(t):
+            old_part[t] = keep.tile([P, S], F32, name=f"old_part{t}")
+            nc.vector.tensor_tensor(old_part[t][:], state[t][:].indirect(trk_sb[:]), keepfrac[t], ALU.mult)
+            nc.vector.scalar_tensor_tensor(keepfrac[t], keepfrac[t], 1.0, neg_y[t][:], ALU.subtract, ALU.mult)
+
+        def put_back(t):
+            nc.vector.tensor_tensor(state[t][:].indirect(trk_sb[:]), old_part[t][:], keepfrac[t], ALU.add)
             nc.sync.dma_start(out_rows[:, t, :], state[t][:])
-            for h in range(2):
-                src = state[t][:, h * HALF : (h + 1) * HALF]
-                if t < PACK - 2:
-                    nc.scalar.copy(woven[h][:, :, t], src)
-                elif t == PACK - 2:
-                    nc.scalar.copy(woven[h][:, :, t:], src.unsqueeze(2).to_broadcast([P, HALF, 2]))
+            if t < PACK - 2:
+                nc.scalar.copy(woven_all[:, :, t], state[t][:])
+            elif t == PACK - 2:
+                nc.scalar.copy(woven[0][:, :, t:], state[t][:, :HALF].unsqueeze(2).to_broadcast([P, HALF, 2]))
+                nc.scalar.copy(woven[1][:, :, t], state[t][:, HALF:])
+            else:
+                for c in range(4):
+                    cols = slice(c * QUARTER, (c + 1) * QUARTER)
+                    if c < 2:
+                        nc.vector.tensor_copy(woven_all[:, cols, t], state[t][:, cols])
+                    else:
+                        nc.scalar.copy(woven_all[:, cols, t], state[t][:, cols])
+
+        for pair in ((0, 1), (2, 3)):
+            for t in pair:
+                weigh(t)
+            for t in pair:
+                put_back(t)
 
         out_scale = keep.tile([P, U], U8, name="out_scale", align_bytes=64)
+        out_codes = keep.tile([P, U], I32, name="out_codes", align_bytes=64)
         out_words = out_1[0].rearrange("p c r -> p (c r)").bitcast(I32)
-        for h in range(2):
-            nc.vector.tensor_copy(woven[h][:, :, PACK - 1], state[PACK - 1][:, h * HALF : (h + 1) * HALF])
-        for h in range(2):
-            cols = slice(h * HALF, (h + 1) * HALF)
-            codes = keep.tile([P, HALF], I32, name=f"out_codes{h}", align_bytes=64)
+        for c in range(4):
+            cols = slice(c * QUARTER, (c + 1) * QUARTER)
             nc.vector.quantize_mx(
-                out=codes[:].bitcast(FP8X4),
+                out=out_codes[:, cols].bitcast(FP8X4),
                 scales=out_scale[:, cols],
-                in_=woven[h][:].rearrange("p c t -> p (c t)"),
+                in_=woven_all[:, cols, :].rearrange("p c t -> p (c t)"),
             )
-            nc.sync.dma_start(out_words[:, cols], codes[:])
+            if c > 0:
+                stored = slice(0, HALF) if c == 1 else cols
+                nc.sync.dma_start(out_words[:, stored], out_codes[:, stored])
         for q in range(4):
             queue = nc.sync if q % 2 == 0 else nc.scalar
             queue.dma_start(

@@ -37,7 +37,7 @@ def tile_picked_kalman8_none_po_kernel(
         offs_sb = keep.tile([P, S // 16], U16, name="offs_sb")
         x_table = keep.tile([P, T], I32, name="x_table", align_bytes=64)
         scale_table = keep.tile([P, T], U8, name="scale_table", align_bytes=64)
-        w_raw = keep.tile([P, PACK, N], F32, name="w_raw")
+        w_raw = [keep.tile([P, 2, N], F32, name=f"w_raw{h}") for h in range(2)]
         state = [keep.tile([P, U], F32, name=f"state{t}") for t in range(PACK)]
         var = [keep.tile([P, U], F32, name=f"var{t}", tag=f"var{t}") for t in range(PACK)]
 
@@ -51,7 +51,9 @@ def tile_picked_kalman8_none_po_kernel(
                 scale_table[32 * q : 32 * q + 4, :].bitcast(I32),
                 x_scales[0, 4 * q : 4 * q + 4, :].bitcast(I32),
             )
-        nc.sync.dma_start(w_raw[:], w1.rearrange("(p j) c -> p j c", j=PACK))
+        w_rows = w1.rearrange("(p j) c -> p j c", j=PACK)
+        for h in range(2):
+            nc.sync.dma_start(w_raw[h][:], w_rows[:, 2 * h : 2 * h + 2, :])
         nc.sync.dma_start(x_table[:], x_words[0].rearrange("p c r -> p (c r)").bitcast(I32))
         nc.sync.dma_start(state[0][:], st_rows[:, 0, :])
         nc.sync.dma_start(state[1][:], st_rows[:, 1, :])
@@ -79,13 +81,15 @@ def tile_picked_kalman8_none_po_kernel(
         nc.vector.tensor_copy(x_scale[:], scale_table[:].indirect(offs_sb[:]))
 
         w_bf = keep.tile([P, N * PACK], BF16, name="w_bf", align_bytes=64)
-        nc.vector.tensor_scalar(
-            w_bf[:].rearrange("p (t m j) -> p m t j", t=PACK, j=PACK),
-            w_raw[:].rearrange("p j (m t) -> p m t j", t=PACK),
-            -1.0,
-            None,
-            ALU.mult,
-        )
+        w_dealt = w_bf[:].rearrange("p (t m j) -> p m t j", t=PACK, j=PACK)
+        for h in range(2):
+            nc.vector.tensor_scalar(
+                w_dealt[:, :, :, 2 * h : 2 * h + 2],
+                w_raw[h][:].rearrange("p j (m t) -> p m t j", t=PACK),
+                -1.0,
+                None,
+                ALU.mult,
+            )
         w_codes = keep.tile([P, N], U32, name="w_codes", align_bytes=64)
         w_scale = keep.tile([P, N], U8, name="w_scale", align_bytes=64)
         nc.vector.quantize_mx(out=w_codes[:].bitcast(FP8X4), scales=w_scale[:], in_=w_bf[:])
@@ -108,19 +112,23 @@ def tile_picked_kalman8_none_po_kernel(
             )
             neg_y.append(bank)
 
+        warm = keep.tile([P, 8], F32, name="warm")
+        nc.scalar.activation(warm[:, 0:1], keepfrac[1][:, 0:1], ACT.Ln, bias=1.0, scale=2.0)
         gains((2, 3))
 
         woven_all = keep.tile([P, U, PACK], BF16, name="woven", tag="log0", align_bytes=64)
         woven = [woven_all[:, h * HALF : (h + 1) * HALF, :] for h in range(2)]
         old_part = {}
+        new_part = {}
 
         def weigh(t):
             old_part[t] = keep.tile([P, S], F32, name=f"old_part{t}")
             nc.vector.tensor_tensor(old_part[t][:], state[t][:].indirect(trk_sb[:]), keepfrac[t], ALU.mult)
-            nc.vector.scalar_tensor_tensor(keepfrac[t], keepfrac[t], 1.0, neg_y[t][:], ALU.subtract, ALU.mult)
+            new_part[t] = keepfrac[t] if t < 2 else keep.tile([P, S], F32, name=f"new_part{t}")[:]
+            nc.vector.scalar_tensor_tensor(new_part[t], keepfrac[t], 1.0, neg_y[t][:], ALU.subtract, ALU.mult)
 
         def put_back(t):
-            nc.vector.tensor_tensor(state[t][:].indirect(trk_sb[:]), old_part[t][:], keepfrac[t], ALU.add)
+            nc.vector.tensor_tensor(state[t][:].indirect(trk_sb[:]), old_part[t][:], new_part[t], ALU.add)
             nc.sync.dma_start(out_rows[:, t, :], state[t][:])
             if t < PACK - 2:
                 nc.scalar.copy(woven_all[:, :, t], state[t][:])

@@ -37,7 +37,7 @@ def tile_picked_kalman8_none_po_kernel(
         offs_sb = keep.tile([P, S // 16], U16, name="offs_sb")
         x_table = keep.tile([P, T], I32, name="x_table", align_bytes=64)
         scale_table = keep.tile([P, T], U8, name="scale_table", align_bytes=64)
-        w_raw = [keep.tile([P, 2, N], F32, name=f"w_raw{h}") for h in range(2)]
+        w_raw = keep.tile([P, PACK, N], F32, name="w_raw")
         state = [keep.tile([P, U], F32, name=f"state{t}") for t in range(PACK)]
         var = [keep.tile([P, U], F32, name=f"var{t}", tag=f"var{t}") for t in range(PACK)]
 
@@ -46,14 +46,10 @@ def tile_picked_kalman8_none_po_kernel(
         nc.sync.dma_start(offs_sb[:], offs)
         nc.sync.dma_start(var[0][:], va_rows[:, 0, :])
         nc.sync.dma_start(var[1][:], va_rows[:, 1, :])
-        for q in range(4):
-            nc.sync.dma_start(
-                scale_table[32 * q : 32 * q + 4, :].bitcast(I32),
-                x_scales[0, 4 * q : 4 * q + 4, :].bitcast(I32),
-            )
+        for r in range(4):
+            nc.sync.dma_start(scale_table[r:P:32, :].bitcast(I32), x_scales[0, r:16:4, :].bitcast(I32))
         w_rows = w1.rearrange("(p j) c -> p j c", j=PACK)
-        for h in range(2):
-            nc.sync.dma_start(w_raw[h][:], w_rows[:, 2 * h : 2 * h + 2, :])
+        nc.sync.dma_start(w_raw[:], w_rows)
         nc.sync.dma_start(x_table[:], x_words[0].rearrange("p c r -> p (c r)").bitcast(I32))
         nc.sync.dma_start(state[0][:], st_rows[:, 0, :])
         nc.sync.dma_start(state[1][:], st_rows[:, 1, :])
@@ -82,14 +78,7 @@ def tile_picked_kalman8_none_po_kernel(
 
         w_bf = keep.tile([P, N * PACK], BF16, name="w_bf", align_bytes=64)
         w_dealt = w_bf[:].rearrange("p (t m j) -> p m t j", t=PACK, j=PACK)
-        for h in range(2):
-            nc.vector.tensor_scalar(
-                w_dealt[:, :, :, 2 * h : 2 * h + 2],
-                w_raw[h][:].rearrange("p j (m t) -> p m t j", t=PACK),
-                -1.0,
-                None,
-                ALU.mult,
-            )
+        nc.vector.tensor_scalar(w_dealt, w_raw[:].rearrange("p j (m t) -> p m t j", t=PACK), -1.0, None, ALU.mult)
         w_codes = keep.tile([P, N], U32, name="w_codes", align_bytes=64)
         w_scale = keep.tile([P, N], U8, name="w_scale", align_bytes=64)
         nc.vector.quantize_mx(out=w_codes[:].bitcast(FP8X4), scales=w_scale[:], in_=w_bf[:])
@@ -118,6 +107,8 @@ def tile_picked_kalman8_none_po_kernel(
 
         woven_all = keep.tile([P, U, PACK], BF16, name="woven", tag="log0", align_bytes=64)
         woven = [woven_all[:, h * HALF : (h + 1) * HALF, :] for h in range(2)]
+        edges = (0, QUARTER, HALF, 3 * QUARTER, U - QUARTER // 2, U)
+        chunks = [slice(lo, hi) for lo, hi in zip(edges, edges[1:])]
         old_part = {}
         new_part = {}
 
@@ -136,8 +127,7 @@ def tile_picked_kalman8_none_po_kernel(
                 nc.scalar.copy(woven[0][:, :, t:], state[t][:, :HALF].unsqueeze(2).to_broadcast([P, HALF, 2]))
                 nc.scalar.copy(woven[1][:, :, t], state[t][:, HALF:])
             else:
-                for c in range(4):
-                    cols = slice(c * QUARTER, (c + 1) * QUARTER)
+                for c, cols in enumerate(chunks):
                     if c < 2:
                         nc.vector.tensor_copy(woven_all[:, cols, t], state[t][:, cols])
                     else:
@@ -152,19 +142,15 @@ def tile_picked_kalman8_none_po_kernel(
         out_scale = keep.tile([P, U], U8, name="out_scale", align_bytes=64)
         out_codes = keep.tile([P, U], I32, name="out_codes", align_bytes=64)
         out_words = out_1[0].rearrange("p c r -> p (c r)").bitcast(I32)
-        for c in range(4):
-            cols = slice(c * QUARTER, (c + 1) * QUARTER)
+        for c, cols in enumerate(chunks):
             nc.vector.quantize_mx(
                 out=out_codes[:, cols].bitcast(FP8X4),
                 scales=out_scale[:, cols],
                 in_=woven_all[:, cols, :].rearrange("p c t -> p (c t)"),
             )
-            if c > 0:
-                stored = slice(0, HALF) if c == 1 else cols
+            if c in (1, 3, 4):
+                stored = slice(edges[c - 1], edges[c + 1]) if c < 4 else cols
                 nc.sync.dma_start(out_words[:, stored], out_codes[:, stored])
-        for q in range(4):
-            queue = nc.sync if q % 2 == 0 else nc.scalar
-            queue.dma_start(
-                out_2[0, 4 * q : 4 * q + 4, :].bitcast(I32),
-                out_scale[32 * q : 32 * q + 4, :].bitcast(I32),
-            )
+        for r in range(4):
+            queue = nc.sync if r % 2 == 0 else nc.scalar
+            queue.dma_start(out_2[0, r:16:4, :].bitcast(I32), out_scale[r:P:32, :].bitcast(I32))

@@ -46,8 +46,7 @@ def tile_picked_kalman8_none_po_kernel(
         nc.sync.dma_start(offs_sb[:], offs)
         nc.sync.dma_start(var[0][:], va_rows[:, 0, :])
         nc.sync.dma_start(var[1][:], va_rows[:, 1, :])
-        for r in range(4):
-            nc.sync.dma_start(scale_table[r:P:32, :].bitcast(I32), x_scales[0, r:16:4, :].bitcast(I32))
+        nc.sync.dma_start(scale_table[0:P:8, :].bitcast(I32), x_scales[0].bitcast(I32))
         w_rows = w1.rearrange("(p j) c -> p j c", j=PACK)
         nc.sync.dma_start(w_raw[:], w_rows)
         nc.sync.dma_start(x_table[:], x_words[0].rearrange("p c r -> p (c r)").bitcast(I32))
@@ -73,8 +72,12 @@ def tile_picked_kalman8_none_po_kernel(
 
         gains((0, 1))
 
+        picked_scale = keep.tile([P, S], U8, name="picked_scale", align_bytes=64)
+        nc.vector.tensor_copy(picked_scale[:], scale_table[:].indirect(offs_sb[:]))
         x_scale = keep.tile([P, S], U8, name="x_scale", align_bytes=64)
-        nc.vector.tensor_copy(x_scale[:], scale_table[:].indirect(offs_sb[:]))
+        nc.vector.memset(x_scale[:].bitcast(I32), 0)
+        for r in range(4):
+            nc.scalar.dma_start(x_scale[r:P:32, :].bitcast(I32), picked_scale[8 * r : P : 32, :].bitcast(I32))
 
         w_bf = keep.tile([P, N * PACK], BF16, name="w_bf", align_bytes=64)
         w_dealt = w_bf[:].rearrange("p (t m j) -> p m t j", t=PACK, j=PACK)

@@ -17,8 +17,12 @@ ACT = mybir.ActivationFunctionType
 
 P = 128
 PACK = 4
+QUADRANT = 32
+SCALE_ROWS = 16
+SPREAD = P // SCALE_ROWS
 HALF = U // 2
 QUARTER = U // 4
+EDGES = (0, QUARTER, HALF, 3 * QUARTER, U - QUARTER // 2, U)
 
 
 def tile_picked_kalman8_none_po_kernel(
@@ -38,26 +42,22 @@ def tile_picked_kalman8_none_po_kernel(
         x_table = keep.tile([P, T], I32, name="x_table", align_bytes=64)
         scale_table = keep.tile([P, T], U8, name="scale_table", align_bytes=64)
         w_raw = keep.tile([P, PACK, N], F32, name="w_raw")
-        state = [keep.tile([P, U], F32, name=f"state{t}") for t in range(PACK)]
-        var = [keep.tile([P, U], F32, name=f"var{t}", tag=f"var{t}") for t in range(PACK)]
+        state = {t: keep.tile([P, U], F32, name=f"state{t}") for t in range(2)}
+        var = {t: keep.tile([P, U], F32, name=f"var{t}", tag=f"var{t}") for t in range(2)}
+        var_slot = {1: "var1", 3: "var0"}
 
         nc.vector.memset(scale_table[:].bitcast(I32), 0)
         nc.sync.dma_start(trk_sb[:], trk)
         nc.sync.dma_start(offs_sb[:], offs)
         nc.sync.dma_start(var[0][:], va_rows[:, 0, :])
         nc.sync.dma_start(var[1][:], va_rows[:, 1, :])
-        nc.sync.dma_start(scale_table[0:P:8, :].bitcast(I32), x_scales[0].bitcast(I32))
-        w_rows = w1.rearrange("(p j) c -> p j c", j=PACK)
-        nc.sync.dma_start(w_raw[:], w_rows)
+        nc.sync.dma_start(scale_table[0:P:SPREAD, :].bitcast(I32), x_scales[0].bitcast(I32))
+        nc.sync.dma_start(w_raw[:], w1.rearrange("(p j) c -> p j c", j=PACK))
         nc.sync.dma_start(x_table[:], x_words[0].rearrange("p c r -> p (c r)").bitcast(I32))
         nc.sync.dma_start(state[0][:], st_rows[:, 0, :])
         nc.sync.dma_start(state[1][:], st_rows[:, 1, :])
-        nc.sync.dma_start(var[2][:], va_rows[:, 2, :])
-        nc.sync.dma_start(var[3][:], va_rows[:, 3, :])
-        nc.sync.dma_start(state[2][:], st_rows[:, 2, :])
-        nc.sync.dma_start(state[3][:], st_rows[:, 3, :])
 
-        keepfrac = {}
+        stay = {}
 
         def gains(pair):
             logs = []
@@ -65,10 +65,10 @@ def tile_picked_kalman8_none_po_kernel(
                 lg = keep.tile([P, U], F32, name=f"log{t}", tag=f"log{(i + t // 2) % 2}", align_bytes=64)
                 nc.scalar.activation(lg[:], var[t][:], ACT.Ln, bias=1.0, scale=2.0)
                 logs.append(lg)
-            both = keep.tile([P, 2 * S], F32, name=f"keepfrac{pair[0]}", tag=f"var{pair[1]}")
+            both = keep.tile([P, 2 * S], F32, name=f"stay{pair[0]}", tag=var_slot[pair[1]])
             for i, t in enumerate(pair):
-                keepfrac[t] = both[:, i * S : (i + 1) * S]
-                nc.scalar.activation(keepfrac[t], logs[i][:].indirect(trk_sb[:]), ACT.Exp, scale=-1.0)
+                stay[t] = both[:, i * S : (i + 1) * S]
+                nc.scalar.activation(stay[t], logs[i][:].indirect(trk_sb[:]), ACT.Exp, scale=-1.0)
 
         gains((0, 1))
 
@@ -76,18 +76,30 @@ def tile_picked_kalman8_none_po_kernel(
         nc.vector.tensor_copy(picked_scale[:], scale_table[:].indirect(offs_sb[:]))
         x_scale = keep.tile([P, S], U8, name="x_scale", align_bytes=64)
         nc.vector.memset(x_scale[:].bitcast(I32), 0)
-        for r in range(4):
-            nc.scalar.dma_start(x_scale[r:P:32, :].bitcast(I32), picked_scale[8 * r : P : 32, :].bitcast(I32))
+        for r in range(SCALE_ROWS * QUADRANT // P):
+            nc.sync.dma_start(
+                x_scale[r:P:QUADRANT, :].bitcast(I32), picked_scale[SPREAD * r : P : QUADRANT, :].bitcast(I32)
+            )
+
+        var[2] = keep.tile([P, U], F32, name="var2", tag="scale_table", align_bytes=64)
+        nc.sync.dma_start(var[2][:], va_rows[:, 2, :])
+        var[3] = keep.tile([P, U], F32, name="var3", tag="var0")
+        nc.sync.dma_start(var[3][:], va_rows[:, 3, :])
 
         w_bf = keep.tile([P, N * PACK], BF16, name="w_bf", align_bytes=64)
         w_dealt = w_bf[:].rearrange("p (t m j) -> p m t j", t=PACK, j=PACK)
         nc.vector.tensor_scalar(w_dealt, w_raw[:].rearrange("p j (m t) -> p m t j", t=PACK), -1.0, None, ALU.mult)
+        state[2] = keep.tile([P, U], F32, name="state2", tag="w_raw")
+        nc.sync.dma_start(state[2][:], st_rows[:, 2, :])
         w_codes = keep.tile([P, N], U32, name="w_codes", align_bytes=64)
         w_scale = keep.tile([P, N], U8, name="w_scale", align_bytes=64)
         nc.vector.quantize_mx(out=w_codes[:].bitcast(FP8X4), scales=w_scale[:], in_=w_bf[:])
 
         x_codes = keep.tile([P, S], U32, name="x_codes", align_bytes=64)
         nc.vector.tensor_copy(x_codes[:], x_table[:].bitcast(U32).indirect(offs_sb[:]))
+
+        state[3] = keep.tile([P, U], F32, name="state3", tag="x_table", align_bytes=64)
+        nc.sync.dma_start(state[3][:], st_rows[:, 3, :])
 
         neg_y = []
         for t in range(PACK):
@@ -104,37 +116,36 @@ def tile_picked_kalman8_none_po_kernel(
             )
             neg_y.append(bank)
 
-        warm = keep.tile([P, 8], F32, name="warm")
-        nc.scalar.activation(warm[:, 0:1], keepfrac[1][:, 0:1], ACT.Ln, bias=1.0, scale=2.0)
         gains((2, 3))
 
-        woven_all = keep.tile([P, U, PACK], BF16, name="woven", tag="log0", align_bytes=64)
-        woven = [woven_all[:, h * HALF : (h + 1) * HALF, :] for h in range(2)]
-        edges = (0, QUARTER, HALF, 3 * QUARTER, U - QUARTER // 2, U)
-        chunks = [slice(lo, hi) for lo, hi in zip(edges, edges[1:])]
+        woven = keep.tile([P, U, PACK], BF16, name="woven", tag="log0", align_bytes=64)
+        pieces = [slice(lo, hi) for lo, hi in zip(EDGES, EDGES[1:])]
+        first_two = keep.tile([P, 2, U], BF16, name="first_two", tag="log1", align_bytes=64)
         old_part = {}
         new_part = {}
 
         def weigh(t):
             old_part[t] = keep.tile([P, S], F32, name=f"old_part{t}")
-            nc.vector.tensor_tensor(old_part[t][:], state[t][:].indirect(trk_sb[:]), keepfrac[t], ALU.mult)
-            new_part[t] = keepfrac[t] if t < 2 else keep.tile([P, S], F32, name=f"new_part{t}")[:]
-            nc.vector.scalar_tensor_tensor(new_part[t], keepfrac[t], 1.0, neg_y[t][:], ALU.subtract, ALU.mult)
+            nc.vector.tensor_tensor(old_part[t][:], state[t][:].indirect(trk_sb[:]), stay[t], ALU.mult)
+            new_part[t] = stay[t] if t < 2 else keep.tile([P, S], F32, name=f"new_part{t}")[:]
+            nc.vector.scalar_tensor_tensor(new_part[t], stay[t], 1.0, neg_y[t][:], ALU.subtract, ALU.mult)
 
         def put_back(t):
             nc.vector.tensor_tensor(state[t][:].indirect(trk_sb[:]), old_part[t][:], new_part[t], ALU.add)
             nc.sync.dma_start(out_rows[:, t, :], state[t][:])
-            if t < PACK - 2:
-                nc.scalar.copy(woven_all[:, :, t], state[t][:])
-            elif t == PACK - 2:
-                nc.scalar.copy(woven[0][:, :, t:], state[t][:, :HALF].unsqueeze(2).to_broadcast([P, HALF, 2]))
-                nc.scalar.copy(woven[1][:, :, t], state[t][:, HALF:])
+            if t < 2:
+                nc.scalar.copy(first_two[:, t, :], state[t][:])
+                if t == 1:
+                    nc.scalar.copy(woven[:, :, 0:2], first_two[:].rearrange("p t u -> p u t"))
+            elif t == 2:
+                nc.scalar.copy(woven[:, :HALF, t:], state[t][:, :HALF].unsqueeze(2).to_broadcast([P, HALF, 2]))
+                nc.scalar.copy(woven[:, HALF:, t], state[t][:, HALF:])
             else:
-                for c, cols in enumerate(chunks):
-                    if c < 2:
-                        nc.vector.tensor_copy(woven_all[:, cols, t], state[t][:, cols])
+                for cols in pieces:
+                    if cols.stop <= HALF:
+                        nc.vector.tensor_copy(woven[:, cols, t], state[t][:, cols])
                     else:
-                        nc.scalar.copy(woven_all[:, cols, t], state[t][:, cols])
+                        nc.scalar.copy(woven[:, cols, t], state[t][:, cols])
 
         for pair in ((0, 1), (2, 3)):
             for t in pair:
@@ -145,15 +156,15 @@ def tile_picked_kalman8_none_po_kernel(
         out_scale = keep.tile([P, U], U8, name="out_scale", align_bytes=64)
         out_codes = keep.tile([P, U], I32, name="out_codes", align_bytes=64)
         out_words = out_1[0].rearrange("p c r -> p (c r)").bitcast(I32)
-        for c, cols in enumerate(chunks):
+        for c, cols in enumerate(pieces):
             nc.vector.quantize_mx(
                 out=out_codes[:, cols].bitcast(FP8X4),
                 scales=out_scale[:, cols],
-                in_=woven_all[:, cols, :].rearrange("p c t -> p (c t)"),
+                in_=woven[:, cols, :].rearrange("p c t -> p (c t)"),
             )
-            if c in (1, 3, 4):
-                stored = slice(edges[c - 1], edges[c + 1]) if c < 4 else cols
+            if c % 2 == 0:
+                stored = slice(EDGES[max(c - 1, 0)], EDGES[c + 1])
                 nc.sync.dma_start(out_words[:, stored], out_codes[:, stored])
-        for r in range(4):
+        for r in range(SCALE_ROWS * QUADRANT // P):
             queue = nc.sync if r % 2 == 0 else nc.scalar
-            queue.dma_start(out_2[0, r:16:4, :].bitcast(I32), out_scale[r:P:32, :].bitcast(I32))
+            queue.dma_start(out_2[0, r:SCALE_ROWS:4, :].bitcast(I32), out_scale[r:P:QUADRANT, :].bitcast(I32))

@@ -47,10 +47,10 @@ def tile_picked_kalman8_none_po_kernel(
         var_slot = {1: "var1", 3: "var0"}
 
         nc.vector.memset(scale_table[:].bitcast(I32), 0)
-        nc.sync.dma_start(trk_sb[:], trk)
-        nc.sync.dma_start(offs_sb[:], offs)
         nc.sync.dma_start(var[0][:], va_rows[:, 0, :])
         nc.sync.dma_start(var[1][:], va_rows[:, 1, :])
+        nc.sync.dma_start(trk_sb[:], trk)
+        nc.sync.dma_start(offs_sb[:], offs)
         nc.sync.dma_start(scale_table[0:P:SPREAD, :].bitcast(I32), x_scales[0].bitcast(I32))
         nc.sync.dma_start(w_raw[:], w1.rearrange("(p j) c -> p j c", j=PACK))
         nc.sync.dma_start(x_table[:], x_words[0].rearrange("p c r -> p (c r)").bitcast(I32))

@@ -20,8 +20,9 @@ PACK = 4
 QUADRANT = 32
 SCALE_ROWS = 16
 SPREAD = P // SCALE_ROWS
-HALF = U // 2
+HALF = 480
 QUARTER = U // 4
+DIRECT = 384
 EDGES = (0, QUARTER, HALF, 3 * QUARTER, U - QUARTER // 2, U)
 
 
@@ -35,42 +36,39 @@ def tile_picked_kalman8_none_po_kernel(
 
     with ExitStack() as ctx:
         keep = ctx.enter_context(tc.tile_pool(name="keep", bufs=1))
+        shared = ctx.enter_context(tc.tile_pool(name="shared", bufs=1))
         psum = ctx.enter_context(tc.psum_pool(name="psum", bufs=1))
+        va_flat = va.rearrange("(p t) u -> p (t u)", t=PACK)
+        ROW = 4 * U
+        LEAD = 32
 
         trk_sb = keep.tile([P, S // 16], U16, name="trk_sb")
         offs_sb = keep.tile([P, S // 16], U16, name="offs_sb")
         x_table = keep.tile([P, T], I32, name="x_table", align_bytes=64)
+        var_head = keep.tile([P, U + LEAD], F32, name="var_head")
         scale_table = keep.tile([P, T], U8, name="scale_table", align_bytes=64)
-        w_raw = keep.tile([P, PACK, N], F32, name="w_raw")
-        state = {t: keep.tile([P, U], F32, name=f"state{t}") for t in range(2)}
-        var = {t: keep.tile([P, U], F32, name=f"var{t}", tag=f"var{t}") for t in range(2)}
-        var_slot = {1: "var1", 3: "var0"}
+        w_raw = [shared.tile([P, 2, N], F32, name=f"w_raw{h}", offset=h * (ROW + ROW // 2)) for h in range(2)]
 
         nc.vector.memset(scale_table[:].bitcast(I32), 0)
-        nc.sync.dma_start(var[0][:], va_rows[:, 0, :])
-        nc.sync.dma_start(var[1][:], va_rows[:, 1, :])
+        nc.sync.dma_start(var_head[:], va_flat[:, : U + LEAD])
         nc.sync.dma_start(trk_sb[:], trk)
         nc.sync.dma_start(offs_sb[:], offs)
         nc.sync.dma_start(scale_table[0:P:SPREAD, :].bitcast(I32), x_scales[0].bitcast(I32))
-        nc.sync.dma_start(w_raw[:], w1.rearrange("(p j) c -> p j c", j=PACK))
+        w_rows = w1.rearrange("(p j) c -> p j c", j=PACK)
+        for h in range(2):
+            nc.sync.dma_start(w_raw[h][:], w_rows[:, 2 * h : 2 * h + 2, :])
         nc.sync.dma_start(x_table[:], x_words[0].rearrange("p c r -> p (c r)").bitcast(I32))
+
+        state = {0: keep.tile([P, U], F32, name="state0")}
         nc.sync.dma_start(state[0][:], st_rows[:, 0, :])
-        nc.sync.dma_start(state[1][:], st_rows[:, 1, :])
 
+        logs = {}
         stay = {}
-
-        def gains(pair):
-            logs = []
-            for i, t in enumerate(pair):
-                lg = keep.tile([P, U], F32, name=f"log{t}", tag=f"log{(i + t // 2) % 2}", align_bytes=64)
-                nc.scalar.activation(lg[:], var[t][:], ACT.Ln, bias=1.0, scale=2.0)
-                logs.append(lg)
-            both = keep.tile([P, 2 * S], F32, name=f"stay{pair[0]}", tag=var_slot[pair[1]])
-            for i, t in enumerate(pair):
-                stay[t] = both[:, i * S : (i + 1) * S]
-                nc.scalar.activation(stay[t], logs[i][:].indirect(trk_sb[:]), ACT.Exp, scale=-1.0)
-
-        gains((0, 1))
+        logs[0] = keep.tile([P, U], F32, name="log0", tag="log0", align_bytes=64)
+        nc.scalar.activation(logs[0][:], var_head[:, :U], ACT.Ln, bias=1.0, scale=2.0)
+        stay0 = keep.tile([P, S], F32, name="stay0")
+        stay[0] = stay0[:]
+        nc.scalar.activation(stay[0], logs[0][:].indirect(trk_sb[:]), ACT.Exp, scale=-1.0)
 
         picked_scale = keep.tile([P, S], U8, name="picked_scale", align_bytes=64)
         nc.vector.tensor_copy(picked_scale[:], scale_table[:].indirect(offs_sb[:]))
@@ -81,16 +79,20 @@ def tile_picked_kalman8_none_po_kernel(
                 x_scale[r:P:QUADRANT, :].bitcast(I32), picked_scale[SPREAD * r : P : QUADRANT, :].bitcast(I32)
             )
 
-        var[2] = keep.tile([P, U], F32, name="var2", tag="scale_table", align_bytes=64)
-        nc.sync.dma_start(var[2][:], va_rows[:, 2, :])
-        var[3] = keep.tile([P, U], F32, name="var3", tag="var0")
-        nc.sync.dma_start(var[3][:], va_rows[:, 3, :])
+        var_rest = keep.tile([P, S // 2 + 3 * U - LEAD], F32, name="var_rest", tag="scale_table", align_bytes=64)
+        var_cols = {t: slice(max(t * U, U + LEAD), (t + 1) * U) for t in range(1, PACK)}
+        var = {t: var_rest[:, S // 2 + c.start - U - LEAD : S // 2 + c.stop - U - LEAD] for t, c in var_cols.items()}
+        for t in range(1, PACK):
+            nc.sync.dma_start(var[t], va_flat[:, var_cols[t]])
 
         w_bf = keep.tile([P, N * PACK], BF16, name="w_bf", align_bytes=64)
         w_dealt = w_bf[:].rearrange("p (t m j) -> p m t j", t=PACK, j=PACK)
-        nc.vector.tensor_scalar(w_dealt, w_raw[:].rearrange("p j (m t) -> p m t j", t=PACK), -1.0, None, ALU.mult)
-        state[2] = keep.tile([P, U], F32, name="state2", tag="w_raw")
-        nc.sync.dma_start(state[2][:], st_rows[:, 2, :])
+        for h in range(2):
+            w_half = w_raw[h][:].rearrange("p j (m t) -> p m t j", t=PACK)
+            nc.vector.tensor_scalar(w_dealt[:, :, :, 2 * h : 2 * h + 2], w_half, -1.0, None, ALU.mult)
+        for i, t in enumerate((2, 3, 1)):
+            state[t] = shared.tile([P, U], F32, name=f"state{t}", offset=i * ROW)
+            nc.sync.dma_start(state[t][:], st_rows[:, t, :])
         w_codes = keep.tile([P, N], U32, name="w_codes", align_bytes=64)
         w_scale = keep.tile([P, N], U8, name="w_scale", align_bytes=64)
         nc.vector.quantize_mx(out=w_codes[:].bitcast(FP8X4), scales=w_scale[:], in_=w_bf[:])
@@ -98,45 +100,67 @@ def tile_picked_kalman8_none_po_kernel(
         x_codes = keep.tile([P, S], U32, name="x_codes", align_bytes=64)
         nc.vector.tensor_copy(x_codes[:], x_table[:].bitcast(U32).indirect(offs_sb[:]))
 
-        state[3] = keep.tile([P, U], F32, name="state3", tag="x_table", align_bytes=64)
-        nc.sync.dma_start(state[3][:], st_rows[:, 3, :])
+        parts = [(slice(h * S // 2, (h + 1) * S // 2), trk_sb[:, h * S // 32 : (h + 1) * S // 32]) for h in range(2)]
 
-        neg_y = []
-        for t in range(PACK):
-            bank = psum.tile([P, S], F32, name=f"neg_y{t}")
+        def project(t, entries):
+            bank = psum.tile([P, entries.stop - entries.start], F32, name=f"neg_y{t}_{entries.start}")
             cols = slice(t * P, (t + 1) * P)
             nc.tensor.matmul_mx(
                 out=bank[:],
                 lhsT=w_codes[:, cols].bitcast(FP8X4),
                 lhsT_scale=w_scale[:, cols],
-                rhs=x_codes[:].bitcast(FP8X4),
-                rhs_scale=x_scale[:],
+                rhs=x_codes[:, entries].bitcast(FP8X4),
+                rhs_scale=x_scale[:, entries],
                 start=True,
                 stop=True,
             )
-            neg_y.append(bank)
+            return bank
 
-        gains((2, 3))
+        neg_y = {0: project(0, slice(0, S))}
+        neg_y2 = [project(2, entries) for entries, offsets in parts]
+        for t in (3, 1):
+            neg_y[t] = project(t, slice(0, S))
 
-        woven = keep.tile([P, U, PACK], BF16, name="woven", tag="log0", align_bytes=64)
+        y = {}
+        logs[1] = keep.tile([P, U], F32, name="log1", tag="log0", align_bytes=64)
+        nc.scalar.activation(logs[1][:, :LEAD], var_head[:, U:], ACT.Ln, bias=1.0, scale=2.0)
+        for t in range(1, PACK):
+            if t > 1:
+                logs[t] = keep.tile([P, U], F32, name=f"log{t}", tag=f"log{t}", align_bytes=64)
+            nc.scalar.activation(logs[t][:, var_cols[t].start - t * U :], var[t], ACT.Ln, bias=1.0, scale=2.0)
+            u = t % 3 + 1
+            if u == 2:
+                y[u] = var_rest[:, :S]
+                nc.scalar.mul(y[u][:, S // 2 :], neg_y2[1][:], -1.0)
+            else:
+                y[u] = var[2][:, :S] if t < 3 else var[2][:, S:]
+                nc.scalar.mul(y[u], neg_y[u][:], -1.0)
+        stay[1] = var[3][:, :S]
+        stay[2] = var[3][:, S:]
+        stay3 = keep.tile([P, S], F32, name="stay3")
+        stay[3] = stay3[:]
+
+        def gain(t, entries=slice(0, S), offsets=trk_sb[:]):
+            nc.scalar.activation(stay[t][:, entries], logs[t][:].indirect(offsets), ACT.Exp, scale=-1.0)
+
+        for entries, offsets in parts:
+            gain(1, entries, offsets)
+        gain(2)
+        gain(3)
+
+        woven = keep.tile([P, U, PACK], BF16, name="woven", tag="log3", align_bytes=64)
         pieces = [slice(lo, hi) for lo, hi in zip(EDGES, EDGES[1:])]
-        first_two = keep.tile([P, 2, U], BF16, name="first_two", tag="log1", align_bytes=64)
-        old_part = {}
-        new_part = {}
+        first_two = keep.tile([P, 2, U], BF16, name="first_two", tag="log0", align_bytes=64)
 
-        def weigh(t):
-            old_part[t] = keep.tile([P, S], F32, name=f"old_part{t}")
-            nc.vector.tensor_tensor(old_part[t][:], state[t][:].indirect(trk_sb[:]), stay[t], ALU.mult)
-            new_part[t] = stay[t] if t < 2 else keep.tile([P, S], F32, name=f"new_part{t}")[:]
-            nc.vector.scalar_tensor_tensor(new_part[t], stay[t], 1.0, neg_y[t][:], ALU.subtract, ALU.mult)
-
-        def put_back(t):
-            nc.vector.tensor_tensor(state[t][:].indirect(trk_sb[:]), old_part[t][:], new_part[t], ALU.add)
+        def put_back(t, a, b):
+            entries, offsets = parts[1] if t == 1 else (slice(0, S), trk_sb[:])
+            nc.vector.tensor_tensor(state[t][:].indirect(offsets), a[:, entries], b[:, entries], ALU.add)
             nc.sync.dma_start(out_rows[:, t, :], state[t][:])
             if t < 2:
-                nc.scalar.copy(first_two[:, t, :], state[t][:])
+                nc.scalar.copy(first_two[:, t, DIRECT:], state[t][:, DIRECT:])
+                nc.scalar.copy(woven[:, :DIRECT, t], state[t][:, :DIRECT])
                 if t == 1:
-                    nc.scalar.copy(woven[:, :, 0:2], first_two[:].rearrange("p t u -> p u t"))
+                    nc.scalar.copy(woven[:, DIRECT:, 0:2], first_two[:, :, DIRECT:].rearrange("p t u -> p u t"))
             elif t == 2:
                 nc.scalar.copy(woven[:, :HALF, t:], state[t][:, :HALF].unsqueeze(2).to_broadcast([P, HALF, 2]))
                 nc.scalar.copy(woven[:, HALF:, t], state[t][:, HALF:])
@@ -147,23 +171,40 @@ def tile_picked_kalman8_none_po_kernel(
                     else:
                         nc.scalar.copy(woven[:, cols, t], state[t][:, cols])
 
-        for pair in ((0, 1), (2, 3)):
-            for t in pair:
-                weigh(t)
-            for t in pair:
-                put_back(t)
+        old0 = keep.tile([P, S], F32, name="old0")
+        new0 = keep.tile([P, S], F32, name="new0")
+        nc.vector.tensor_tensor(old0[:], state[0][:].indirect(trk_sb[:]), stay[0], ALU.mult)
+        nc.vector.scalar_tensor_tensor(new0[:], stay[0], 1.0, neg_y[0][:], ALU.subtract, ALU.mult)
+        nc.vector.tensor_scalar(y[2][:, : S // 2], neg_y2[0][:], -1.0, None, ALU.mult)
+        put_back(0, old0[:], new0[:])
+        diff = {}
+        for t in (2, 3, 1):
+            diff[t] = keep.tile([P, S], F32, name=f"diff{t}")
+            for entries, offsets in parts if t == 1 else [(slice(0, S), trk_sb[:])]:
+                nc.vector.tensor_tensor(diff[t][:, entries], state[t][:].indirect(offsets), y[t][:, entries], ALU.subtract)
+        for entries, offsets in parts:
+            nc.vector.tensor_tensor(diff[1][:, entries], diff[1][:, entries], stay[1][:, entries], ALU.mult)
+        entries, offsets = parts[0]
+        nc.vector.tensor_tensor(state[1][:].indirect(offsets), diff[1][:, entries], y[1][:, entries], ALU.add)
+        nc.vector.tensor_tensor(stay[1], diff[2][:], stay[2], ALU.mult)
+        put_back(1, diff[1][:], y[1])
+        nc.vector.tensor_tensor(stay[2], diff[3][:], stay[3], ALU.mult)
+        put_back(2, stay[1], y[2])
+        put_back(3, stay[2], y[3])
 
         out_scale = keep.tile([P, U], U8, name="out_scale", align_bytes=64)
         out_codes = keep.tile([P, U], I32, name="out_codes", align_bytes=64)
         out_words = out_1[0].rearrange("p c r -> p (c r)").bitcast(I32)
-        for c, cols in enumerate(pieces):
+        q_edges = (0, 256, 384, 512, 768, 896, 1024)
+        store_from = {384: 0, 768: 384, 1024: 768}
+        for cols in [slice(lo, hi) for lo, hi in zip(q_edges, q_edges[1:])]:
             nc.vector.quantize_mx(
                 out=out_codes[:, cols].bitcast(FP8X4),
                 scales=out_scale[:, cols],
                 in_=woven[:, cols, :].rearrange("p c t -> p (c t)"),
             )
-            if c % 2 == 0:
-                stored = slice(EDGES[max(c - 1, 0)], EDGES[c + 1])
+            if cols.stop in store_from:
+                stored = slice(store_from[cols.stop], cols.stop)
                 nc.sync.dma_start(out_words[:, stored], out_codes[:, stored])
         for r in range(SCALE_ROWS * QUADRANT // P):
             queue = nc.sync if r % 2 == 0 else nc.scalar

@@ -17,13 +17,24 @@ ACT = mybir.ActivationFunctionType
 
 P = 128
 PACK = 4
+GROUP = 16
 QUADRANT = 32
 SCALE_ROWS = 16
+RUN = SCALE_ROWS * QUADRANT // P
 SPREAD = P // SCALE_ROWS
-HALF = 480
-QUARTER = U // 4
-DIRECT = 384
-EDGES = (0, QUARTER, HALF, 3 * QUARTER, U - QUARTER // 2, U)
+ROW_BYTES = 4 * U
+EIGHTH = U // 8
+
+LEAD = 32
+DIRECT = U // 2
+ON_VECTOR = 480
+ROUND_EDGES = (0, 2 * EIGHTH, ON_VECTOR, 6 * EIGHTH, 7 * EIGHTH, U)
+QUANT_EDGES = (0, 2 * EIGHTH, 3 * EIGHTH, 4 * EIGHTH, 6 * EIGHTH, 7 * EIGHTH, U)
+STORE_EDGES = (0, 3 * EIGHTH, 6 * EIGHTH, U)
+
+
+def pieces(edges):
+    return [slice(lo, hi) for lo, hi in zip(edges, edges[1:])]
 
 
 def tile_picked_kalman8_none_po_kernel(
@@ -32,66 +43,70 @@ def tile_picked_kalman8_none_po_kernel(
     nc = tc.nc
     st_rows = st.rearrange("(p t) u -> p t u", t=PACK)
     va_rows = va.rearrange("(p t) u -> p t u", t=PACK)
+    va_flat = va.rearrange("(p t) u -> p (t u)", t=PACK)
+    w_rows = w1.rearrange("(p j) c -> p j c", j=PACK)
     out_rows = out_0.rearrange("(p t) u -> p t u", t=PACK)
 
     with ExitStack() as ctx:
         keep = ctx.enter_context(tc.tile_pool(name="keep", bufs=1))
         shared = ctx.enter_context(tc.tile_pool(name="shared", bufs=1))
         psum = ctx.enter_context(tc.psum_pool(name="psum", bufs=1))
-        va_flat = va.rearrange("(p t) u -> p (t u)", t=PACK)
-        ROW = 4 * U
-        LEAD = 32
 
-        trk_sb = keep.tile([P, S // 16], U16, name="trk_sb")
-        offs_sb = keep.tile([P, S // 16], U16, name="offs_sb")
+        trk_sb = keep.tile([P, S // GROUP], U16, name="trk_sb")
+        offs_sb = keep.tile([P, S // GROUP], U16, name="offs_sb")
         x_table = keep.tile([P, T], I32, name="x_table", align_bytes=64)
         var_head = keep.tile([P, U + LEAD], F32, name="var_head")
         scale_table = keep.tile([P, T], U8, name="scale_table", align_bytes=64)
-        w_raw = [shared.tile([P, 2, N], F32, name=f"w_raw{h}", offset=h * (ROW + ROW // 2)) for h in range(2)]
+        w_raw = [shared.tile([P, 2, N], F32, name=f"w_raw{h}", offset=h * ROW_BYTES * 3 // 2) for h in range(2)]
 
         nc.vector.memset(scale_table[:].bitcast(I32), 0)
         nc.sync.dma_start(var_head[:], va_flat[:, : U + LEAD])
         nc.sync.dma_start(trk_sb[:], trk)
         nc.sync.dma_start(offs_sb[:], offs)
         nc.sync.dma_start(scale_table[0:P:SPREAD, :].bitcast(I32), x_scales[0].bitcast(I32))
-        w_rows = w1.rearrange("(p j) c -> p j c", j=PACK)
         for h in range(2):
             nc.sync.dma_start(w_raw[h][:], w_rows[:, 2 * h : 2 * h + 2, :])
         nc.sync.dma_start(x_table[:], x_words[0].rearrange("p c r -> p (c r)").bitcast(I32))
-
         state = {0: keep.tile([P, U], F32, name="state0")}
         nc.sync.dma_start(state[0][:], st_rows[:, 0, :])
 
+        whole = (slice(0, S), trk_sb[:])
+        halves = [(e, trk_sb[:, e.start // GROUP : e.stop // GROUP]) for e in pieces((0, S // 2, S))]
         logs = {}
         stay = {}
+
+        def gain(t, share):
+            entries, offsets = share
+            nc.scalar.activation(stay[t][:, entries], logs[t][:].indirect(offsets), ACT.Exp, scale=-1.0)
+
         logs[0] = keep.tile([P, U], F32, name="log0", tag="log0", align_bytes=64)
         nc.scalar.activation(logs[0][:], var_head[:, :U], ACT.Ln, bias=1.0, scale=2.0)
-        stay0 = keep.tile([P, S], F32, name="stay0")
-        stay[0] = stay0[:]
-        nc.scalar.activation(stay[0], logs[0][:].indirect(trk_sb[:]), ACT.Exp, scale=-1.0)
+        stay[0] = keep.tile([P, S], F32, name="stay0")[:]
+        gain(0, whole)
 
         picked_scale = keep.tile([P, S], U8, name="picked_scale", align_bytes=64)
         nc.vector.tensor_copy(picked_scale[:], scale_table[:].indirect(offs_sb[:]))
         x_scale = keep.tile([P, S], U8, name="x_scale", align_bytes=64)
         nc.vector.memset(x_scale[:].bitcast(I32), 0)
-        for r in range(SCALE_ROWS * QUADRANT // P):
+        for r in range(RUN):
             nc.sync.dma_start(
                 x_scale[r:P:QUADRANT, :].bitcast(I32), picked_scale[SPREAD * r : P : QUADRANT, :].bitcast(I32)
             )
 
-        var_rest = keep.tile([P, S // 2 + 3 * U - LEAD], F32, name="var_rest", tag="scale_table", align_bytes=64)
-        var_cols = {t: slice(max(t * U, U + LEAD), (t + 1) * U) for t in range(1, PACK)}
-        var = {t: var_rest[:, S // 2 + c.start - U - LEAD : S // 2 + c.stop - U - LEAD] for t, c in var_cols.items()}
-        for t in range(1, PACK):
-            nc.sync.dma_start(var[t], va_flat[:, var_cols[t]])
+        var_rest = keep.tile([P, 3 * U + S], F32, name="var_rest", tag="scale_table", align_bytes=64)
+        var_at = {1: 0, 2: U + S // 2, 3: 2 * U + S // 2}
+        var_pieces = [(1, LEAD, U // 2), (1, U // 2, U), (2, 0, U // 2), (2, U // 2, U), (3, 0, U)]
+        for t, lo, hi in var_pieces:
+            nc.sync.dma_start(var_rest[:, var_at[t] + lo : var_at[t] + hi], va_rows[:, t, lo:hi])
 
         w_bf = keep.tile([P, N * PACK], BF16, name="w_bf", align_bytes=64)
         w_dealt = w_bf[:].rearrange("p (t m j) -> p m t j", t=PACK, j=PACK)
         for h in range(2):
             w_half = w_raw[h][:].rearrange("p j (m t) -> p m t j", t=PACK)
             nc.vector.tensor_scalar(w_dealt[:, :, :, 2 * h : 2 * h + 2], w_half, -1.0, None, ALU.mult)
-        for i, t in enumerate((2, 3, 1)):
-            state[t] = shared.tile([P, U], F32, name=f"state{t}", offset=i * ROW)
+        gather_order = (2, 3, 1)
+        for i, t in enumerate(gather_order):
+            state[t] = shared.tile([P, U], F32, name=f"state{t}", offset=i * ROW_BYTES)
             nc.sync.dma_start(state[t][:], st_rows[:, t, :])
         w_codes = keep.tile([P, N], U32, name="w_codes", align_bytes=64)
         w_scale = keep.tile([P, N], U8, name="w_scale", align_bytes=64)
@@ -100,9 +115,8 @@ def tile_picked_kalman8_none_po_kernel(
         x_codes = keep.tile([P, S], U32, name="x_codes", align_bytes=64)
         nc.vector.tensor_copy(x_codes[:], x_table[:].bitcast(U32).indirect(offs_sb[:]))
 
-        parts = [(slice(h * S // 2, (h + 1) * S // 2), trk_sb[:, h * S // 32 : (h + 1) * S // 32]) for h in range(2)]
-
-        def project(t, entries):
+        def project(t, share):
+            entries = share[0]
             bank = psum.tile([P, entries.stop - entries.start], F32, name=f"neg_y{t}_{entries.start}")
             cols = slice(t * P, (t + 1) * P)
             nc.tensor.matmul_mx(
@@ -114,47 +128,45 @@ def tile_picked_kalman8_none_po_kernel(
                 start=True,
                 stop=True,
             )
-            return bank
+            return bank[:]
 
-        neg_y = {0: project(0, slice(0, S))}
-        neg_y2 = [project(2, entries) for entries, offsets in parts]
-        for t in (3, 1):
-            neg_y[t] = project(t, slice(0, S))
+        neg_y0 = [project(0, share) for share in halves]
+        neg_y2 = [project(2, share) for share in halves]
+        neg_y3 = project(3, whole)
+        neg_y1 = project(1, whole)
 
-        y = {}
         logs[1] = keep.tile([P, U], F32, name="log1", tag="log0", align_bytes=64)
+        for t in (2, 3):
+            logs[t] = keep.tile([P, U], F32, name=f"log{t}", tag=f"log{t}", align_bytes=64)
+        over = [var_rest[:, cols] for cols in pieces(range(U, 3 * U + S + 1, S))]
+        y = {2: over[0], 3: over[1], 1: over[2]}
+        stay[1] = over[3]
+        stay[2] = over[4]
+        copy_after = {
+            var_pieces[2]: (y[2][:, halves[1][0]], neg_y2[1]),
+            var_pieces[3]: (y[3], neg_y3),
+            var_pieces[4]: (y[1], neg_y1),
+        }
         nc.scalar.activation(logs[1][:, :LEAD], var_head[:, U:], ACT.Ln, bias=1.0, scale=2.0)
-        for t in range(1, PACK):
-            if t > 1:
-                logs[t] = keep.tile([P, U], F32, name=f"log{t}", tag=f"log{t}", align_bytes=64)
-            nc.scalar.activation(logs[t][:, var_cols[t].start - t * U :], var[t], ACT.Ln, bias=1.0, scale=2.0)
-            u = t % 3 + 1
-            if u == 2:
-                y[u] = var_rest[:, :S]
-                nc.scalar.mul(y[u][:, S // 2 :], neg_y2[1][:], -1.0)
-            else:
-                y[u] = var[2][:, :S] if t < 3 else var[2][:, S:]
-                nc.scalar.mul(y[u], neg_y[u][:], -1.0)
-        stay[1] = var[3][:, :S]
-        stay[2] = var[3][:, S:]
-        stay3 = keep.tile([P, S], F32, name="stay3")
-        stay[3] = stay3[:]
-
-        def gain(t, entries=slice(0, S), offsets=trk_sb[:]):
-            nc.scalar.activation(stay[t][:, entries], logs[t][:].indirect(offsets), ACT.Exp, scale=-1.0)
-
-        for entries, offsets in parts:
-            gain(1, entries, offsets)
-        gain(2)
-        gain(3)
+        for t, lo, hi in var_pieces:
+            piece = var_rest[:, var_at[t] + lo : var_at[t] + hi]
+            nc.scalar.activation(logs[t][:, lo:hi], piece, ACT.Ln, bias=1.0, scale=2.0)
+            if (t, lo, hi) in copy_after:
+                nc.scalar.mul(*copy_after[(t, lo, hi)], -1.0)
+        stay[3] = keep.tile([P, S], F32, name="stay3")[:]
+        for share in halves:
+            gain(1, share)
+        gain(2, whole)
+        gain(3, whole)
 
         woven = keep.tile([P, U, PACK], BF16, name="woven", tag="log3", align_bytes=64)
-        pieces = [slice(lo, hi) for lo, hi in zip(EDGES, EDGES[1:])]
         first_two = keep.tile([P, 2, U], BF16, name="first_two", tag="log0", align_bytes=64)
 
-        def put_back(t, a, b):
-            entries, offsets = parts[1] if t == 1 else (slice(0, S), trk_sb[:])
-            nc.vector.tensor_tensor(state[t][:].indirect(offsets), a[:, entries], b[:, entries], ALU.add)
+        def scatter(t, share, one, other):
+            entries, offsets = share
+            nc.vector.tensor_tensor(state[t][:].indirect(offsets), one[:, entries], other[:, entries], ALU.add)
+
+        def hand_out(t):
             nc.sync.dma_start(out_rows[:, t, :], state[t][:])
             if t < 2:
                 nc.scalar.copy(first_two[:, t, DIRECT:], state[t][:, DIRECT:])
@@ -162,50 +174,57 @@ def tile_picked_kalman8_none_po_kernel(
                 if t == 1:
                     nc.scalar.copy(woven[:, DIRECT:, 0:2], first_two[:, :, DIRECT:].rearrange("p t u -> p u t"))
             elif t == 2:
-                nc.scalar.copy(woven[:, :HALF, t:], state[t][:, :HALF].unsqueeze(2).to_broadcast([P, HALF, 2]))
-                nc.scalar.copy(woven[:, HALF:, t], state[t][:, HALF:])
+                twice = state[t][:, :ON_VECTOR].unsqueeze(2).to_broadcast([P, ON_VECTOR, 2])
+                nc.scalar.copy(woven[:, :ON_VECTOR, t:], twice)
+                nc.scalar.copy(woven[:, ON_VECTOR:, t], state[t][:, ON_VECTOR:])
             else:
-                for cols in pieces:
-                    if cols.stop <= HALF:
+                for cols in pieces(ROUND_EDGES):
+                    if cols.stop <= ON_VECTOR:
                         nc.vector.tensor_copy(woven[:, cols, t], state[t][:, cols])
                     else:
                         nc.scalar.copy(woven[:, cols, t], state[t][:, cols])
 
-        old0 = keep.tile([P, S], F32, name="old0")
-        new0 = keep.tile([P, S], F32, name="new0")
-        nc.vector.tensor_tensor(old0[:], state[0][:].indirect(trk_sb[:]), stay[0], ALU.mult)
-        nc.vector.scalar_tensor_tensor(new0[:], stay[0], 1.0, neg_y[0][:], ALU.subtract, ALU.mult)
-        nc.vector.tensor_scalar(y[2][:, : S // 2], neg_y2[0][:], -1.0, None, ALU.mult)
-        put_back(0, old0[:], new0[:])
+        old_part = keep.tile([P, S], F32, name="old_part")
+        new_part = keep.tile([P, S], F32, name="new_part")
+        nc.vector.tensor_tensor(old_part[:], state[0][:].indirect(trk_sb[:]), stay[0], ALU.mult)
+        for (entries, offsets), bank in zip(halves, neg_y0):
+            nc.vector.scalar_tensor_tensor(new_part[:, entries], stay[0][:, entries], 1.0, bank, ALU.subtract, ALU.mult)
+        nc.vector.tensor_scalar(y[2][:, halves[0][0]], neg_y2[0], -1.0, None, ALU.mult)
+        scatter(0, whole, old_part[:], new_part[:])
+        hand_out(0)
+
         diff = {}
-        for t in (2, 3, 1):
-            diff[t] = keep.tile([P, S], F32, name=f"diff{t}")
-            for entries, offsets in parts if t == 1 else [(slice(0, S), trk_sb[:])]:
-                nc.vector.tensor_tensor(diff[t][:, entries], state[t][:].indirect(offsets), y[t][:, entries], ALU.subtract)
-        for entries, offsets in parts:
+        for t in gather_order:
+            diff[t] = keep.tile([P, S], F32, name=f"diff{t}")[:]
+            for entries, offsets in halves if t == 1 else [whole]:
+                nc.vector.tensor_tensor(
+                    diff[t][:, entries], state[t][:].indirect(offsets), y[t][:, entries], ALU.subtract
+                )
+        for entries, offsets in halves:
             nc.vector.tensor_tensor(diff[1][:, entries], diff[1][:, entries], stay[1][:, entries], ALU.mult)
-        entries, offsets = parts[0]
-        nc.vector.tensor_tensor(state[1][:].indirect(offsets), diff[1][:, entries], y[1][:, entries], ALU.add)
-        nc.vector.tensor_tensor(stay[1], diff[2][:], stay[2], ALU.mult)
-        put_back(1, diff[1][:], y[1])
-        nc.vector.tensor_tensor(stay[2], diff[3][:], stay[3], ALU.mult)
-        put_back(2, stay[1], y[2])
-        put_back(3, stay[2], y[3])
+        kept = {1: diff[1], 2: stay[1], 3: stay[2]}
+        scatter(1, halves[0], kept[1], y[1])
+        nc.vector.tensor_tensor(kept[2], diff[2], stay[2], ALU.mult)
+        scatter(1, halves[1], kept[1], y[1])
+        hand_out(1)
+        nc.vector.tensor_tensor(kept[3], diff[3], stay[3], ALU.mult)
+        for t in (2, 3):
+            scatter(t, whole, kept[t], y[t])
+            hand_out(t)
 
         out_scale = keep.tile([P, U], U8, name="out_scale", align_bytes=64)
         out_codes = keep.tile([P, U], I32, name="out_codes", align_bytes=64)
         out_words = out_1[0].rearrange("p c r -> p (c r)").bitcast(I32)
-        q_edges = (0, 256, 384, 512, 768, 896, 1024)
-        store_from = {384: 0, 768: 384, 1024: 768}
-        for cols in [slice(lo, hi) for lo, hi in zip(q_edges, q_edges[1:])]:
+        store_ending_at = {cols.stop: cols for cols in pieces(STORE_EDGES)}
+        for cols in pieces(QUANT_EDGES):
             nc.vector.quantize_mx(
                 out=out_codes[:, cols].bitcast(FP8X4),
                 scales=out_scale[:, cols],
                 in_=woven[:, cols, :].rearrange("p c t -> p (c t)"),
             )
-            if cols.stop in store_from:
-                stored = slice(store_from[cols.stop], cols.stop)
+            if cols.stop in store_ending_at:
+                stored = store_ending_at[cols.stop]
                 nc.sync.dma_start(out_words[:, stored], out_codes[:, stored])
-        for r in range(SCALE_ROWS * QUADRANT // P):
+        for r in range(RUN):
             queue = nc.sync if r % 2 == 0 else nc.scalar
-            queue.dma_start(out_2[0, r:SCALE_ROWS:4, :].bitcast(I32), out_scale[r:P:QUADRANT, :].bitcast(I32))
+            queue.dma_start(out_2[0, r:SCALE_ROWS:RUN, :].bitcast(I32), out_scale[r:P:QUADRANT, :].bitcast(I32))

@@ -24,10 +24,10 @@ RUN = SCALE_ROWS * QUADRANT // P
 SPREAD = P // SCALE_ROWS
 ROW_BYTES = 4 * U
 EIGHTH = U // 8
+HALF = S // 2
 
-LEAD = 32
-DIRECT = U // 2
 ON_VECTOR = 480
+SEAL = 16
 ROUND_EDGES = (0, 2 * EIGHTH, ON_VECTOR, 6 * EIGHTH, 7 * EIGHTH, U)
 QUANT_EDGES = (0, 2 * EIGHTH, 3 * EIGHTH, 4 * EIGHTH, 6 * EIGHTH, 7 * EIGHTH, U)
 STORE_EDGES = (0, 3 * EIGHTH, 6 * EIGHTH, U)
@@ -43,7 +43,6 @@ def tile_picked_kalman8_none_po_kernel(
     nc = tc.nc
     st_rows = st.rearrange("(p t) u -> p t u", t=PACK)
     va_rows = va.rearrange("(p t) u -> p t u", t=PACK)
-    va_flat = va.rearrange("(p t) u -> p (t u)", t=PACK)
     w_rows = w1.rearrange("(p j) c -> p j c", j=PACK)
     out_rows = out_0.rearrange("(p t) u -> p t u", t=PACK)
 
@@ -52,37 +51,28 @@ def tile_picked_kalman8_none_po_kernel(
         shared = ctx.enter_context(tc.tile_pool(name="shared", bufs=1))
         psum = ctx.enter_context(tc.psum_pool(name="psum", bufs=1))
 
+        def place(i):
+            return int(i * ROW_BYTES)
+
         trk_sb = keep.tile([P, S // GROUP], U16, name="trk_sb")
         offs_sb = keep.tile([P, S // GROUP], U16, name="offs_sb")
         x_table = keep.tile([P, T], I32, name="x_table", align_bytes=64)
-        var_head = keep.tile([P, U + LEAD], F32, name="var_head")
-        scale_table = keep.tile([P, T], U8, name="scale_table", align_bytes=64)
-        w_raw = [shared.tile([P, 2, N], F32, name=f"w_raw{h}", offset=h * ROW_BYTES * 3 // 2) for h in range(2)]
+        scale_table = shared.tile([P, T], U8, name="scale_table", offset=place(0.75), align_bytes=64)
+        w_raw = [shared.tile([P, 2, N], F32, name=f"w_raw{h}", offset=place(2.5 + 2 * h), align_bytes=64) for h in range(2)]
+        w_bf = shared.tile([P, N * PACK], BF16, name="w_bf", offset=place(6), align_bytes=64)
+        var = {0: keep.tile([P, U], F32, name="var0")}
 
         nc.vector.memset(scale_table[:].bitcast(I32), 0)
-        nc.sync.dma_start(var_head[:], va_flat[:, : U + LEAD])
-        nc.sync.dma_start(trk_sb[:], trk)
+        nc.sync.dma_start(w_raw[0][:], w_rows[:, 0:2, :])
         nc.sync.dma_start(offs_sb[:], offs)
+        nc.sync.dma_start(trk_sb[:], trk)
         nc.sync.dma_start(scale_table[0:P:SPREAD, :].bitcast(I32), x_scales[0].bitcast(I32))
-        for h in range(2):
-            nc.sync.dma_start(w_raw[h][:], w_rows[:, 2 * h : 2 * h + 2, :])
+        nc.sync.dma_start(var[0][:], va_rows[:, 0, :])
+        nc.sync.dma_start(w_raw[1][:], w_rows[:, 2:4, :])
         nc.sync.dma_start(x_table[:], x_words[0].rearrange("p c r -> p (c r)").bitcast(I32))
-        state = {0: keep.tile([P, U], F32, name="state0")}
-        nc.sync.dma_start(state[0][:], st_rows[:, 0, :])
 
         whole = (slice(0, S), trk_sb[:])
-        halves = [(e, trk_sb[:, e.start // GROUP : e.stop // GROUP]) for e in pieces((0, S // 2, S))]
-        logs = {}
-        stay = {}
-
-        def gain(t, share):
-            entries, offsets = share
-            nc.scalar.activation(stay[t][:, entries], logs[t][:].indirect(offsets), ACT.Exp, scale=-1.0)
-
-        logs[0] = keep.tile([P, U], F32, name="log0", tag="log0", align_bytes=64)
-        nc.scalar.activation(logs[0][:], var_head[:, :U], ACT.Ln, bias=1.0, scale=2.0)
-        stay[0] = keep.tile([P, S], F32, name="stay0")[:]
-        gain(0, whole)
+        halves = [(e, trk_sb[:, e.start // GROUP : e.stop // GROUP]) for e in pieces((0, HALF, S))]
 
         picked_scale = keep.tile([P, S], U8, name="picked_scale", align_bytes=64)
         nc.vector.tensor_copy(picked_scale[:], scale_table[:].indirect(offs_sb[:]))
@@ -93,27 +83,26 @@ def tile_picked_kalman8_none_po_kernel(
                 x_scale[r:P:QUADRANT, :].bitcast(I32), picked_scale[SPREAD * r : P : QUADRANT, :].bitcast(I32)
             )
 
-        var_rest = keep.tile([P, 3 * U + S], F32, name="var_rest", tag="scale_table", align_bytes=64)
-        var_at = {1: 0, 2: U + S // 2, 3: 2 * U + S // 2}
-        var_pieces = [(1, LEAD, U // 2), (1, U // 2, U), (2, 0, U // 2), (2, U // 2, U), (3, 0, U)]
-        for t, lo, hi in var_pieces:
-            nc.sync.dma_start(var_rest[:, var_at[t] + lo : var_at[t] + hi], va_rows[:, t, lo:hi])
-
-        w_bf = keep.tile([P, N * PACK], BF16, name="w_bf", align_bytes=64)
         w_dealt = w_bf[:].rearrange("p (t m j) -> p m t j", t=PACK, j=PACK)
         for h in range(2):
             w_half = w_raw[h][:].rearrange("p j (m t) -> p m t j", t=PACK)
             nc.vector.tensor_scalar(w_dealt[:, :, :, 2 * h : 2 * h + 2], w_half, -1.0, None, ALU.mult)
-        gather_order = (2, 3, 1)
-        for i, t in enumerate(gather_order):
-            state[t] = shared.tile([P, U], F32, name=f"state{t}", offset=i * ROW_BYTES)
-            nc.sync.dma_start(state[t][:], st_rows[:, t, :])
         w_codes = keep.tile([P, N], U32, name="w_codes", align_bytes=64)
         w_scale = keep.tile([P, N], U8, name="w_scale", align_bytes=64)
         nc.vector.quantize_mx(out=w_codes[:].bitcast(FP8X4), scales=w_scale[:], in_=w_bf[:])
 
+        state = {}
+        later = [("st", 0), ("st", 1), ("va", 1), ("st", 2), ("st", 3), ("va", 2), ("va", 3)]
+        for i, (kind, t) in enumerate(later):
+            tile = shared.tile([P, U], F32, name=f"{kind}{t}", offset=place(i), align_bytes=64)
+            (state if kind == "st" else var)[t] = tile
+            nc.sync.dma_start(tile[:], (st_rows if kind == "st" else va_rows)[:, t, :])
+
         x_codes = keep.tile([P, S], U32, name="x_codes", align_bytes=64)
-        nc.vector.tensor_copy(x_codes[:], x_table[:].bitcast(U32).indirect(offs_sb[:]))
+        for e in pieces((0, HALF, S)):
+            nc.vector.tensor_copy(
+                x_codes[:, e], x_table[:].bitcast(U32).indirect(offs_sb[:, e.start // GROUP : e.stop // GROUP])
+            )
 
         def project(t, share):
             entries = share[0]
@@ -131,86 +120,117 @@ def tile_picked_kalman8_none_po_kernel(
             return bank[:]
 
         neg_y0 = [project(0, share) for share in halves]
-        neg_y2 = [project(2, share) for share in halves]
-        neg_y3 = project(3, whole)
-        neg_y1 = project(1, whole)
+        neg_y = {t: project(t, whole) for t in (1, 2, 3)}
 
-        logs[1] = keep.tile([P, U], F32, name="log1", tag="log0", align_bytes=64)
-        for t in (2, 3):
-            logs[t] = keep.tile([P, U], F32, name=f"log{t}", tag=f"log{t}", align_bytes=64)
-        over = [var_rest[:, cols] for cols in pieces(range(U, 3 * U + S + 1, S))]
-        y = {2: over[0], 3: over[1], 1: over[2]}
-        stay[1] = over[3]
-        stay[2] = over[4]
-        copy_after = {
-            var_pieces[2]: (y[2][:, halves[1][0]], neg_y2[1]),
-            var_pieces[3]: (y[3], neg_y3),
-            var_pieces[4]: (y[1], neg_y1),
-        }
-        nc.scalar.activation(logs[1][:, :LEAD], var_head[:, U:], ACT.Ln, bias=1.0, scale=2.0)
-        for t, lo, hi in var_pieces:
-            piece = var_rest[:, var_at[t] + lo : var_at[t] + hi]
-            nc.scalar.activation(logs[t][:, lo:hi], piece, ACT.Ln, bias=1.0, scale=2.0)
-            if (t, lo, hi) in copy_after:
-                nc.scalar.mul(*copy_after[(t, lo, hi)], -1.0)
-        stay[3] = keep.tile([P, S], F32, name="stay3")[:]
+        def look_up(out, window, share):
+            entries, offsets = share
+            nc.scalar.activation(out[:, entries], window[:].indirect(offsets), ACT.Copy)
+
+        def root(out, in_):
+            nc.scalar.activation(out, in_, ACT.Abs_reciprocal_sqrt, bias=1.0, scale=2.0)
+
+        def strip(name):
+            return keep.tile([P, S + HALF], F32, name=name)
+
+        gains = [strip(f"gains{t}") for t in range(3)]
+        stay = {t: [gains[t][:, :HALF], gains[t][:, S:]] for t in range(3)}
+        diff = {t + 1: gains[t][:, :S] for t in range(3)}
+        old = {t: keep.tile([P, S], F32, name=f"old{t}")[:] for t in range(3)}
+        picked = {0: keep.tile([P, S], F32, name="picked0")[:]}
+        root0 = keep.tile([P, U], F32, name="root0")
+        root(root0[:], var[0][:])
         for share in halves:
-            gain(1, share)
-        gain(2, whole)
-        gain(3, whole)
-
-        woven = keep.tile([P, U, PACK], BF16, name="woven", tag="log3", align_bytes=64)
-        first_two = keep.tile([P, 2, U], BF16, name="first_two", tag="log0", align_bytes=64)
+            look_up(picked[0], root0, share)
+        for (entries, offsets), out in zip(halves, stay[0]):
+            nc.scalar.square(out, picked[0][:, entries])
+        for share in halves:
+            look_up(old[0], state[0], share)
 
         def scatter(t, share, one, other):
             entries, offsets = share
             nc.vector.tensor_tensor(state[t][:].indirect(offsets), one[:, entries], other[:, entries], ALU.add)
 
-        def hand_out(t):
+        def store(t):
             nc.sync.dma_start(out_rows[:, t, :], state[t][:])
-            if t < 2:
-                nc.scalar.copy(first_two[:, t, DIRECT:], state[t][:, DIRECT:])
-                nc.scalar.copy(woven[:, :DIRECT, t], state[t][:, :DIRECT])
-                if t == 1:
-                    nc.scalar.copy(woven[:, DIRECT:, 0:2], first_two[:, :, DIRECT:].rearrange("p t u -> p u t"))
-            elif t == 2:
-                twice = state[t][:, :ON_VECTOR].unsqueeze(2).to_broadcast([P, ON_VECTOR, 2])
-                nc.scalar.copy(woven[:, :ON_VECTOR, t:], twice)
-                nc.scalar.copy(woven[:, ON_VECTOR:, t], state[t][:, ON_VECTOR:])
-            else:
-                for cols in pieces(ROUND_EDGES):
-                    if cols.stop <= ON_VECTOR:
-                        nc.vector.tensor_copy(woven[:, cols, t], state[t][:, cols])
-                    else:
-                        nc.scalar.copy(woven[:, cols, t], state[t][:, cols])
 
-        old_part = keep.tile([P, S], F32, name="old_part")
         new_part = keep.tile([P, S], F32, name="new_part")
-        nc.vector.tensor_tensor(old_part[:], state[0][:].indirect(trk_sb[:]), stay[0], ALU.mult)
-        for (entries, offsets), bank in zip(halves, neg_y0):
-            nc.vector.scalar_tensor_tensor(new_part[:, entries], stay[0][:, entries], 1.0, bank, ALU.subtract, ALU.mult)
-        nc.vector.tensor_scalar(y[2][:, halves[0][0]], neg_y2[0], -1.0, None, ALU.mult)
-        scatter(0, whole, old_part[:], new_part[:])
-        hand_out(0)
+        for (entries, offsets), bank, keeps in zip(halves, neg_y0, stay[0]):
+            nc.vector.scalar_tensor_tensor(new_part[:, entries], keeps, 1.0, bank, ALU.subtract, ALU.mult)
+            nc.vector.tensor_tensor(old[0][:, entries], old[0][:, entries], keeps, ALU.mult)
 
-        diff = {}
-        for t in gather_order:
-            diff[t] = keep.tile([P, S], F32, name=f"diff{t}")[:]
-            for entries, offsets in halves if t == 1 else [whole]:
-                nc.vector.tensor_tensor(
-                    diff[t][:, entries], state[t][:].indirect(offsets), y[t][:, entries], ALU.subtract
+        def differ(t, share):
+            entries = share[0]
+            nc.vector.tensor_tensor(diff[t][:, entries], old[t][:, entries], neg_y[t][:, entries], ALU.add)
+
+        def weigh(t):
+            for (entries, offsets), keeps in zip(halves, stay[t]):
+                nc.vector.scalar_tensor_tensor(
+                    diff[t][:, entries], keeps, 1.0, diff[t][:, entries], ALU.subtract, ALU.mult
                 )
-        for entries, offsets in halves:
-            nc.vector.tensor_tensor(diff[1][:, entries], diff[1][:, entries], stay[1][:, entries], ALU.mult)
-        kept = {1: diff[1], 2: stay[1], 3: stay[2]}
-        scatter(1, halves[0], kept[1], y[1])
-        nc.vector.tensor_tensor(kept[2], diff[2], stay[2], ALU.mult)
-        scatter(1, halves[1], kept[1], y[1])
-        hand_out(1)
-        nc.vector.tensor_tensor(kept[3], diff[3], stay[3], ALU.mult)
-        for t in (2, 3):
-            scatter(t, whole, kept[t], y[t])
-            hand_out(t)
+
+        def gain(t, picked, roots, between):
+            for (entries, offsets), out in zip(halves, picked):
+                nc.scalar.activation(out, var[t][:].indirect(offsets), ACT.Copy)
+            for out, in_ in zip(roots, picked):
+                root(out, in_)
+            for u, share in between:
+                look_up(old[u], state[u], share)
+            for out, in_ in zip(stay[t], roots):
+                nc.scalar.square(out, in_)
+
+        planes = keep.tile([P, 3 * U], F32, name="planes")
+        plane = [planes[:, t * U : (t + 1) * U] for t in range(3)]
+        stay[3] = [plane[2][:, S : S + HALF], keep.tile([P, HALF], F32, name="stay3")[:]]
+        third = strip("third")
+        old[3] = third[:, :S]
+        last = keep.tile([P, S], F32, name="last")
+        spare = keep.tile([P, 3, HALF], F32, name="spare")
+        middle = slice(HALF // 2, HALF // 2 + HALF)
+
+        for share in halves:
+            look_up(old[1], state[1], share)
+        gain(1, [old[2][:, :HALF], spare[:, 0, :]], [third[:, HALF:][:, middle], old[2][:, HALF:]], [(2, halves[0])])
+        look_up(old[2], state[2], halves[1])
+        gain(2, [third[:, HALF:S], third[:, S:]], [last[:, middle], spare[:, 1, :]], [(3, whole)])
+        gain(3, [last[:, :HALF], last[:, HALF:]], [spare[:, 2, :], plane[2][:, middle]], [])
+
+        scatter(0, halves[0], old[0], new_part[:])
+        differ(1, halves[0])
+        scatter(0, halves[1], old[0], new_part[:])
+        store(0)
+        nc.sync.dma_start(plane[0], state[0][:])
+        differ(1, halves[1])
+        weigh(1)
+        differ(2, halves[0])
+        scatter(1, whole, old[1], diff[1])
+        nc.sync.dma_start(plane[1], state[1][:])
+        store(1)
+        differ(2, halves[1])
+        weigh(2)
+        differ(3, whole)
+        scatter(2, whole, old[2], diff[2])
+        store(2)
+        weigh(3)
+        nc.vector.tensor_copy(plane[2][:, S:], state[2][:, S:])
+        scatter(3, whole, old[3], diff[3])
+        store(3)
+        for cols in pieces((0, HALF, S)):
+            nc.scalar.copy(plane[2][:, cols], state[2][:, cols])
+
+        woven = keep.tile([P, U, PACK], BF16, name="woven", align_bytes=64)
+        three = planes[:].rearrange("p (t u) -> p u t", t=3)
+        for cols in pieces(ROUND_EDGES[:3]):
+            nc.scalar.copy(woven[:, cols, 0:3], three[:, cols, :])
+        seal = slice(ROUND_EDGES[1] - SEAL // 2, ROUND_EDGES[1] + SEAL // 2)
+        twice = plane[2][:, seal].unsqueeze(2).to_broadcast([P, SEAL, 2])
+        nc.scalar.copy(woven[:, seal, 2:], twice)
+        for cols in pieces((ON_VECTOR, 6 * EIGHTH, U)):
+            nc.scalar.copy(woven[:, cols, 0:3], three[:, cols, :])
+        for cols in pieces(ROUND_EDGES):
+            if cols.stop <= ON_VECTOR:
+                nc.vector.tensor_copy(woven[:, cols, 3], state[3][:, cols])
+            else:
+                nc.scalar.copy(woven[:, cols, 3], state[3][:, cols])
 
         out_scale = keep.tile([P, U], U8, name="out_scale", align_bytes=64)
         out_codes = keep.tile([P, U], I32, name="out_codes", align_bytes=64)

@@ -27,7 +27,6 @@ EIGHTH = U // 8
 HALF = S // 2
 
 ON_VECTOR = 480
-SEAL = 16
 ROUND_EDGES = (0, 2 * EIGHTH, ON_VECTOR, 6 * EIGHTH, 7 * EIGHTH, U)
 QUANT_EDGES = (0, 2 * EIGHTH, 3 * EIGHTH, 4 * EIGHTH, 6 * EIGHTH, 7 * EIGHTH, U)
 STORE_EDGES = (0, 3 * EIGHTH, 6 * EIGHTH, U)
@@ -35,6 +34,10 @@ STORE_EDGES = (0, 3 * EIGHTH, 6 * EIGHTH, U)
 
 def pieces(edges):
     return [slice(lo, hi) for lo, hi in zip(edges, edges[1:])]
+
+
+def from_top(edges):
+    return [slice(U - hi, U - lo) for lo, hi in zip(edges, edges[1:])]
 
 
 def tile_picked_kalman8_none_po_kernel(
@@ -179,12 +182,13 @@ def tile_picked_kalman8_none_po_kernel(
                 nc.scalar.square(out, in_)
 
         planes = keep.tile([P, 3 * U], F32, name="planes")
-        plane = [planes[:, t * U : (t + 1) * U] for t in range(3)]
-        stay[3] = [plane[2][:, S : S + HALF], keep.tile([P, HALF], F32, name="stay3")[:]]
+        plane = [planes[:].rearrange("p (h t c) -> p t h c", h=2, t=3)[:, t, :, :] for t in range(2)]
+        stay[3] = [planes[:, U : U + HALF], keep.tile([P, HALF], F32, name="stay3")[:]]
+        root3 = shared.tile([P, S], F32, name="root3", offset=place(2), align_bytes=64)
         third = strip("third")
         old[3] = third[:, :S]
         last = keep.tile([P, S], F32, name="last")
-        spare = keep.tile([P, 3, HALF], F32, name="spare")
+        spare = keep.tile([P, 2, HALF], F32, name="spare")
         middle = slice(HALF // 2, HALF // 2 + HALF)
 
         for share in halves:
@@ -192,42 +196,36 @@ def tile_picked_kalman8_none_po_kernel(
         gain(1, [old[2][:, :HALF], spare[:, 0, :]], [third[:, HALF:][:, middle], old[2][:, HALF:]], [(2, halves[0])])
         look_up(old[2], state[2], halves[1])
         gain(2, [third[:, HALF:S], third[:, S:]], [last[:, middle], spare[:, 1, :]], [(3, whole)])
-        gain(3, [last[:, :HALF], last[:, HALF:]], [spare[:, 2, :], plane[2][:, middle]], [])
+        gain(3, [last[:, :HALF], last[:, HALF:]], [root3[:, :HALF], root3[:, HALF:]], [])
 
         scatter(0, halves[0], old[0], new_part[:])
         differ(1, halves[0])
         scatter(0, halves[1], old[0], new_part[:])
         store(0)
-        nc.sync.dma_start(plane[0], state[0][:])
+        nc.sync.dma_start(plane[0], state[0][:].rearrange("p (h c) -> p h c", h=2))
         differ(1, halves[1])
         weigh(1)
         differ(2, halves[0])
         scatter(1, whole, old[1], diff[1])
-        nc.sync.dma_start(plane[1], state[1][:])
-        store(1)
+        nc.sync.dma_start(plane[1], state[1][:].rearrange("p (h c) -> p h c", h=2))
+        nc.sync.dma_start(out_rows[:, 1, :].rearrange("p (h c) -> p h c", h=2), plane[1])
         differ(2, halves[1])
         weigh(2)
         differ(3, whole)
         scatter(2, whole, old[2], diff[2])
         store(2)
         weigh(3)
-        nc.vector.tensor_copy(plane[2][:, S:], state[2][:, S:])
+        woven = shared.tile([P, U, PACK], BF16, name="woven", offset=place(1), align_bytes=64)
+        nc.vector.tensor_copy(planes[:, U : U + S], state[2][:, :S])
+        nc.scalar.copy(woven[:, S:, 0:2], planes[:, U + S : 2 * U + S].rearrange("p (t c) -> p c t", t=2))
+        twice = state[2][:, U - ON_VECTOR :].unsqueeze(2).to_broadcast([P, ON_VECTOR, 2])
+        nc.scalar.copy(woven[:, U - ON_VECTOR :, 2:], twice)
+        nc.scalar.copy(woven[:, S : U - ON_VECTOR, 2], state[2][:, S : U - ON_VECTOR])
+        nc.scalar.copy(woven[:, :S, 0:3], planes[:, : U + S].rearrange("p (t c) -> p c t", t=3))
         scatter(3, whole, old[3], diff[3])
         store(3)
-        for cols in pieces((0, HALF, S)):
-            nc.scalar.copy(plane[2][:, cols], state[2][:, cols])
-
-        woven = keep.tile([P, U, PACK], BF16, name="woven", align_bytes=64)
-        three = planes[:].rearrange("p (t u) -> p u t", t=3)
-        for cols in pieces(ROUND_EDGES[:3]):
-            nc.scalar.copy(woven[:, cols, 0:3], three[:, cols, :])
-        seal = slice(ROUND_EDGES[1] - SEAL // 2, ROUND_EDGES[1] + SEAL // 2)
-        twice = plane[2][:, seal].unsqueeze(2).to_broadcast([P, SEAL, 2])
-        nc.scalar.copy(woven[:, seal, 2:], twice)
-        for cols in pieces((ON_VECTOR, 6 * EIGHTH, U)):
-            nc.scalar.copy(woven[:, cols, 0:3], three[:, cols, :])
-        for cols in pieces(ROUND_EDGES):
-            if cols.stop <= ON_VECTOR:
+        for cols in from_top(ROUND_EDGES):
+            if cols.start >= U - ON_VECTOR:
                 nc.vector.tensor_copy(woven[:, cols, 3], state[3][:, cols])
             else:
                 nc.scalar.copy(woven[:, cols, 3], state[3][:, cols])
@@ -235,15 +233,15 @@ def tile_picked_kalman8_none_po_kernel(
         out_scale = keep.tile([P, U], U8, name="out_scale", align_bytes=64)
         out_codes = keep.tile([P, U], I32, name="out_codes", align_bytes=64)
         out_words = out_1[0].rearrange("p c r -> p (c r)").bitcast(I32)
-        store_ending_at = {cols.stop: cols for cols in pieces(STORE_EDGES)}
-        for cols in pieces(QUANT_EDGES):
+        store_ending_at = {cols.start: cols for cols in from_top(STORE_EDGES)}
+        for cols in from_top(QUANT_EDGES):
             nc.vector.quantize_mx(
                 out=out_codes[:, cols].bitcast(FP8X4),
                 scales=out_scale[:, cols],
                 in_=woven[:, cols, :].rearrange("p c t -> p (c t)"),
             )
-            if cols.stop in store_ending_at:
-                stored = store_ending_at[cols.stop]
+            if cols.start in store_ending_at:
+                stored = store_ending_at[cols.start]
                 nc.sync.dma_start(out_words[:, stored], out_codes[:, stored])
         for r in range(RUN):
             queue = nc.sync if r % 2 == 0 else nc.scalar

@@ -62,7 +62,7 @@ def tile_picked_kalman8_none_po_kernel(
         x_table = keep.tile([P, T], I32, name="x_table", align_bytes=64)
         scale_table = shared.tile([P, T], U8, name="scale_table", offset=place(0.75), align_bytes=64)
         w_raw = [shared.tile([P, 2, N], F32, name=f"w_raw{h}", offset=place(2.5 + 2 * h), align_bytes=64) for h in range(2)]
-        w_bf = shared.tile([P, N * PACK], BF16, name="w_bf", offset=place(6), align_bytes=64)
+        w_bf = keep.tile([P, N * PACK], BF16, name="w_bf", align_bytes=64)
         var = {0: keep.tile([P, U], F32, name="var0")}
 
         nc.vector.memset(scale_table[:].bitcast(I32), 0)
@@ -73,6 +73,8 @@ def tile_picked_kalman8_none_po_kernel(
         nc.sync.dma_start(var[0][:], va_rows[:, 0, :])
         nc.sync.dma_start(w_raw[1][:], w_rows[:, 2:4, :])
         nc.sync.dma_start(x_table[:], x_words[0].rearrange("p c r -> p (c r)").bitcast(I32))
+        state = {0: keep.tile([P, U], F32, name="st0")}
+        nc.sync.dma_start(state[0][:], st_rows[:, 0, :])
 
         whole = (slice(0, S), trk_sb[:])
         halves = [(e, trk_sb[:, e.start // GROUP : e.stop // GROUP]) for e in pieces((0, HALF, S))]
@@ -94,8 +96,7 @@ def tile_picked_kalman8_none_po_kernel(
         w_scale = keep.tile([P, N], U8, name="w_scale", align_bytes=64)
         nc.vector.quantize_mx(out=w_codes[:].bitcast(FP8X4), scales=w_scale[:], in_=w_bf[:])
 
-        state = {}
-        later = [("st", 0), ("st", 1), ("va", 1), ("st", 2), ("st", 3), ("va", 2), ("va", 3)]
+        later = [("st", 1), ("va", 1), ("st", 2), ("st", 3), ("va", 2), ("va", 3)]
         for i, (kind, t) in enumerate(later):
             tile = shared.tile([P, U], F32, name=f"{kind}{t}", offset=place(i), align_bytes=64)
             (state if kind == "st" else var)[t] = tile
@@ -146,8 +147,7 @@ def tile_picked_kalman8_none_po_kernel(
             look_up(picked[0], root0, share)
         for (entries, offsets), out in zip(halves, stay[0]):
             nc.scalar.square(out, picked[0][:, entries])
-        for share in halves:
-            look_up(old[0], state[0], share)
+        look_up(old[0], state[0], halves[1])
 
         def scatter(t, share, one, other):
             entries, offsets = share
@@ -157,9 +157,15 @@ def tile_picked_kalman8_none_po_kernel(
             nc.sync.dma_start(out_rows[:, t, :], state[t][:])
 
         new_part = keep.tile([P, S], F32, name="new_part")
-        for (entries, offsets), bank, keeps in zip(halves, neg_y0, stay[0]):
-            nc.vector.scalar_tensor_tensor(new_part[:, entries], keeps, 1.0, bank, ALU.subtract, ALU.mult)
-            nc.vector.tensor_tensor(old[0][:, entries], old[0][:, entries], keeps, ALU.mult)
+
+        def weigh_new(h):
+            nc.vector.scalar_tensor_tensor(
+                new_part[:, halves[h][0]], stay[0][h], 1.0, neg_y0[h], ALU.subtract, ALU.mult
+            )
+
+        nc.vector.tensor_tensor(old[0][:, :HALF], state[0][:].indirect(halves[0][1]), stay[0][0], ALU.mult)
+        weigh_new(0)
+        nc.vector.tensor_tensor(old[0][:, HALF:], old[0][:, HALF:], stay[0][1], ALU.mult)
 
         def differ(t, share):
             entries = share[0]
@@ -184,7 +190,7 @@ def tile_picked_kalman8_none_po_kernel(
         planes = keep.tile([P, 3 * U], F32, name="planes")
         plane = [planes[:].rearrange("p (h t c) -> p t h c", h=2, t=3)[:, t, :, :] for t in range(2)]
         stay[3] = [planes[:, U : U + HALF], keep.tile([P, HALF], F32, name="stay3")[:]]
-        root3 = shared.tile([P, S], F32, name="root3", offset=place(2), align_bytes=64)
+        root3 = planes[:, S:U]
         third = strip("third")
         old[3] = third[:, :S]
         last = keep.tile([P, S], F32, name="last")
@@ -199,6 +205,7 @@ def tile_picked_kalman8_none_po_kernel(
         gain(3, [last[:, :HALF], last[:, HALF:]], [root3[:, :HALF], root3[:, HALF:]], [])
 
         scatter(0, halves[0], old[0], new_part[:])
+        weigh_new(1)
         differ(1, halves[0])
         scatter(0, halves[1], old[0], new_part[:])
         store(0)
@@ -207,7 +214,8 @@ def tile_picked_kalman8_none_po_kernel(
         weigh(1)
         differ(2, halves[0])
         scatter(1, whole, old[1], diff[1])
-        nc.sync.dma_start(plane[1], state[1][:].rearrange("p (h c) -> p h c", h=2))
+        nc.sync.dma_start(plane[1][:, 1, :], state[1][:, S:])
+        nc.scalar.copy(plane[1][:, 0, :], state[1][:, :S])
         nc.sync.dma_start(out_rows[:, 1, :].rearrange("p (h c) -> p h c", h=2), plane[1])
         differ(2, halves[1])
         weigh(2)
@@ -215,13 +223,19 @@ def tile_picked_kalman8_none_po_kernel(
         scatter(2, whole, old[2], diff[2])
         store(2)
         weigh(3)
-        woven = shared.tile([P, U, PACK], BF16, name="woven", offset=place(1), align_bytes=64)
+        woven = shared.tile([P, U, PACK], BF16, name="woven", offset=place(0), align_bytes=64)
+
+        def weave(out, in_):
+            nc.scalar.copy(
+                out.rearrange("p (c i) t -> p c t i", i=PACK), in_.rearrange("p (t c i) -> p c t i", i=PACK, c=S // PACK)
+            )
+
         nc.vector.tensor_copy(planes[:, U : U + S], state[2][:, :S])
-        nc.scalar.copy(woven[:, S:, 0:2], planes[:, U + S : 2 * U + S].rearrange("p (t c) -> p c t", t=2))
+        weave(woven[:, S:, 0:2], planes[:, U + S : 2 * U + S])
         twice = state[2][:, U - ON_VECTOR :].unsqueeze(2).to_broadcast([P, ON_VECTOR, 2])
         nc.scalar.copy(woven[:, U - ON_VECTOR :, 2:], twice)
         nc.scalar.copy(woven[:, S : U - ON_VECTOR, 2], state[2][:, S : U - ON_VECTOR])
-        nc.scalar.copy(woven[:, :S, 0:3], planes[:, : U + S].rearrange("p (t c) -> p c t", t=3))
+        weave(woven[:, :S, 0:3], planes[:, : U + S])
         scatter(3, whole, old[3], diff[3])
         store(3)
         for cols in from_top(ROUND_EDGES):

@@ -226,9 +226,7 @@ def tile_picked_kalman8_none_po_kernel(
         woven = shared.tile([P, U, PACK], BF16, name="woven", offset=place(0), align_bytes=64)
 
         def weave(out, in_):
-            nc.scalar.copy(
-                out.rearrange("p (c i) t -> p c t i", i=PACK), in_.rearrange("p (t c i) -> p c t i", i=PACK, c=S // PACK)
-            )
+            nc.scalar.copy(out, in_.rearrange("p (t c) -> p c t", c=S))
 
         nc.vector.tensor_copy(planes[:, U : U + S], state[2][:, :S])
         weave(woven[:, S:, 0:2], planes[:, U + S : 2 * U + S])

@@ -60,18 +60,18 @@ def tile_picked_kalman8_none_po_kernel(
         trk_sb = keep.tile([P, S // GROUP], U16, name="trk_sb")
         offs_sb = keep.tile([P, S // GROUP], U16, name="offs_sb")
         x_table = keep.tile([P, T], I32, name="x_table", align_bytes=64)
-        scale_table = shared.tile([P, T], U8, name="scale_table", offset=place(0.75), align_bytes=64)
-        w_raw = [shared.tile([P, 2, N], F32, name=f"w_raw{h}", offset=place(2.5 + 2 * h), align_bytes=64) for h in range(2)]
-        w_bf = keep.tile([P, N * PACK], BF16, name="w_bf", align_bytes=64)
-        var = {0: keep.tile([P, U], F32, name="var0")}
+        scale_table = keep.tile([P, T], U8, name="scale_table", align_bytes=64)
+        w_raw = [shared.tile([P, 2, N], F32, name=f"w_raw{h}", offset=place(0.5 + 2 * h), align_bytes=64) for h in range(2)]
+        w_bf = shared.tile([P, N * PACK], BF16, name="w_bf", offset=place(4.5), align_bytes=64)
+        var = {0: keep.tile([P, U], F32, name="var0", tag="var0", align_bytes=64)}
 
         nc.vector.memset(scale_table[:].bitcast(I32), 0)
-        nc.sync.dma_start(w_raw[0][:], w_rows[:, 0:2, :])
+        nc.sync.dma_start(var[0][:], va_rows[:, 0, :])
         nc.sync.dma_start(offs_sb[:], offs)
         nc.sync.dma_start(trk_sb[:], trk)
         nc.sync.dma_start(scale_table[0:P:SPREAD, :].bitcast(I32), x_scales[0].bitcast(I32))
-        nc.sync.dma_start(var[0][:], va_rows[:, 0, :])
-        nc.sync.dma_start(w_raw[1][:], w_rows[:, 2:4, :])
+        for h in range(2):
+            nc.sync.dma_start(w_raw[h][:], w_rows[:, 2 * h : 2 * h + 2, :])
         nc.sync.dma_start(x_table[:], x_words[0].rearrange("p c r -> p (c r)").bitcast(I32))
         state = {0: keep.tile([P, U], F32, name="st0")}
         nc.sync.dma_start(state[0][:], st_rows[:, 0, :])
@@ -79,12 +79,18 @@ def tile_picked_kalman8_none_po_kernel(
         whole = (slice(0, S), trk_sb[:])
         halves = [(e, trk_sb[:, e.start // GROUP : e.stop // GROUP]) for e in pieces((0, HALF, S))]
 
+        def root(out, in_):
+            nc.scalar.activation(out, in_, ACT.Abs_reciprocal_sqrt, bias=1.0, scale=2.0)
+
+        root0 = keep.tile([P, U], F32, name="root0")
+        root(root0[:], var[0][:])
+
         picked_scale = keep.tile([P, S], U8, name="picked_scale", align_bytes=64)
         nc.vector.tensor_copy(picked_scale[:], scale_table[:].indirect(offs_sb[:]))
-        x_scale = keep.tile([P, S], U8, name="x_scale", align_bytes=64)
+        x_scale = keep.tile([P, S], U8, name="x_scale", tag="var0", align_bytes=64)
         nc.vector.memset(x_scale[:].bitcast(I32), 0)
         for r in range(RUN):
-            nc.sync.dma_start(
+            nc.scalar.dma_start(
                 x_scale[r:P:QUADRANT, :].bitcast(I32), picked_scale[SPREAD * r : P : QUADRANT, :].bitcast(I32)
             )
 
@@ -130,9 +136,6 @@ def tile_picked_kalman8_none_po_kernel(
             entries, offsets = share
             nc.scalar.activation(out[:, entries], window[:].indirect(offsets), ACT.Copy)
 
-        def root(out, in_):
-            nc.scalar.activation(out, in_, ACT.Abs_reciprocal_sqrt, bias=1.0, scale=2.0)
-
         def strip(name):
             return keep.tile([P, S + HALF], F32, name=name)
 
@@ -141,8 +144,6 @@ def tile_picked_kalman8_none_po_kernel(
         diff = {t + 1: gains[t][:, :S] for t in range(3)}
         old = {t: keep.tile([P, S], F32, name=f"old{t}")[:] for t in range(3)}
         picked = {0: keep.tile([P, S], F32, name="picked0")[:]}
-        root0 = keep.tile([P, U], F32, name="root0")
-        root(root0[:], var[0][:])
         for share in halves:
             look_up(picked[0], root0, share)
         for (entries, offsets), out in zip(halves, stay[0]):

@@ -23,8 +23,9 @@ SCALE_ROWS = 16
 RUN = SCALE_ROWS * QUADRANT // P
 SPREAD = P // SCALE_ROWS
 ROW_BYTES = 4 * U
-EIGHTH = U // 8
 HALF = S // 2
+MID = U // 2
+EIGHTH = U // 8
 
 ON_VECTOR = 480
 ROUND_EDGES = (0, 2 * EIGHTH, ON_VECTOR, 6 * EIGHTH, 7 * EIGHTH, U)
@@ -32,12 +33,12 @@ QUANT_EDGES = (0, 2 * EIGHTH, 3 * EIGHTH, 4 * EIGHTH, 6 * EIGHTH, 7 * EIGHTH, U)
 STORE_EDGES = (0, 3 * EIGHTH, 6 * EIGHTH, U)
 
 
-def pieces(edges):
-    return [slice(lo, hi) for lo, hi in zip(edges, edges[1:])]
-
-
 def from_top(edges):
     return [slice(U - hi, U - lo) for lo, hi in zip(edges, edges[1:])]
+
+
+def two(ap):
+    return [ap[:, :HALF], ap[:, HALF:S]]
 
 
 def tile_picked_kalman8_none_po_kernel(
@@ -54,15 +55,16 @@ def tile_picked_kalman8_none_po_kernel(
         shared = ctx.enter_context(tc.tile_pool(name="shared", bufs=1))
         psum = ctx.enter_context(tc.psum_pool(name="psum", bufs=1))
 
-        def place(i):
-            return int(i * ROW_BYTES)
+        def placed(shape, dtype, name, place, across=0):
+            offset = place * ROW_BYTES + across * ROW_BYTES // 2
+            return shared.tile(shape, dtype, name=name, offset=offset, align_bytes=64)
 
         trk_sb = keep.tile([P, S // GROUP], U16, name="trk_sb")
         offs_sb = keep.tile([P, S // GROUP], U16, name="offs_sb")
         x_table = keep.tile([P, T], I32, name="x_table", align_bytes=64)
         scale_table = keep.tile([P, T], U8, name="scale_table", align_bytes=64)
-        w_raw = [shared.tile([P, 2, N], F32, name=f"w_raw{h}", offset=place(0.5 + 2 * h), align_bytes=64) for h in range(2)]
-        w_bf = shared.tile([P, N * PACK], BF16, name="w_bf", offset=place(4.5), align_bytes=64)
+        w_raw = [placed([P, 2, N], F32, f"w_raw{h}", 2 * h, across=1) for h in range(2)]
+        w_bf = placed([P, N * PACK], BF16, "w_bf", 4, across=1)
         var = {0: keep.tile([P, U], F32, name="var0", tag="var0", align_bytes=64)}
 
         nc.vector.memset(scale_table[:].bitcast(I32), 0)
@@ -77,7 +79,8 @@ def tile_picked_kalman8_none_po_kernel(
         nc.sync.dma_start(state[0][:], st_rows[:, 0, :])
 
         whole = (slice(0, S), trk_sb[:])
-        halves = [(e, trk_sb[:, e.start // GROUP : e.stop // GROUP]) for e in pieces((0, HALF, S))]
+        half_columns = [slice(h * HALF // GROUP, (h + 1) * HALF // GROUP) for h in range(2)]
+        halves = [(slice(h * HALF, (h + 1) * HALF), trk_sb[:, half_columns[h]]) for h in range(2)]
 
         def root(out, in_):
             nc.scalar.activation(out, in_, ACT.Abs_reciprocal_sqrt, bias=1.0, scale=2.0)
@@ -102,17 +105,14 @@ def tile_picked_kalman8_none_po_kernel(
         w_scale = keep.tile([P, N], U8, name="w_scale", align_bytes=64)
         nc.vector.quantize_mx(out=w_codes[:].bitcast(FP8X4), scales=w_scale[:], in_=w_bf[:])
 
-        later = [("st", 1), ("va", 1), ("st", 2), ("st", 3), ("va", 2), ("va", 3)]
-        for i, (kind, t) in enumerate(later):
-            tile = shared.tile([P, U], F32, name=f"{kind}{t}", offset=place(i), align_bytes=64)
-            (state if kind == "st" else var)[t] = tile
-            nc.sync.dma_start(tile[:], (st_rows if kind == "st" else va_rows)[:, t, :])
+        later = [(state, 1), (var, 1), (state, 2), (state, 3), (var, 2), (var, 3)]
+        for place, (tiles, t) in enumerate(later):
+            tiles[t] = placed([P, U], F32, f"later{place}", place)
+            nc.sync.dma_start(tiles[t][:], (st_rows if tiles is state else va_rows)[:, t, :])
 
         x_codes = keep.tile([P, S], U32, name="x_codes", align_bytes=64)
-        for e in pieces((0, HALF, S)):
-            nc.vector.tensor_copy(
-                x_codes[:, e], x_table[:].bitcast(U32).indirect(offs_sb[:, e.start // GROUP : e.stop // GROUP])
-            )
+        for out, columns in zip(two(x_codes), half_columns):
+            nc.vector.tensor_copy(out, x_table[:].bitcast(U32).indirect(offs_sb[:, columns]))
 
         def project(t, share):
             entries = share[0]
@@ -130,115 +130,121 @@ def tile_picked_kalman8_none_po_kernel(
             return bank[:]
 
         neg_y0 = [project(0, share) for share in halves]
-        neg_y = {t: project(t, whole) for t in (1, 2, 3)}
+        neg_y = {t: project(t, whole) for t in range(1, PACK)}
 
-        def look_up(out, window, share):
+        def look_up(out, window, h):
+            nc.scalar.activation(out, window[:].indirect(halves[h][1]), ACT.Copy)
+
+        strips = [keep.tile([P, S + HALF], F32, name=f"strip{t}") for t in range(PACK - 1)]
+        stay = {t: [strip[:, :HALF], strip[:, S:]] for t, strip in enumerate(strips)}
+        diff = {t + 1: strip[:, :S] for t, strip in enumerate(strips)}
+        old = {t: keep.tile([P, S], F32, name=f"old{t}")[:] for t in range(PACK - 1)}
+        picked_root0 = two(keep.tile([P, S], F32, name="picked_root0"))
+        for h in range(2):
+            look_up(picked_root0[h], root0, h)
+        for h in range(2):
+            nc.scalar.square(stay[0][h], picked_root0[h])
+
+        def look_up_states(t, h):
+            look_up(two(old[t])[h], state[t], h)
+
+        def scatter(t, share, other):
             entries, offsets = share
-            nc.scalar.activation(out[:, entries], window[:].indirect(offsets), ACT.Copy)
-
-        def strip(name):
-            return keep.tile([P, S + HALF], F32, name=name)
-
-        gains = [strip(f"gains{t}") for t in range(3)]
-        stay = {t: [gains[t][:, :HALF], gains[t][:, S:]] for t in range(3)}
-        diff = {t + 1: gains[t][:, :S] for t in range(3)}
-        old = {t: keep.tile([P, S], F32, name=f"old{t}")[:] for t in range(3)}
-        picked = {0: keep.tile([P, S], F32, name="picked0")[:]}
-        for share in halves:
-            look_up(picked[0], root0, share)
-        for (entries, offsets), out in zip(halves, stay[0]):
-            nc.scalar.square(out, picked[0][:, entries])
-        look_up(old[0], state[0], halves[1])
-
-        def scatter(t, share, one, other):
-            entries, offsets = share
-            nc.vector.tensor_tensor(state[t][:].indirect(offsets), one[:, entries], other[:, entries], ALU.add)
+            nc.vector.tensor_tensor(state[t][:].indirect(offsets), old[t][:, entries], other[:, entries], ALU.add)
 
         def store(t):
             nc.sync.dma_start(out_rows[:, t, :], state[t][:])
 
+        look_up_states(0, 1)
         new_part = keep.tile([P, S], F32, name="new_part")
 
-        def weigh_new(h):
-            nc.vector.scalar_tensor_tensor(
-                new_part[:, halves[h][0]], stay[0][h], 1.0, neg_y0[h], ALU.subtract, ALU.mult
-            )
+        def weigh_y0(h):
+            nc.vector.scalar_tensor_tensor(two(new_part)[h], stay[0][h], 1.0, neg_y0[h], ALU.subtract, ALU.mult)
 
-        nc.vector.tensor_tensor(old[0][:, :HALF], state[0][:].indirect(halves[0][1]), stay[0][0], ALU.mult)
-        weigh_new(0)
-        nc.vector.tensor_tensor(old[0][:, HALF:], old[0][:, HALF:], stay[0][1], ALU.mult)
+        nc.vector.tensor_tensor(two(old[0])[0], state[0][:].indirect(halves[0][1]), stay[0][0], ALU.mult)
+        weigh_y0(0)
+        nc.vector.tensor_tensor(two(old[0])[1], two(old[0])[1], stay[0][1], ALU.mult)
 
-        def differ(t, share):
-            entries = share[0]
-            nc.vector.tensor_tensor(diff[t][:, entries], old[t][:, entries], neg_y[t][:, entries], ALU.add)
+        def differ(t, h):
+            nc.vector.tensor_tensor(two(diff[t])[h], two(old[t])[h], two(neg_y[t])[h], ALU.add)
 
         def weigh(t):
-            for (entries, offsets), keeps in zip(halves, stay[t]):
-                nc.vector.scalar_tensor_tensor(
-                    diff[t][:, entries], keeps, 1.0, diff[t][:, entries], ALU.subtract, ALU.mult
-                )
+            for keeps, part in zip(stay[t], two(diff[t])):
+                nc.vector.scalar_tensor_tensor(part, keeps, 1.0, part, ALU.subtract, ALU.mult)
 
-        def gain(t, picked, roots, between):
-            for (entries, offsets), out in zip(halves, picked):
-                nc.scalar.activation(out, var[t][:].indirect(offsets), ACT.Copy)
-            for out, in_ in zip(roots, picked):
-                root(out, in_)
-            for u, share in between:
-                look_up(old[u], state[u], share)
-            for out, in_ in zip(stay[t], roots):
-                nc.scalar.square(out, in_)
+        def take_roots(t, picked, roots):
+            for h in range(2):
+                look_up(picked[h], var[t], h)
+            for h in range(2):
+                root(roots[h], picked[h])
+
+        def square(t, roots):
+            for h in range(2):
+                nc.scalar.square(stay[t][h], roots[h])
 
         planes = keep.tile([P, 3 * U], F32, name="planes")
-        plane = [planes[:].rearrange("p (h t c) -> p t h c", h=2, t=3)[:, t, :, :] for t in range(2)]
-        stay[3] = [planes[:, U : U + HALF], keep.tile([P, HALF], F32, name="stay3")[:]]
-        root3 = planes[:, S:U]
-        third = strip("third")
-        old[3] = third[:, :S]
-        last = keep.tile([P, S], F32, name="last")
-        spare = keep.tile([P, 2, HALF], F32, name="spare")
-        middle = slice(HALF // 2, HALF // 2 + HALF)
+        by_tile = planes[:].rearrange("p (h t c) -> p t h c", h=2, t=3)
+        lower = [by_tile[:, t, 0, :] for t in range(3)]
+        upper1 = by_tile[:, 1, 1, :]
+        stay[3] = [lower[2][:, :HALF], keep.tile([P, HALF], F32, name="stay3")[:]]
+        roots3 = two(lower[1])
+        old[3] = keep.tile([P, S], F32, name="old3")[:]
+        picked3 = keep.tile([P, S], F32, name="picked3")
+        picked1_second = keep.tile([P, HALF], F32, name="picked1_second")
 
-        for share in halves:
-            look_up(old[1], state[1], share)
-        gain(1, [old[2][:, :HALF], spare[:, 0, :]], [third[:, HALF:][:, middle], old[2][:, HALF:]], [(2, halves[0])])
-        look_up(old[2], state[2], halves[1])
-        gain(2, [third[:, HALF:S], third[:, S:]], [last[:, middle], spare[:, 1, :]], [(3, whole)])
-        gain(3, [last[:, :HALF], last[:, HALF:]], [root3[:, :HALF], root3[:, HALF:]], [])
+        for h in range(2):
+            look_up_states(1, h)
+        roots1 = two(old[2])
+        take_roots(1, [two(old[3])[0], picked1_second[:]], roots1)
+        square(1, roots1)
+        look_up_states(2, 0)
+        roots2 = [picked3[:, HALF // 2 : HALF // 2 + HALF], two(old[3])[1]]
+        take_roots(2, [two(old[2])[1], two(old[3])[0]], roots2)
+        look_up_states(2, 1)
+        look_up_states(3, 0)
+        square(2, roots2)
+        look_up_states(3, 1)
+        take_roots(3, two(picked3), roots3)
+        square(3, roots3)
 
-        scatter(0, halves[0], old[0], new_part[:])
-        weigh_new(1)
-        differ(1, halves[0])
-        scatter(0, halves[1], old[0], new_part[:])
+        scatter(0, halves[0], new_part[:])
+        weigh_y0(1)
+        differ(1, 0)
+        scatter(0, halves[1], new_part[:])
         store(0)
-        nc.sync.dma_start(plane[0], state[0][:].rearrange("p (h c) -> p h c", h=2))
-        differ(1, halves[1])
+        nc.sync.dma_start(by_tile[:, 0, :, :], state[0][:].rearrange("p (h c) -> p h c", h=2))
+        differ(1, 1)
         weigh(1)
-        differ(2, halves[0])
-        scatter(1, whole, old[1], diff[1])
-        nc.sync.dma_start(plane[1][:, 1, :], state[1][:, S:])
-        nc.scalar.copy(plane[1][:, 0, :], state[1][:, :S])
-        nc.sync.dma_start(out_rows[:, 1, :].rearrange("p (h c) -> p h c", h=2), plane[1])
-        differ(2, halves[1])
+        scatter(1, halves[0], diff[1])
+        differ(2, 0)
+        scatter(1, halves[1], diff[1])
+        nc.sync.dma_start(upper1, state[1][:, MID:])
+        nc.scalar.copy(lower[1], state[1][:, :MID])
+        nc.sync.dma_start(out_rows[:, 1, :].rearrange("p (h c) -> p h c", h=2), by_tile[:, 1, :, :])
+        differ(2, 1)
         weigh(2)
-        differ(3, whole)
-        scatter(2, whole, old[2], diff[2])
+        differ(3, 0)
+        scatter(2, whole, diff[2])
         store(2)
+        differ(3, 1)
         weigh(3)
-        woven = shared.tile([P, U, PACK], BF16, name="woven", offset=place(0), align_bytes=64)
+
+        woven = placed([P, U, PACK], BF16, "woven", 0)
 
         def weave(out, in_):
-            nc.scalar.copy(out, in_.rearrange("p (t c) -> p c t", c=S))
+            nc.scalar.copy(out, in_.rearrange("p (t c) -> p c t", c=MID))
 
-        nc.vector.tensor_copy(planes[:, U : U + S], state[2][:, :S])
-        weave(woven[:, S:, 0:2], planes[:, U + S : 2 * U + S])
-        twice = state[2][:, U - ON_VECTOR :].unsqueeze(2).to_broadcast([P, ON_VECTOR, 2])
-        nc.scalar.copy(woven[:, U - ON_VECTOR :, 2:], twice)
-        nc.scalar.copy(woven[:, S : U - ON_VECTOR, 2], state[2][:, S : U - ON_VECTOR])
-        weave(woven[:, :S, 0:3], planes[:, : U + S])
-        scatter(3, whole, old[3], diff[3])
+        nc.vector.tensor_copy(lower[2], state[2][:, :MID])
+        weave(woven[:, MID:, 0:2], planes[:, 3 * MID : 5 * MID])
+        on_vector = slice(U - ON_VECTOR, U)
+        twice = state[2][:, on_vector].unsqueeze(2).to_broadcast([P, ON_VECTOR, 2])
+        nc.scalar.copy(woven[:, on_vector, 2:], twice)
+        nc.scalar.copy(woven[:, MID : on_vector.start, 2], state[2][:, MID : on_vector.start])
+        weave(woven[:, :MID, 0:3], planes[:, : 3 * MID])
+        scatter(3, whole, diff[3])
         store(3)
         for cols in from_top(ROUND_EDGES):
-            if cols.start >= U - ON_VECTOR:
+            if cols.start >= on_vector.start:
                 nc.vector.tensor_copy(woven[:, cols, 3], state[3][:, cols])
             else:
                 nc.scalar.copy(woven[:, cols, 3], state[3][:, cols])
@@ -246,15 +252,15 @@ def tile_picked_kalman8_none_po_kernel(
         out_scale = keep.tile([P, U], U8, name="out_scale", align_bytes=64)
         out_codes = keep.tile([P, U], I32, name="out_codes", align_bytes=64)
         out_words = out_1[0].rearrange("p c r -> p (c r)").bitcast(I32)
-        store_ending_at = {cols.start: cols for cols in from_top(STORE_EDGES)}
+        store_down_to = {cols.start: cols for cols in from_top(STORE_EDGES)}
         for cols in from_top(QUANT_EDGES):
             nc.vector.quantize_mx(
                 out=out_codes[:, cols].bitcast(FP8X4),
                 scales=out_scale[:, cols],
                 in_=woven[:, cols, :].rearrange("p c t -> p (c t)"),
             )
-            if cols.start in store_ending_at:
-                stored = store_ending_at[cols.start]
+            if cols.start in store_down_to:
+                stored = store_down_to[cols.start]
                 nc.sync.dma_start(out_words[:, stored], out_codes[:, stored])
         for r in range(RUN):
             queue = nc.sync if r % 2 == 0 else nc.scalar

@@ -24,8 +24,9 @@ RUN = SCALE_ROWS * QUADRANT // P
 SPREAD = P // SCALE_ROWS
 ROW_BYTES = 4 * U
 HALF = S // 2
-MID = U // 2
+QUARTER = U // 4
 EIGHTH = U // 8
+WALK = 4
 
 ON_VECTOR = 480
 ROUND_EDGES = (0, 2 * EIGHTH, ON_VECTOR, 6 * EIGHTH, 7 * EIGHTH, U)
@@ -33,8 +34,8 @@ QUANT_EDGES = (0, 2 * EIGHTH, 3 * EIGHTH, 4 * EIGHTH, 6 * EIGHTH, 7 * EIGHTH, U)
 STORE_EDGES = (0, 3 * EIGHTH, 6 * EIGHTH, U)
 
 
-def from_top(edges):
-    return [slice(U - hi, U - lo) for lo, hi in zip(edges, edges[1:])]
+def pieces(edges):
+    return [slice(lo, hi) for lo, hi in zip(edges, edges[1:])]
 
 
 def two(ap):
@@ -182,12 +183,10 @@ def tile_picked_kalman8_none_po_kernel(
             for h in range(2):
                 nc.scalar.square(stay[t][h], roots[h])
 
-        planes = keep.tile([P, 3 * U], F32, name="planes")
-        by_tile = planes[:].rearrange("p (h t c) -> p t h c", h=2, t=3)
-        lower = [by_tile[:, t, 0, :] for t in range(3)]
-        upper1 = by_tile[:, 1, 1, :]
-        stay[3] = [lower[2][:, :HALF], keep.tile([P, HALF], F32, name="stay3")[:]]
-        roots3 = two(lower[1])
+        planes = keep.tile([P, PACK * U], F32, name="planes")
+        by_tile = planes[:].rearrange("p (q t c) -> p t q c", q=4, t=PACK)
+        stay[3] = [by_tile[:, 2, 3, :], by_tile[:, 3, 3, :]]
+        roots3 = [by_tile[:, 3, h, :] for h in range(2)]
         old[3] = keep.tile([P, S], F32, name="old3")[:]
         picked3 = keep.tile([P, S], F32, name="picked3")
         picked1_second = keep.tile([P, HALF], F32, name="picked1_second")
@@ -211,40 +210,43 @@ def tile_picked_kalman8_none_po_kernel(
         weigh_y0(1)
         differ(1, 0)
         scatter(0, halves[1], new_part[:])
+
+        def quarters(t):
+            return state[t][:].rearrange("p (q c) -> p q c", q=4)
+
         store(0)
-        nc.sync.dma_start(by_tile[:, 0, :, :], state[0][:].rearrange("p (h c) -> p h c", h=2))
+        nc.sync.dma_start(by_tile[:, 0, :, :], quarters(0))
         differ(1, 1)
         weigh(1)
         scatter(1, halves[0], diff[1])
         differ(2, 0)
         scatter(1, halves[1], diff[1])
-        nc.sync.dma_start(upper1, state[1][:, MID:])
-        nc.scalar.copy(lower[1], state[1][:, :MID])
-        nc.sync.dma_start(out_rows[:, 1, :].rearrange("p (h c) -> p h c", h=2), by_tile[:, 1, :, :])
+        nc.sync.dma_start(by_tile[:, 1, :, :], quarters(1))
+        store(1)
         differ(2, 1)
         weigh(2)
         differ(3, 0)
         scatter(2, whole, diff[2])
         store(2)
         differ(3, 1)
+        nc.vector.tensor_copy(by_tile[:, 2, 0:2, :], quarters(2)[:, 0:2, :])
         weigh(3)
+        nc.vector.tensor_copy(by_tile[:, 2, 3, :], quarters(2)[:, 3, :])
 
-        woven = placed([P, U, PACK], BF16, "woven", 0)
+        woven = keep.tile([P, U, PACK], BF16, name="woven", align_bytes=64)
 
-        def weave(out, in_):
-            nc.scalar.copy(out, in_.rearrange("p (t c) -> p c t", c=MID))
+        woven_walk = woven[:].rearrange("p (q c i) t -> p q c t i", q=4, i=WALK)
+        planes_walk = planes[:].rearrange("p (q t c i) -> p q c t i", q=4, t=PACK, i=WALK)
 
-        nc.vector.tensor_copy(lower[2], state[2][:, :MID])
-        weave(woven[:, MID:, 0:2], planes[:, 3 * MID : 5 * MID])
-        on_vector = slice(U - ON_VECTOR, U)
-        twice = state[2][:, on_vector].unsqueeze(2).to_broadcast([P, ON_VECTOR, 2])
-        nc.scalar.copy(woven[:, on_vector, 2:], twice)
-        nc.scalar.copy(woven[:, MID : on_vector.start, 2], state[2][:, MID : on_vector.start])
-        weave(woven[:, :MID, 0:3], planes[:, : 3 * MID])
+        twice = planes_walk[:, 2, :, 0:2, :].unsqueeze(2).to_broadcast([P, QUARTER // WALK, 2, 2, WALK])
+        nc.scalar.copy(woven_walk[:, 2].rearrange("p c (a t) i -> p c a t i", a=2), twice)
+        nc.scalar.copy(woven[:, 2 * QUARTER : 3 * QUARTER, 2], quarters(2)[:, 2, :])
+        nc.scalar.copy(woven_walk[:, 0:2], planes_walk[:, 0:2])
+        nc.scalar.copy(woven_walk[:, 3], planes_walk[:, 3])
         scatter(3, whole, diff[3])
         store(3)
-        for cols in from_top(ROUND_EDGES):
-            if cols.start >= on_vector.start:
+        for cols in pieces(ROUND_EDGES):
+            if cols.stop <= ON_VECTOR:
                 nc.vector.tensor_copy(woven[:, cols, 3], state[3][:, cols])
             else:
                 nc.scalar.copy(woven[:, cols, 3], state[3][:, cols])
@@ -252,15 +254,15 @@ def tile_picked_kalman8_none_po_kernel(
         out_scale = keep.tile([P, U], U8, name="out_scale", align_bytes=64)
         out_codes = keep.tile([P, U], I32, name="out_codes", align_bytes=64)
         out_words = out_1[0].rearrange("p c r -> p (c r)").bitcast(I32)
-        store_down_to = {cols.start: cols for cols in from_top(STORE_EDGES)}
-        for cols in from_top(QUANT_EDGES):
+        store_up_to = {cols.stop: cols for cols in pieces(STORE_EDGES)}
+        for cols in pieces(QUANT_EDGES):
             nc.vector.quantize_mx(
                 out=out_codes[:, cols].bitcast(FP8X4),
                 scales=out_scale[:, cols],
                 in_=woven[:, cols, :].rearrange("p c t -> p (c t)"),
             )
-            if cols.start in store_down_to:
-                stored = store_down_to[cols.start]
+            if cols.stop in store_up_to:
+                stored = store_up_to[cols.stop]
                 nc.sync.dma_start(out_words[:, stored], out_codes[:, stored])
         for r in range(RUN):
             queue = nc.sync if r % 2 == 0 else nc.scalar

@@ -1,6 +1,7 @@
 from contextlib import ExitStack
 
 import concourse.mybir as mybir
+from concourse.masks import make_identity
 
 K, T, S, N, U = 512, 2048, 512, 512, 1024
 FLOPS = 2 * K * S * N
@@ -69,6 +70,9 @@ def tile_picked_kalman8_none_po_kernel(
         var = {0: keep.tile([P, U], F32, name="var0", tag="var0", align_bytes=64)}
 
         nc.vector.memset(scale_table[:].bitcast(I32), 0)
+        ident = keep.tile([P, P], F32, name="ident")
+        nc.vector.memset(ident[:], 0.0)
+        make_identity(nc, ident[:], nomemset=True)
         nc.sync.dma_start(var[0][:], va_rows[:, 0, :])
         nc.sync.dma_start(offs_sb[:], offs)
         nc.sync.dma_start(trk_sb[:], trk)
@@ -173,6 +177,24 @@ def tile_picked_kalman8_none_po_kernel(
             for keeps, part in zip(stay[t], two(diff[t])):
                 nc.vector.scalar_tensor_tensor(part, keeps, 1.0, part, ALU.subtract, ALU.mult)
 
+        def blocks(ap):
+            return [ap[:, b * P : (b + 1) * P] for b in range(HALF // P)]
+
+        def add_turned(t, neg_y_sb):
+            nc.scalar.copy(neg_y_sb[:], two(neg_y[t])[1])
+            bank = psum.tile([P, HALF], F32, name=f"turned{t}")
+            for out, a, b in zip(blocks(bank), blocks(neg_y_sb), blocks(two(old[t])[1])):
+                nc.tensor.matmul(out, lhsT=a, rhs=ident[:], is_transpose=True, start=True, stop=False)
+                nc.tensor.matmul(out, lhsT=b, rhs=ident[:], is_transpose=True, start=False, stop=True)
+            return bank
+
+        def turn_back(t, turned, turned_sb):
+            nc.scalar.copy(turned_sb, turned[:])
+            bank = psum.tile([P, HALF], F32, name=f"diff_bank{t}")
+            for out, a in zip(blocks(bank), blocks(turned_sb)):
+                nc.tensor.transpose(out, a, ident[:])
+            return bank
+
         def take_roots(t, picked, roots):
             for h in range(2):
                 look_up(picked[h], var[t], h)
@@ -185,8 +207,8 @@ def tile_picked_kalman8_none_po_kernel(
 
         planes = keep.tile([P, PACK * U], F32, name="planes")
         by_tile = planes[:].rearrange("p (q t c) -> p t q c", q=4, t=PACK)
-        stay[3] = [by_tile[:, 2, 3, :], by_tile[:, 3, 3, :]]
-        roots3 = [by_tile[:, 3, h, :] for h in range(2)]
+        stay[3] = [by_tile[:, 3, h, :] for h in range(2)]
+        roots3 = [placed([P, HALF], F32, "root3", 6)[:], by_tile[:, 2, 0, :]]
         old[3] = keep.tile([P, S], F32, name="old3")[:]
         picked3 = keep.tile([P, S], F32, name="picked3")
         picked1_second = keep.tile([P, HALF], F32, name="picked1_second")
@@ -203,7 +225,12 @@ def tile_picked_kalman8_none_po_kernel(
         look_up_states(3, 0)
         square(2, roots2)
         look_up_states(3, 1)
-        take_roots(3, two(picked3), roots3)
+        turned3 = add_turned(3, picked1_second)
+        for h in range(2):
+            look_up(two(picked3)[h], var[3], h)
+        diff3_second = turn_back(3, turned3, by_tile[:, 2, 1, :])
+        for h in range(2):
+            root(roots3[h], two(picked3)[h])
         square(3, roots3)
 
         scatter(0, halves[0], new_part[:])
@@ -228,21 +255,24 @@ def tile_picked_kalman8_none_po_kernel(
         differ(3, 0)
         scatter(2, whole, diff[2])
         store(2)
-        differ(3, 1)
-        nc.vector.tensor_copy(by_tile[:, 2, 0:2, :], quarters(2)[:, 0:2, :])
-        weigh(3)
-        nc.vector.tensor_copy(by_tile[:, 2, 3, :], quarters(2)[:, 3, :])
+        for keeps, part, source in zip(stay[3], two(diff[3]), [two(diff[3])[0], diff3_second[:]]):
+            nc.vector.scalar_tensor_tensor(part, keeps, 1.0, source, ALU.subtract, ALU.mult)
+        split = "p q (h c) -> p h q c"
+        nc.vector.tensor_copy(by_tile[:, 2, 0:3, :].rearrange(split, h=2), quarters(2)[:, 0:3, :].rearrange(split, h=2))
 
-        woven = keep.tile([P, U, PACK], BF16, name="woven", align_bytes=64)
+        woven = placed([P, U, PACK], BF16, "woven", 6)
 
         woven_walk = woven[:].rearrange("p (q c i) t -> p q c t i", q=4, i=WALK)
         planes_walk = planes[:].rearrange("p (q t c i) -> p q c t i", q=4, t=PACK, i=WALK)
 
-        twice = planes_walk[:, 2, :, 0:2, :].unsqueeze(2).to_broadcast([P, QUARTER // WALK, 2, 2, WALK])
-        nc.scalar.copy(woven_walk[:, 2].rearrange("p c (a t) i -> p c a t i", a=2), twice)
-        nc.scalar.copy(woven[:, 2 * QUARTER : 3 * QUARTER, 2], quarters(2)[:, 2, :])
+        eighths = [slice(h * EIGHTH // WALK, (h + 1) * EIGHTH // WALK) for h in range(2)]
+        for groups in eighths:
+            twice = planes_walk[:, 3, groups, 0:2, :].unsqueeze(2).to_broadcast([P, EIGHTH // WALK, 2, 2, WALK])
+            nc.scalar.copy(woven_walk[:, 3, groups].rearrange("p c (a t) i -> p c a t i", a=2), twice)
+        for cols in pieces((6 * EIGHTH, 7 * EIGHTH, U)):
+            nc.scalar.copy(woven[:, cols, 2], state[2][:, cols])
         nc.scalar.copy(woven_walk[:, 0:2], planes_walk[:, 0:2])
-        nc.scalar.copy(woven_walk[:, 3], planes_walk[:, 3])
+        nc.scalar.copy(woven_walk[:, 2, :, 0:3, :], planes_walk[:, 2, :, 0:3, :])
         scatter(3, whole, diff[3])
         store(3)
         for cols in pieces(ROUND_EDGES):

@@ -58,7 +58,7 @@ def tile_picked_kalman8_none_po_kernel(
         psum = ctx.enter_context(tc.psum_pool(name="psum", bufs=1))
 
         def placed(shape, dtype, name, place, across=0):
-            offset = place * ROW_BYTES + across * ROW_BYTES // 2
+            offset = (place + 1) * ROW_BYTES + across * ROW_BYTES // 2
             return shared.tile(shape, dtype, name=name, offset=offset, align_bytes=64)
 
         trk_sb = keep.tile([P, S // GROUP], U16, name="trk_sb")
@@ -144,6 +144,8 @@ def tile_picked_kalman8_none_po_kernel(
         stay = {t: [strip[:, :HALF], strip[:, S:]] for t, strip in enumerate(strips)}
         diff = {t + 1: strip[:, :S] for t, strip in enumerate(strips)}
         old = {t: keep.tile([P, S], F32, name=f"old{t}")[:] for t in range(PACK - 1)}
+        planes = keep.tile([P, PACK * U], F32, name="planes")
+        by_tile = planes[:].rearrange("p (q t c) -> p t q c", q=4, t=PACK)
         picked_root0 = two(keep.tile([P, S], F32, name="picked_root0"))
         for h in range(2):
             look_up(picked_root0[h], root0, h)
@@ -173,16 +175,17 @@ def tile_picked_kalman8_none_po_kernel(
         def differ(t, h):
             nc.vector.tensor_tensor(two(diff[t])[h], two(old[t])[h], two(neg_y[t])[h], ALU.add)
 
-        def weigh(t):
-            for keeps, part in zip(stay[t], two(diff[t])):
-                nc.vector.scalar_tensor_tensor(part, keeps, 1.0, part, ALU.subtract, ALU.mult)
+        def weigh(t, second):
+            for h in range(2):
+                source = (two(diff[t])[0], second)[h]
+                nc.vector.scalar_tensor_tensor(two(diff[t])[h], stay[t][h], 1.0, source, ALU.subtract, ALU.mult)
 
         def blocks(ap):
             return [ap[:, b * P : (b + 1) * P] for b in range(HALF // P)]
 
         def add_turned(t, neg_y_sb):
             nc.scalar.copy(neg_y_sb[:], two(neg_y[t])[1])
-            bank = psum.tile([P, HALF], F32, name=f"turned{t}")
+            bank = psum.tile([P, HALF], F32, name=f"turned{t}", tag="turned")
             for out, a, b in zip(blocks(bank), blocks(neg_y_sb), blocks(two(old[t])[1])):
                 nc.tensor.matmul(out, lhsT=a, rhs=ident[:], is_transpose=True, start=True, stop=False)
                 nc.tensor.matmul(out, lhsT=b, rhs=ident[:], is_transpose=True, start=False, stop=True)
@@ -205,27 +208,33 @@ def tile_picked_kalman8_none_po_kernel(
             for h in range(2):
                 nc.scalar.square(stay[t][h], roots[h])
 
-        planes = keep.tile([P, PACK * U], F32, name="planes")
-        by_tile = planes[:].rearrange("p (q t c) -> p t q c", q=4, t=PACK)
         stay[3] = [by_tile[:, 3, h, :] for h in range(2)]
-        roots3 = [placed([P, HALF], F32, "root3", 6)[:], by_tile[:, 2, 0, :]]
+        picked1_second = placed([P, HALF], F32, "picked1_second", -1)
+        roots3 = [picked1_second[:], by_tile[:, 2, 0, :]]
         old[3] = keep.tile([P, S], F32, name="old3")[:]
         picked3 = keep.tile([P, S], F32, name="picked3")
-        picked1_second = keep.tile([P, HALF], F32, name="picked1_second")
 
         for h in range(2):
             look_up_states(1, h)
-        roots1 = two(old[2])
+        across = slice(HALF // 2, HALF // 2 + HALF)
+        roots1 = [old[2][:, across], picked3[:, across]]
         take_roots(1, [two(old[3])[0], picked1_second[:]], roots1)
         square(1, roots1)
-        look_up_states(2, 0)
-        roots2 = [picked3[:, HALF // 2 : HALF // 2 + HALF], two(old[3])[1]]
-        take_roots(2, [two(old[2])[1], two(old[3])[0]], roots2)
-        look_up_states(2, 1)
+        for h in range(2):
+            look_up_states(2, h)
+        turned2 = add_turned(2, picked1_second)
+        picked2 = [two(old[3])[0], two(picked3)[1]]
+        for h in range(2):
+            look_up(picked2[h], var[2], h)
+        turned2_sb = placed([P, HALF], F32, "turned2_sb", later.index((var, 2)))
+        diff2_second = turn_back(2, turned2, turned2_sb[:])
+        roots2 = [two(picked3)[0], two(old[3])[1]]
+        for h in range(2):
+            root(roots2[h], picked2[h])
         look_up_states(3, 0)
         square(2, roots2)
         look_up_states(3, 1)
-        turned3 = add_turned(3, picked1_second)
+        turned3 = add_turned(3, turned2_sb)
         for h in range(2):
             look_up(two(picked3)[h], var[3], h)
         diff3_second = turn_back(3, turned3, by_tile[:, 2, 1, :])
@@ -244,34 +253,29 @@ def tile_picked_kalman8_none_po_kernel(
         store(0)
         nc.sync.dma_start(by_tile[:, 0, :, :], quarters(0))
         differ(1, 1)
-        weigh(1)
+        weigh(1, two(diff[1])[1])
         scatter(1, halves[0], diff[1])
         differ(2, 0)
         scatter(1, halves[1], diff[1])
         nc.sync.dma_start(by_tile[:, 1, :, :], quarters(1))
         store(1)
-        differ(2, 1)
-        weigh(2)
+        weigh(2, diff2_second[:])
         differ(3, 0)
         scatter(2, whole, diff[2])
         store(2)
-        for keeps, part, source in zip(stay[3], two(diff[3]), [two(diff[3])[0], diff3_second[:]]):
-            nc.vector.scalar_tensor_tensor(part, keeps, 1.0, source, ALU.subtract, ALU.mult)
+        weigh(3, diff3_second[:])
         split = "p q (h c) -> p h q c"
         nc.vector.tensor_copy(by_tile[:, 2, 0:3, :].rearrange(split, h=2), quarters(2)[:, 0:3, :].rearrange(split, h=2))
 
-        woven = placed([P, U, PACK], BF16, "woven", 6)
+        woven = placed([P, U, PACK], BF16, "woven", -1)
 
         woven_walk = woven[:].rearrange("p (q c i) t -> p q c t i", q=4, i=WALK)
         planes_walk = planes[:].rearrange("p (q t c i) -> p q c t i", q=4, t=PACK, i=WALK)
 
-        eighths = [slice(h * EIGHTH // WALK, (h + 1) * EIGHTH // WALK) for h in range(2)]
-        for groups in eighths:
-            twice = planes_walk[:, 3, groups, 0:2, :].unsqueeze(2).to_broadcast([P, EIGHTH // WALK, 2, 2, WALK])
-            nc.scalar.copy(woven_walk[:, 3, groups].rearrange("p c (a t) i -> p c a t i", a=2), twice)
-        for cols in pieces((6 * EIGHTH, 7 * EIGHTH, U)):
-            nc.scalar.copy(woven[:, cols, 2], state[2][:, cols])
-        nc.scalar.copy(woven_walk[:, 0:2], planes_walk[:, 0:2])
+        nc.scalar.copy(woven_walk[:, 3, :, 0:2, :], planes_walk[:, 3, :, 0:2, :])
+        nc.scalar.copy(woven[:, 3 * QUARTER :, 2], quarters(2)[:, 3, :])
+        nc.scalar.copy(woven_walk[:, 0:2, 2:, 0:3, :], planes_walk[:, 0:2, 2:, 0:3, :])
+        nc.scalar.copy(woven_walk[:, 0:2, :2], planes_walk[:, 0:2, :2])
         nc.scalar.copy(woven_walk[:, 2, :, 0:3, :], planes_walk[:, 2, :, 0:3, :])
         scatter(3, whole, diff[3])
         store(3)

@@ -134,8 +134,11 @@ def tile_picked_kalman8_none_po_kernel(
             )
             return bank[:]
 
-        neg_y0 = [project(0, share) for share in halves]
-        neg_y = {t: project(t, whole) for t in range(1, PACK)}
+        neg_y0, neg_y = [project(0, halves[0])], {1: [None, project(1, halves[1])]}
+        neg_y0.append(project(0, halves[1]))
+        neg_y[1][0] = project(1, halves[0])
+        for t in range(2, PACK):
+            neg_y[t] = two(project(t, whole))
 
         def look_up(out, window, h):
             nc.scalar.activation(out, window[:].indirect(halves[h][1]), ACT.Copy)
@@ -173,7 +176,7 @@ def tile_picked_kalman8_none_po_kernel(
         nc.vector.tensor_tensor(two(old[0])[1], two(old[0])[1], stay[0][1], ALU.mult)
 
         def differ(t, h):
-            nc.vector.tensor_tensor(two(diff[t])[h], two(old[t])[h], two(neg_y[t])[h], ALU.add)
+            nc.vector.tensor_tensor(two(diff[t])[h], two(old[t])[h], neg_y[t][h], ALU.add)
 
         def weigh(t, second):
             for h in range(2):
@@ -183,8 +186,10 @@ def tile_picked_kalman8_none_po_kernel(
         def blocks(ap):
             return [ap[:, b * P : (b + 1) * P] for b in range(HALF // P)]
 
+        def copy_y(t, neg_y_sb):
+            nc.scalar.copy(neg_y_sb[:, :], neg_y[t][1])
+
         def add_turned(t, neg_y_sb):
-            nc.scalar.copy(neg_y_sb[:], two(neg_y[t])[1])
             bank = psum.tile([P, HALF], F32, name=f"turned{t}", tag="turned")
             for out, a, b in zip(blocks(bank), blocks(neg_y_sb), blocks(two(old[t])[1])):
                 nc.tensor.matmul(out, lhsT=a, rhs=ident[:], is_transpose=True, start=True, stop=False)
@@ -193,16 +198,10 @@ def tile_picked_kalman8_none_po_kernel(
 
         def turn_back(t, turned, turned_sb):
             nc.scalar.copy(turned_sb, turned[:])
-            bank = psum.tile([P, HALF], F32, name=f"diff_bank{t}")
+            bank = psum.tile([P, HALF], F32, name=f"diff_bank{t}", tag="diff_bank")
             for out, a in zip(blocks(bank), blocks(turned_sb)):
                 nc.tensor.transpose(out, a, ident[:])
             return bank
-
-        def take_roots(t, picked, roots):
-            for h in range(2):
-                look_up(picked[h], var[t], h)
-            for h in range(2):
-                root(roots[h], picked[h])
 
         def square(t, roots):
             for h in range(2):
@@ -212,35 +211,23 @@ def tile_picked_kalman8_none_po_kernel(
         picked1_second = placed([P, HALF], F32, "picked1_second", -1)
         roots3 = [picked1_second[:], by_tile[:, 2, 0, :]]
         old[3] = keep.tile([P, S], F32, name="old3")[:]
+        diff[3] = placed([P, S], F32, "diff3", later.index((var, 2)))[:]
         picked3 = keep.tile([P, S], F32, name="picked3")
 
-        for h in range(2):
+        neg_y_sb = keep.tile([P, HALF], F32, name="neg_y_sb")
+        copy_y(1, neg_y_sb)
+        for h in (1, 0):
             look_up_states(1, h)
-        across = slice(HALF // 2, HALF // 2 + HALF)
-        roots1 = [old[2][:, across], picked3[:, across]]
-        take_roots(1, [two(old[3])[0], picked1_second[:]], roots1)
+        turned1 = add_turned(1, neg_y_sb)
+        picked1 = [two(old[3])[0], picked1_second[:]]
+        for h in range(2):
+            look_up(picked1[h], var[1], h)
+        turned1_sb = placed([P, HALF], F32, "turned1_sb", later.index((var, 1)))
+        diff1_second = turn_back(1, turned1, turned1_sb[:])
+        roots1 = [two(old[2])[0], two(picked3)[0]]
+        for h in range(2):
+            root(roots1[h], picked1[h])
         square(1, roots1)
-        for h in range(2):
-            look_up_states(2, h)
-        turned2 = add_turned(2, picked1_second)
-        picked2 = [two(old[3])[0], two(picked3)[1]]
-        for h in range(2):
-            look_up(picked2[h], var[2], h)
-        turned2_sb = placed([P, HALF], F32, "turned2_sb", later.index((var, 2)))
-        diff2_second = turn_back(2, turned2, turned2_sb[:])
-        roots2 = [two(picked3)[0], two(old[3])[1]]
-        for h in range(2):
-            root(roots2[h], picked2[h])
-        look_up_states(3, 0)
-        square(2, roots2)
-        look_up_states(3, 1)
-        turned3 = add_turned(3, turned2_sb)
-        for h in range(2):
-            look_up(two(picked3)[h], var[3], h)
-        diff3_second = turn_back(3, turned3, by_tile[:, 2, 1, :])
-        for h in range(2):
-            root(roots3[h], two(picked3)[h])
-        square(3, roots3)
 
         scatter(0, halves[0], new_part[:])
         weigh_y0(1)
@@ -252,16 +239,42 @@ def tile_picked_kalman8_none_po_kernel(
 
         store(0)
         nc.sync.dma_start(by_tile[:, 0, :, :], quarters(0))
-        differ(1, 1)
-        weigh(1, two(diff[1])[1])
+        weigh(1, diff1_second[:])
+
+        look_up_states(2, 0)
+        picked2 = [two(picked3)[0], two(old[3])[0]]
+        for h in range(2):
+            look_up(picked2[h], var[2], h)
+        look_up_states(2, 1)
+        roots2 = [two(picked3)[1], two(old[3])[1]]
+        copy_y(2, picked1_second)
+        turned2 = add_turned(2, picked1_second)
+        root(roots2[0], picked2[0])
+        diff2_second = turn_back(2, turned2, two(diff[3])[0])
+        root(roots2[1], picked2[1])
+        square(2, roots2)
+
         scatter(1, halves[0], diff[1])
         differ(2, 0)
         scatter(1, halves[1], diff[1])
         nc.sync.dma_start(by_tile[:, 1, :, :], quarters(1))
         store(1)
         weigh(2, diff2_second[:])
+
+        for h in range(2):
+            look_up_states(3, h)
+        copy_y(3, stay[2][0])
+        turned3 = add_turned(3, stay[2][0])
+        for h in range(2):
+            look_up(two(picked3)[h], var[3], h)
+        diff3_second = turn_back(3, turned3, by_tile[:, 2, 1, :])
+        for h in range(2):
+            root(roots3[h], two(picked3)[h])
+        square(3, roots3)
+
+        scatter(2, halves[0], diff[2])
         differ(3, 0)
-        scatter(2, whole, diff[2])
+        scatter(2, halves[1], diff[2])
         store(2)
         weigh(3, diff3_second[:])
         split = "p q (h c) -> p h q c"

@@ -119,9 +119,9 @@ def tile_picked_kalman8_none_po_kernel(
         for out, columns in zip(two(x_codes), half_columns):
             nc.vector.tensor_copy(out, x_table[:].bitcast(U32).indirect(offs_sb[:, columns]))
 
-        def project(t, share):
+        def project(t, share, tag):
             entries = share[0]
-            bank = psum.tile([P, entries.stop - entries.start], F32, name=f"neg_y{t}_{entries.start}")
+            bank = psum.tile([P, entries.stop - entries.start], F32, name=f"neg_y{t}_{entries.start}", tag=tag)
             cols = slice(t * P, (t + 1) * P)
             nc.tensor.matmul_mx(
                 out=bank[:],
@@ -134,11 +134,9 @@ def tile_picked_kalman8_none_po_kernel(
             )
             return bank[:]
 
-        neg_y0, neg_y = [project(0, halves[0])], {1: [None, project(1, halves[1])]}
-        neg_y0.append(project(0, halves[1]))
-        neg_y[1][0] = project(1, halves[0])
-        for t in range(2, PACK):
-            neg_y[t] = two(project(t, whole))
+        neg_y0, neg_y = [project(0, halves[0], "y0a")], {1: [None, project(1, halves[1], "y1b")]}
+        neg_y0.append(project(0, halves[1], "y0b"))
+        neg_y[1][0] = project(1, halves[0], "y1a")
 
         def look_up(out, window, h):
             nc.scalar.activation(out, window[:].indirect(halves[h][1]), ACT.Copy)
@@ -178,8 +176,8 @@ def tile_picked_kalman8_none_po_kernel(
         def differ(t, h):
             nc.vector.tensor_tensor(two(diff[t])[h], two(old[t])[h], neg_y[t][h], ALU.add)
 
-        def weigh(t, second):
-            for h in range(2):
+        def weigh(t, second, order=(0, 1)):
+            for h in order:
                 source = (two(diff[t])[0], second)[h]
                 nc.vector.scalar_tensor_tensor(two(diff[t])[h], stay[t][h], 1.0, source, ALU.subtract, ALU.mult)
 
@@ -190,56 +188,59 @@ def tile_picked_kalman8_none_po_kernel(
             nc.scalar.copy(neg_y_sb[:, :], neg_y[t][1])
 
         def add_turned(t, neg_y_sb):
-            bank = psum.tile([P, HALF], F32, name=f"turned{t}", tag="turned")
-            for out, a, b in zip(blocks(bank), blocks(neg_y_sb), blocks(two(old[t])[1])):
+            bank = psum.tile([P, HALF], F32, name=f"turned{t}", tag="y2" if t == 1 else "turned")
+            for out, a, b in zip(blocks(bank), blocks(two(old[t])[1]), blocks(neg_y_sb)):
                 nc.tensor.matmul(out, lhsT=a, rhs=ident[:], is_transpose=True, start=True, stop=False)
                 nc.tensor.matmul(out, lhsT=b, rhs=ident[:], is_transpose=True, start=False, stop=True)
             return bank
 
         def turn_back(t, turned, turned_sb):
             nc.scalar.copy(turned_sb, turned[:])
-            bank = psum.tile([P, HALF], F32, name=f"diff_bank{t}", tag="diff_bank")
+            bank = psum.tile([P, HALF], F32, name=f"diff_bank{t}", tag="y3" if t == 1 else "diff_bank")
             for out, a in zip(blocks(bank), blocks(turned_sb)):
                 nc.tensor.transpose(out, a, ident[:])
             return bank
 
-        def square(t, roots):
-            for h in range(2):
+        def square(t, roots, order=(0, 1)):
+            for h in order:
                 nc.scalar.square(stay[t][h], roots[h])
 
-        stay[3] = [by_tile[:, 3, h, :] for h in range(2)]
+        stay[3] = [keep.tile([P, HALF], F32, name="stay3")[:], by_tile[:, 3, 1, :]]
+        stay[2][0] = planes[:, 2 * QUARTER + HALF // 4 :][:, :HALF]
         picked1_second = placed([P, HALF], F32, "picked1_second", -1)
-        roots3 = [picked1_second[:], by_tile[:, 2, 0, :]]
+        roots3 = [by_tile[:, 3, 0, :], by_tile[:, 2, 0, :]]
         old[3] = keep.tile([P, S], F32, name="old3")[:]
         diff[3] = placed([P, S], F32, "diff3", later.index((var, 2)))[:]
         picked3 = keep.tile([P, S], F32, name="picked3")
 
         neg_y_sb = keep.tile([P, HALF], F32, name="neg_y_sb")
         copy_y(1, neg_y_sb)
-        for h in (1, 0):
+        for h in range(2):
             look_up_states(1, h)
         turned1 = add_turned(1, neg_y_sb)
         picked1 = [two(old[3])[0], picked1_second[:]]
-        for h in range(2):
+        for h in (1, 0):
             look_up(picked1[h], var[1], h)
         turned1_sb = placed([P, HALF], F32, "turned1_sb", later.index((var, 1)))
         diff1_second = turn_back(1, turned1, turned1_sb[:])
-        roots1 = [two(old[2])[0], two(picked3)[0]]
-        for h in range(2):
+        roots1 = [two(picked3)[0], two(old[2])[0]]
+        for h in (1, 0):
             root(roots1[h], picked1[h])
-        square(1, roots1)
+        square(1, roots1, (1, 0))
 
         scatter(0, halves[0], new_part[:])
         weigh_y0(1)
-        differ(1, 0)
         scatter(0, halves[1], new_part[:])
+        differ(1, 0)
 
         def quarters(t):
             return state[t][:].rearrange("p (q c) -> p q c", q=4)
 
         store(0)
         nc.sync.dma_start(by_tile[:, 0, :, :], quarters(0))
-        weigh(1, diff1_second[:])
+        weigh(1, diff1_second[:], (1, 0))
+        for t in range(2, PACK):
+            neg_y[t] = two(project(t, whole, f"y{t}"))
 
         look_up_states(2, 0)
         picked2 = [two(picked3)[0], two(old[3])[0]]
@@ -254,9 +255,9 @@ def tile_picked_kalman8_none_po_kernel(
         root(roots2[1], picked2[1])
         square(2, roots2)
 
-        scatter(1, halves[0], diff[1])
-        differ(2, 0)
         scatter(1, halves[1], diff[1])
+        differ(2, 0)
+        scatter(1, halves[0], diff[1])
         nc.sync.dma_start(by_tile[:, 1, :, :], quarters(1))
         store(1)
         weigh(2, diff2_second[:])

@@ -138,6 +138,9 @@ def tile_picked_kalman8_none_po_kernel(
         neg_y0.append(project(0, halves[1], "y0b"))
         neg_y[1][0] = project(1, halves[0], "y1a")
 
+        def look_up_all(out, window):
+            nc.scalar.activation(out, window[:].indirect(whole[1]), ACT.Copy)
+
         def look_up(out, window, h):
             nc.scalar.activation(out, window[:].indirect(halves[h][1]), ACT.Copy)
 
@@ -147,9 +150,9 @@ def tile_picked_kalman8_none_po_kernel(
         old = {t: keep.tile([P, S], F32, name=f"old{t}")[:] for t in range(PACK - 1)}
         planes = keep.tile([P, PACK * U], F32, name="planes")
         by_tile = planes[:].rearrange("p (q t c) -> p t q c", q=4, t=PACK)
-        picked_root0 = two(keep.tile([P, S], F32, name="picked_root0"))
-        for h in range(2):
-            look_up(picked_root0[h], root0, h)
+        picked_all = keep.tile([P, S], F32, name="picked_root0")
+        picked_root0 = two(picked_all)
+        look_up_all(picked_all[:], root0)
         for h in range(2):
             nc.scalar.square(stay[0][h], picked_root0[h])
 
@@ -215,8 +218,7 @@ def tile_picked_kalman8_none_po_kernel(
 
         neg_y_sb = keep.tile([P, HALF], F32, name="neg_y_sb")
         copy_y(1, neg_y_sb)
-        for h in range(2):
-            look_up_states(1, h)
+        look_up_all(old[1], state[1])
         turned1 = add_turned(1, neg_y_sb)
         picked1 = [two(old[3])[0], picked1_second[:]]
         for h in (1, 0):

@@ -147,14 +147,21 @@ def tile_picked_kalman8_none_po_kernel(
         strips = [keep.tile([P, S + HALF], F32, name=f"strip{t}") for t in range(PACK - 1)]
         stay = {t: [strip[:, :HALF], strip[:, S:]] for t, strip in enumerate(strips)}
         diff = {t + 1: strip[:, :S] for t, strip in enumerate(strips)}
-        old = {t: keep.tile([P, S], F32, name=f"old{t}")[:] for t in range(PACK - 1)}
+        old = {t: keep.tile([P, S], F32, name=f"old{t}")[:] for t in (0, 2)}
+        around = keep.tile([P, 4, HALF], F32, name="around")
+        old[1] = around[:, 1:3, :].rearrange("p a c -> p (a c)")
+        stay_last = around[:, 0:4:3, 0:GROUP:2]
         planes = keep.tile([P, PACK * U], F32, name="planes")
         by_tile = planes[:].rearrange("p (q t c) -> p t q c", q=4, t=PACK)
         picked_all = keep.tile([P, S], F32, name="picked_root0")
         picked_root0 = two(picked_all)
         look_up_all(picked_all[:], root0)
-        for h in range(2):
-            nc.scalar.square(stay[0][h], picked_root0[h])
+        by_half = "p (h c) -> p h c"
+        nc.scalar.square(strips[0][:].rearrange(by_half, c=HALF)[:, 0:3:2, :], picked_all[:].rearrange(by_half, h=2))
+
+        in_two = "p (a c) -> p a c"
+        most, last = slice(0, HALF - GROUP), slice(HALF - GROUP, HALF)
+        nc.scalar.square(stay_last, picked_root0[1][:, last].rearrange(in_two, a=2))
 
         def look_up_states(t, h):
             look_up(two(old[t])[h], state[t], h)
@@ -169,18 +176,18 @@ def tile_picked_kalman8_none_po_kernel(
         look_up_states(0, 1)
         new_part = keep.tile([P, S], F32, name="new_part")
 
-        def weigh_y0(h):
-            nc.vector.scalar_tensor_tensor(two(new_part)[h], stay[0][h], 1.0, neg_y0[h], ALU.subtract, ALU.mult)
+        def weigh_y0(out, keeps, neg_part):
+            nc.vector.scalar_tensor_tensor(out, keeps, 1.0, neg_part, ALU.subtract, ALU.mult)
 
         nc.vector.tensor_tensor(two(old[0])[0], state[0][:].indirect(halves[0][1]), stay[0][0], ALU.mult)
-        weigh_y0(0)
+        weigh_y0(two(new_part)[0], stay[0][0], neg_y0[0])
         nc.vector.tensor_tensor(two(old[0])[1], two(old[0])[1], stay[0][1], ALU.mult)
 
         def differ(t, h):
             nc.vector.tensor_tensor(two(diff[t])[h], two(old[t])[h], neg_y[t][h], ALU.add)
 
-        def weigh(t, second, order=(0, 1)):
-            for h in order:
+        def weigh(t, second):
+            for h in range(2):
                 source = (two(diff[t])[0], second)[h]
                 nc.vector.scalar_tensor_tensor(two(diff[t])[h], stay[t][h], 1.0, source, ALU.subtract, ALU.mult)
 
@@ -204,8 +211,8 @@ def tile_picked_kalman8_none_po_kernel(
                 nc.tensor.transpose(out, a, ident[:])
             return bank
 
-        def square(t, roots, order=(0, 1)):
-            for h in order:
+        def square(t, roots):
+            for h in range(2):
                 nc.scalar.square(stay[t][h], roots[h])
 
         stay[3] = [keep.tile([P, HALF], F32, name="stay3")[:], by_tile[:, 3, 1, :]]
@@ -221,34 +228,35 @@ def tile_picked_kalman8_none_po_kernel(
         look_up_all(old[1], state[1])
         turned1 = add_turned(1, neg_y_sb)
         picked1 = [two(old[3])[0], picked1_second[:]]
-        for h in (1, 0):
+        for h in range(2):
             look_up(picked1[h], var[1], h)
         turned1_sb = placed([P, HALF], F32, "turned1_sb", later.index((var, 1)))
         diff1_second = turn_back(1, turned1, turned1_sb[:])
-        roots1 = [two(picked3)[0], two(old[2])[0]]
-        for h in (1, 0):
+        roots1 = [two(old[2])[0], two(picked3)[0]]
+        for h in range(2):
             root(roots1[h], picked1[h])
-        square(1, roots1, (1, 0))
+        square(1, roots1)
 
         scatter(0, halves[0], new_part[:])
-        weigh_y0(1)
-        scatter(0, halves[1], new_part[:])
+        second = two(new_part)[1]
+        weigh_y0(second[:, most], stay[0][1][:, most], neg_y0[1][:, most])
+        weigh_y0(second[:, last].rearrange(in_two, a=2), stay_last, neg_y0[1][:, last].rearrange(in_two, a=2))
         differ(1, 0)
+        scatter(0, halves[1], new_part[:])
 
         def quarters(t):
             return state[t][:].rearrange("p (q c) -> p q c", q=4)
 
         store(0)
         nc.sync.dma_start(by_tile[:, 0, :, :], quarters(0))
-        weigh(1, diff1_second[:], (1, 0))
+        weigh(1, diff1_second[:])
         for t in range(2, PACK):
             neg_y[t] = two(project(t, whole, f"y{t}"))
 
-        look_up_states(2, 0)
+        look_up_all(old[2], state[2])
         picked2 = [two(picked3)[0], two(old[3])[0]]
         for h in range(2):
             look_up(picked2[h], var[2], h)
-        look_up_states(2, 1)
         roots2 = [two(picked3)[1], two(old[3])[1]]
         copy_y(2, picked1_second)
         turned2 = add_turned(2, picked1_second)
@@ -257,9 +265,9 @@ def tile_picked_kalman8_none_po_kernel(
         root(roots2[1], picked2[1])
         square(2, roots2)
 
-        scatter(1, halves[1], diff[1])
-        differ(2, 0)
         scatter(1, halves[0], diff[1])
+        differ(2, 0)
+        scatter(1, halves[1], diff[1])
         nc.sync.dma_start(by_tile[:, 1, :, :], quarters(1))
         store(1)
         weigh(2, diff2_second[:])
@@ -268,8 +276,7 @@ def tile_picked_kalman8_none_po_kernel(
             look_up_states(3, h)
         copy_y(3, stay[2][0])
         turned3 = add_turned(3, stay[2][0])
-        for h in range(2):
-            look_up(two(picked3)[h], var[3], h)
+        look_up_all(picked3[:], var[3])
         diff3_second = turn_back(3, turned3, by_tile[:, 2, 1, :])
         for h in range(2):
             root(roots3[h], two(picked3)[h])

@@ -285,10 +285,10 @@ def tile_picked_kalman8_none_po_kernel(
         scatter(2, halves[0], diff[2])
         differ(3, 0)
         scatter(2, halves[1], diff[2])
+        nc.sync.dma_start(by_tile[:, 2, 2, :], quarters(2)[:, 2, :])
         store(2)
         weigh(3, diff3_second[:])
-        split = "p q (h c) -> p h q c"
-        nc.vector.tensor_copy(by_tile[:, 2, 0:3, :].rearrange(split, h=2), quarters(2)[:, 0:3, :].rearrange(split, h=2))
+        nc.vector.tensor_copy(by_tile[:, 2, 0:2, :], quarters(2)[:, 0:2, :])
 
         woven = placed([P, U, PACK], BF16, "woven", -1)
 

@@ -1,7 +1,6 @@
 from contextlib import ExitStack
 
 import concourse.mybir as mybir
-from concourse.masks import make_identity
 
 K, T, S, N, U = 512, 2048, 512, 512, 1024
 FLOPS = 2 * K * S * N
@@ -27,16 +26,6 @@ ROW_BYTES = 4 * U
 HALF = S // 2
 QUARTER = U // 4
 EIGHTH = U // 8
-WALK = 4
-
-ON_VECTOR = 480
-ROUND_EDGES = (0, 2 * EIGHTH, ON_VECTOR, 6 * EIGHTH, 7 * EIGHTH, U)
-QUANT_EDGES = (0, 2 * EIGHTH, 3 * EIGHTH, 4 * EIGHTH, 6 * EIGHTH, 7 * EIGHTH, U)
-STORE_EDGES = (0, 3 * EIGHTH, 6 * EIGHTH, U)
-
-
-def pieces(edges):
-    return [slice(lo, hi) for lo, hi in zip(edges, edges[1:])]
 
 
 def two(ap):
@@ -58,7 +47,7 @@ def tile_picked_kalman8_none_po_kernel(
         psum = ctx.enter_context(tc.psum_pool(name="psum", bufs=1))
 
         def placed(shape, dtype, name, place, across=0):
-            offset = (place + 1) * ROW_BYTES + across * ROW_BYTES // 2
+            offset = place * ROW_BYTES + across * ROW_BYTES // 2
             return shared.tile(shape, dtype, name=name, offset=offset, align_bytes=64)
 
         trk_sb = keep.tile([P, S // GROUP], U16, name="trk_sb")
@@ -68,24 +57,20 @@ def tile_picked_kalman8_none_po_kernel(
         w_raw = [placed([P, 2, N], F32, f"w_raw{h}", 2 * h, across=1) for h in range(2)]
         w_bf = placed([P, N * PACK], BF16, "w_bf", 4, across=1)
         var = {0: keep.tile([P, U], F32, name="var0", tag="var0", align_bytes=64)}
+        var[1] = keep.tile([P, U], F32, name="var1")
 
         nc.vector.memset(scale_table[:].bitcast(I32), 0)
-        ident = keep.tile([P, P], F32, name="ident")
-        nc.vector.memset(ident[:], 0.0)
-        make_identity(nc, ident[:], nomemset=True)
         nc.sync.dma_start(var[0][:], va_rows[:, 0, :])
         nc.sync.dma_start(offs_sb[:], offs)
         nc.sync.dma_start(trk_sb[:], trk)
         nc.sync.dma_start(scale_table[0:P:SPREAD, :].bitcast(I32), x_scales[0].bitcast(I32))
         for h in range(2):
             nc.sync.dma_start(w_raw[h][:], w_rows[:, 2 * h : 2 * h + 2, :])
+        nc.sync.dma_start(var[1][:], va_rows[:, 1, :])
         nc.sync.dma_start(x_table[:], x_words[0].rearrange("p c r -> p (c r)").bitcast(I32))
-        state = {0: keep.tile([P, U], F32, name="st0")}
-        nc.sync.dma_start(state[0][:], st_rows[:, 0, :])
 
-        whole = (slice(0, S), trk_sb[:])
         half_columns = [slice(h * HALF // GROUP, (h + 1) * HALF // GROUP) for h in range(2)]
-        halves = [(slice(h * HALF, (h + 1) * HALF), trk_sb[:, half_columns[h]]) for h in range(2)]
+        trk_half = [trk_sb[:, cols] for cols in half_columns]
 
         def root(out, in_):
             nc.scalar.activation(out, in_, ACT.Abs_reciprocal_sqrt, bias=1.0, scale=2.0)
@@ -110,7 +95,8 @@ def tile_picked_kalman8_none_po_kernel(
         w_scale = keep.tile([P, N], U8, name="w_scale", align_bytes=64)
         nc.vector.quantize_mx(out=w_codes[:].bitcast(FP8X4), scales=w_scale[:], in_=w_bf[:])
 
-        later = [(state, 1), (var, 1), (state, 2), (state, 3), (var, 2), (var, 3)]
+        state = {}
+        later = [(var, 2), (state, 0), (var, 3), (state, 1), (state, 2), (state, 3)]
         for place, (tiles, t) in enumerate(later):
             tiles[t] = placed([P, U], F32, f"later{place}", place)
             nc.sync.dma_start(tiles[t][:], (st_rows if tiles is state else va_rows)[:, t, :])
@@ -119,9 +105,8 @@ def tile_picked_kalman8_none_po_kernel(
         for out, columns in zip(two(x_codes), half_columns):
             nc.vector.tensor_copy(out, x_table[:].bitcast(U32).indirect(offs_sb[:, columns]))
 
-        def project(t, share, tag):
-            entries = share[0]
-            bank = psum.tile([P, entries.stop - entries.start], F32, name=f"neg_y{t}_{entries.start}", tag=tag)
+        def project(t, entries, name):
+            bank = psum.tile([P, entries.stop - entries.start], F32, name=name)
             cols = slice(t * P, (t + 1) * P)
             nc.tensor.matmul_mx(
                 out=bank[:],
@@ -134,193 +119,114 @@ def tile_picked_kalman8_none_po_kernel(
             )
             return bank[:]
 
-        neg_y0, neg_y = [project(0, halves[0], "y0a")], {1: [None, project(1, halves[1], "y1b")]}
-        neg_y0.append(project(0, halves[1], "y0b"))
-        neg_y[1][0] = project(1, halves[0], "y1a")
+        neg_y = {0: [], 1: []}
+        for h in range(2):
+            for t in range(2):
+                neg_y[t].append(project(t, slice(h * HALF, (h + 1) * HALF), f"neg_y{t}_{h}"))
+        whole_y = {t: project(t, slice(0, S), f"neg_y{t}") for t in (2, 3)}
+        neg_y[3] = two(whole_y[3])
 
-        def look_up_all(out, window):
-            nc.scalar.activation(out, window[:].indirect(whole[1]), ACT.Copy)
+        stay = {t: keep.tile([P, S], F32, name=f"stay{t}") for t in range(PACK)}
+        picked = keep.tile([P, S], F32, name="picked")
+        roots = keep.tile([P, S], F32, name="roots")
+        nc.scalar.activation(picked[:], root0[:].indirect(trk_sb[:]), ACT.Copy)
+        nc.scalar.square(stay[0][:], picked[:])
 
-        def look_up(out, window, h):
-            nc.scalar.activation(out, window[:].indirect(halves[h][1]), ACT.Copy)
+        def gain(t):
+            for h in range(2):
+                nc.scalar.activation(two(picked)[h], var[t][:].indirect(trk_half[h]), ACT.Copy)
+            for h in range(2):
+                root(two(roots)[h], two(picked)[h])
+            for h in range(2):
+                nc.scalar.square(two(stay[t])[h], two(roots)[h])
 
-        strips = [keep.tile([P, S + HALF], F32, name=f"strip{t}") for t in range(PACK - 1)]
-        stay = {t: [strip[:, :HALF], strip[:, S:]] for t, strip in enumerate(strips)}
-        diff = {t + 1: strip[:, :S] for t, strip in enumerate(strips)}
-        old = {t: keep.tile([P, S], F32, name=f"old{t}")[:] for t in (0, 2)}
-        around = keep.tile([P, 4, HALF], F32, name="around")
-        old[1] = around[:, 1:3, :].rearrange("p a c -> p (a c)")
-        stay_last = around[:, 0:4:3, 0:GROUP:2]
-        planes = keep.tile([P, PACK * U], F32, name="planes")
-        by_tile = planes[:].rearrange("p (q t c) -> p t q c", q=4, t=PACK)
-        picked_all = keep.tile([P, S], F32, name="picked_root0")
-        picked_root0 = two(picked_all)
-        look_up_all(picked_all[:], root0)
-        by_half = "p (h c) -> p h c"
-        nc.scalar.square(strips[0][:].rearrange(by_half, c=HALF)[:, 0:3:2, :], picked_all[:].rearrange(by_half, h=2))
+        for t in range(1, PACK):
+            gain(t)
 
-        in_two = "p (a c) -> p a c"
-        most, last = slice(0, HALF - GROUP), slice(HALF - GROUP, HALF)
-        nc.scalar.square(stay_last, picked_root0[1][:, last].rearrange(in_two, a=2))
+        kept = {t: keep.tile([P, S], F32, name=f"kept{t}") for t in range(PACK)}
+        fresh = {t: keep.tile([P, S], F32, name=f"fresh{t}") for t in range(2)}
+        fresh[2], fresh[3] = stay[0], stay[2]
 
-        def look_up_states(t, h):
-            look_up(two(old[t])[h], state[t], h)
+        def weigh_y(out, keeps, neg_part):
+            nc.vector.scalar_tensor_tensor(out, keeps, 1.0, neg_part, ALU.subtract, ALU.mult)
 
-        def scatter(t, share, other):
-            entries, offsets = share
-            nc.vector.tensor_tensor(state[t][:].indirect(offsets), old[t][:, entries], other[:, entries], ALU.add)
+        def weigh_states(t, h):
+            nc.vector.tensor_tensor(two(kept[t])[h], state[t][:].indirect(trk_half[h]), two(stay[t])[h], ALU.mult)
+
+        def add(t, h):
+            nc.vector.tensor_tensor(two(kept[t])[h], two(kept[t])[h], two(fresh[t])[h], ALU.add)
 
         def store(t):
             nc.sync.dma_start(out_rows[:, t, :], state[t][:])
 
-        look_up_states(0, 1)
-        new_part = keep.tile([P, S], F32, name="new_part")
-
-        def weigh_y0(out, keeps, neg_part):
-            nc.vector.scalar_tensor_tensor(out, keeps, 1.0, neg_part, ALU.subtract, ALU.mult)
-
-        nc.vector.tensor_tensor(two(old[0])[0], state[0][:].indirect(halves[0][1]), stay[0][0], ALU.mult)
-        weigh_y0(two(new_part)[0], stay[0][0], neg_y0[0])
-        nc.vector.tensor_tensor(two(old[0])[1], two(old[0])[1], stay[0][1], ALU.mult)
-
-        def differ(t, h):
-            nc.vector.tensor_tensor(two(diff[t])[h], two(old[t])[h], neg_y[t][h], ALU.add)
-
-        def weigh(t, second):
-            for h in range(2):
-                source = (two(diff[t])[0], second)[h]
-                nc.vector.scalar_tensor_tensor(two(diff[t])[h], stay[t][h], 1.0, source, ALU.subtract, ALU.mult)
-
-        def blocks(ap):
-            return [ap[:, b * P : (b + 1) * P] for b in range(HALF // P)]
-
-        def copy_y(t, neg_y_sb):
-            nc.scalar.copy(neg_y_sb[:, :], neg_y[t][1])
-
-        def add_turned(t, neg_y_sb):
-            bank = psum.tile([P, HALF], F32, name=f"turned{t}", tag="y2" if t == 1 else "turned")
-            for out, a, b in zip(blocks(bank), blocks(two(old[t])[1]), blocks(neg_y_sb)):
-                nc.tensor.matmul(out, lhsT=a, rhs=ident[:], is_transpose=True, start=True, stop=False)
-                nc.tensor.matmul(out, lhsT=b, rhs=ident[:], is_transpose=True, start=False, stop=True)
-            return bank
-
-        def turn_back(t, turned, turned_sb):
-            nc.scalar.copy(turned_sb, turned[:])
-            bank = psum.tile([P, HALF], F32, name=f"diff_bank{t}", tag="y3" if t == 1 else "diff_bank")
-            for out, a in zip(blocks(bank), blocks(turned_sb)):
-                nc.tensor.transpose(out, a, ident[:])
-            return bank
-
-        def square(t, roots):
-            for h in range(2):
-                nc.scalar.square(stay[t][h], roots[h])
-
-        stay[3] = [keep.tile([P, HALF], F32, name="stay3")[:], by_tile[:, 3, 1, :]]
-        stay[2][0] = planes[:, 2 * QUARTER + HALF // 4 :][:, :HALF]
-        picked1_second = placed([P, HALF], F32, "picked1_second", -1)
-        roots3 = [by_tile[:, 3, 0, :], by_tile[:, 2, 0, :]]
-        old[3] = keep.tile([P, S], F32, name="old3")[:]
-        diff[3] = placed([P, S], F32, "diff3", later.index((var, 2)))[:]
-        picked3 = keep.tile([P, S], F32, name="picked3")
-
-        neg_y_sb = keep.tile([P, HALF], F32, name="neg_y_sb")
-        copy_y(1, neg_y_sb)
-        look_up_all(old[1], state[1])
-        turned1 = add_turned(1, neg_y_sb)
-        picked1 = [two(old[3])[0], picked1_second[:]]
-        for h in range(2):
-            look_up(picked1[h], var[1], h)
-        turned1_sb = placed([P, HALF], F32, "turned1_sb", later.index((var, 1)))
-        diff1_second = turn_back(1, turned1, turned1_sb[:])
-        roots1 = [two(old[2])[0], two(picked3)[0]]
-        for h in range(2):
-            root(roots1[h], picked1[h])
-        square(1, roots1)
-
-        scatter(0, halves[0], new_part[:])
-        second = two(new_part)[1]
-        weigh_y0(second[:, most], stay[0][1][:, most], neg_y0[1][:, most])
-        weigh_y0(second[:, last].rearrange(in_two, a=2), stay_last, neg_y0[1][:, last].rearrange(in_two, a=2))
-        differ(1, 0)
-        scatter(0, halves[1], new_part[:])
+        planes = keep.tile([P, PACK * U], F32, name="planes")
+        by_tile = planes[:].rearrange("p (q t c) -> p t q c", q=4, t=PACK)
 
         def quarters(t):
             return state[t][:].rearrange("p (q c) -> p q c", q=4)
 
+        for h in range(2):
+            for t in range(2):
+                weigh_y(two(fresh[t])[h], two(stay[t])[h], neg_y[t][h])
+        for h in range(2):
+            weigh_states(0, h)
+        for h in range(2):
+            add(0, h)
+        nc.scalar.activation(state[0][:].indirect(trk_sb[:]), kept[0][:], ACT.Copy)
         store(0)
         nc.sync.dma_start(by_tile[:, 0, :, :], quarters(0))
-        weigh(1, diff1_second[:])
-        for t in range(2, PACK):
-            neg_y[t] = two(project(t, whole, f"y{t}"))
-
-        look_up_all(old[2], state[2])
-        picked2 = [two(picked3)[0], two(old[3])[0]]
-        for h in range(2):
-            look_up(picked2[h], var[2], h)
-        roots2 = [two(picked3)[1], two(old[3])[1]]
-        copy_y(2, picked1_second)
-        turned2 = add_turned(2, picked1_second)
-        root(roots2[0], picked2[0])
-        diff2_second = turn_back(2, turned2, two(diff[3])[0])
-        root(roots2[1], picked2[1])
-        square(2, roots2)
-
-        scatter(1, halves[0], diff[1])
-        differ(2, 0)
-        scatter(1, halves[1], diff[1])
+        weigh_y(fresh[2][:], stay[2][:], whole_y[2])
+        weigh_states(1, 1)
+        weigh_states(1, 0)
+        add(1, 1)
+        nc.vector.tensor_tensor(state[1][:].indirect(trk_half[0]), two(kept[1])[0], two(fresh[1])[0], ALU.add)
+        nc.scalar.activation(state[1][:].indirect(trk_half[1]), two(kept[1])[1], ACT.Copy)
         nc.sync.dma_start(by_tile[:, 1, :, :], quarters(1))
         store(1)
-        weigh(2, diff2_second[:])
-
         for h in range(2):
-            look_up_states(3, h)
-        copy_y(3, stay[2][0])
-        turned3 = add_turned(3, stay[2][0])
-        look_up_all(picked3[:], var[3])
-        diff3_second = turn_back(3, turned3, by_tile[:, 2, 1, :])
+            weigh_states(2, h)
+        add(2, 0)
+        add(2, 1)
         for h in range(2):
-            root(roots3[h], two(picked3)[h])
-        square(3, roots3)
-
-        scatter(2, halves[0], diff[2])
-        differ(3, 0)
-        scatter(2, halves[1], diff[2])
-        nc.sync.dma_start(by_tile[:, 2, 2, :], quarters(2)[:, 2, :])
+            weigh_y(two(fresh[3])[h], two(stay[3])[h], neg_y[3][h])
+        nc.scalar.activation(state[2][:].indirect(trk_sb[:]), kept[2][:], ACT.Copy)
         store(2)
-        weigh(3, diff3_second[:])
-        nc.vector.tensor_copy(by_tile[:, 2, 0:2, :], quarters(2)[:, 0:2, :])
-
-        woven = placed([P, U, PACK], BF16, "woven", -1)
-
-        woven_walk = woven[:].rearrange("p (q c i) t -> p q c t i", q=4, i=WALK)
-        planes_walk = planes[:].rearrange("p (q t c i) -> p q c t i", q=4, t=PACK, i=WALK)
-
-        nc.scalar.copy(woven_walk[:, 3, :, 0:2, :], planes_walk[:, 3, :, 0:2, :])
-        nc.scalar.copy(woven[:, 3 * QUARTER :, 2], quarters(2)[:, 3, :])
-        nc.scalar.copy(woven_walk[:, 0:2, 2:, 0:3, :], planes_walk[:, 0:2, 2:, 0:3, :])
-        nc.scalar.copy(woven_walk[:, 0:2, :2], planes_walk[:, 0:2, :2])
-        nc.scalar.copy(woven_walk[:, 2, :, 0:3, :], planes_walk[:, 2, :, 0:3, :])
-        scatter(3, whole, diff[3])
+        nc.vector.tensor_tensor(kept[3][:], state[3][:].indirect(trk_sb[:]), stay[3][:], ALU.mult)
+        nc.vector.tensor_tensor(state[3][:].indirect(trk_sb[:]), kept[3][:], fresh[3][:], ALU.add)
         store(3)
-        for cols in pieces(ROUND_EDGES):
-            if cols.stop <= ON_VECTOR:
-                nc.vector.tensor_copy(woven[:, cols, 3], state[3][:, cols])
-            else:
-                nc.scalar.copy(woven[:, cols, 3], state[3][:, cols])
+
+        nc.scalar.copy(by_tile[:, 2, 2:4, :], quarters(2)[:, 2:4, :])
+        nc.scalar.copy(by_tile[:, 2, 0:2, :], quarters(2)[:, 0:2, :])
+        nc.vector.tensor_copy(by_tile[:, 3, 2, :], quarters(3)[:, 2, :])
+        nc.vector.tensor_copy(by_tile[:, 3, 0:2, :], quarters(3)[:, 0:2, :])
+        nc.vector.tensor_copy(by_tile[:, 3, 3, :], quarters(3)[:, 3, :])
+
+        woven = keep.tile([P, U, PACK], BF16, name="woven", align_bytes=64)
+        across = planes[:].rearrange("p (q t c) -> p q c t", q=4, t=PACK)
+
+        def piece(lo, hi):
+            q = lo // QUARTER
+            return woven[:, lo:hi, :], across[:, q, lo - q * QUARTER : hi - q * QUARTER, :]
+
+        nc.vector.tensor_copy(*piece(0, QUARTER))
+        nc.vector.tensor_copy(*piece(QUARTER, 2 * QUARTER))
+        nc.scalar.copy(*piece(2 * QUARTER, 3 * QUARTER))
+        nc.scalar.copy(*piece(3 * QUARTER, 7 * EIGHTH))
+        nc.scalar.copy(*piece(7 * EIGHTH, U))
 
         out_scale = keep.tile([P, U], U8, name="out_scale", align_bytes=64)
         out_codes = keep.tile([P, U], I32, name="out_codes", align_bytes=64)
         out_words = out_1[0].rearrange("p c r -> p (c r)").bitcast(I32)
-        store_up_to = {cols.stop: cols for cols in pieces(STORE_EDGES)}
-        for cols in pieces(QUANT_EDGES):
+        edges = (0, QUARTER, 2 * QUARTER, 3 * QUARTER, 7 * EIGHTH, U)
+        stores = {2 * QUARTER: 0, 3 * QUARTER: 2 * QUARTER, U: 3 * QUARTER}
+        for lo, hi in zip(edges, edges[1:]):
             nc.vector.quantize_mx(
-                out=out_codes[:, cols].bitcast(FP8X4),
-                scales=out_scale[:, cols],
-                in_=woven[:, cols, :].rearrange("p c t -> p (c t)"),
+                out=out_codes[:, lo:hi].bitcast(FP8X4),
+                scales=out_scale[:, lo:hi],
+                in_=woven[:, lo:hi, :].rearrange("p c t -> p (c t)"),
             )
-            if cols.stop in store_up_to:
-                stored = store_up_to[cols.stop]
-                nc.sync.dma_start(out_words[:, stored], out_codes[:, stored])
+            if hi in stores:
+                nc.sync.dma_start(out_words[:, stores[hi] : hi], out_codes[:, stores[hi] : hi])
         for r in range(RUN):
             queue = nc.sync if r % 2 == 0 else nc.scalar
             queue.dma_start(out_2[0, r:SCALE_ROWS:RUN, :].bitcast(I32), out_scale[r:P:QUADRANT, :].bitcast(I32))

@@ -26,6 +26,7 @@ ROW_BYTES = 4 * U
 HALF = S // 2
 QUARTER = U // 4
 EIGHTH = U // 8
+WALK = 4
 
 
 def two(ap):
@@ -96,7 +97,7 @@ def tile_picked_kalman8_none_po_kernel(
         nc.vector.quantize_mx(out=w_codes[:].bitcast(FP8X4), scales=w_scale[:], in_=w_bf[:])
 
         state = {}
-        later = [(var, 2), (state, 0), (var, 3), (state, 1), (state, 2), (state, 3)]
+        later = [(var, 2), (var, 3), (state, 0), (state, 1), (state, 2), (state, 3)]
         for place, (tiles, t) in enumerate(later):
             tiles[t] = placed([P, U], F32, f"later{place}", place)
             nc.sync.dma_start(tiles[t][:], (st_rows if tiles is state else va_rows)[:, t, :])
@@ -123,90 +124,101 @@ def tile_picked_kalman8_none_po_kernel(
         for h in range(2):
             for t in range(2):
                 neg_y[t].append(project(t, slice(h * HALF, (h + 1) * HALF), f"neg_y{t}_{h}"))
-        whole_y = {t: project(t, slice(0, S), f"neg_y{t}") for t in (2, 3)}
-        neg_y[3] = two(whole_y[3])
+        for t in (2, 3):
+            neg_y[t] = project(t, slice(0, S), f"neg_y{t}")
 
-        stay = {t: keep.tile([P, S], F32, name=f"stay{t}") for t in range(PACK)}
+        planes = keep.tile([P, PACK * U], F32, name="planes")
+        by_tile = planes[:].rearrange("p (h t c) -> p t h c", h=2, t=PACK)
+        stay = {t: keep.tile([P, S], F32, name=f"stay{t}") for t in (0, 1)}
+        strip = keep.tile([P, HALF + S], F32, name="strip")
+        stay[3] = strip[:, HALF:]
+        stay[2] = by_tile[:, 2, 0, :]
         picked = keep.tile([P, S], F32, name="picked")
         roots = keep.tile([P, S], F32, name="roots")
         nc.scalar.activation(picked[:], root0[:].indirect(trk_sb[:]), ACT.Copy)
         nc.scalar.square(stay[0][:], picked[:])
 
+        def look_up(t, h):
+            nc.scalar.activation(two(picked)[h], var[t][:].indirect(trk_half[h]), ACT.Copy)
+
         def gain(t):
-            for h in range(2):
-                nc.scalar.activation(two(picked)[h], var[t][:].indirect(trk_half[h]), ACT.Copy)
             for h in range(2):
                 root(two(roots)[h], two(picked)[h])
             for h in range(2):
                 nc.scalar.square(two(stay[t])[h], two(roots)[h])
 
-        for t in range(1, PACK):
-            gain(t)
+        for h in range(2):
+            look_up(1, h)
+        gain(1)
+        look_up(2, 0)
+        nc.vector.tensor_copy(two(picked)[1], var[2][:].indirect(trk_half[1]))
+        gain(2)
+        for h in range(2):
+            look_up(3, h)
+        gain(3)
 
-        kept = {t: keep.tile([P, S], F32, name=f"kept{t}") for t in range(PACK)}
-        fresh = {t: keep.tile([P, S], F32, name=f"fresh{t}") for t in range(2)}
-        fresh[2], fresh[3] = stay[0], stay[2]
+        kept = {t: two(keep.tile([P, S], F32, name=f"kept{t}")) for t in range(2)}
+        new = {t: keep.tile([P, S], F32, name=f"new{t}")[:] for t in range(2)}
+        kept[2] = [strip[:, :HALF], keep.tile([P, HALF], F32, name="kept2")[:]]
+        new[2] = strip[:, :S]
+        kept3 = by_tile[:, 2, 1, :]
+        kept[3] = two(kept3)
+        fresh = [placed([P, S], F32, f"fresh{t}", later.index((var, 2)), across=t)[:] for t in range(2)]
+        fresh = fresh + [stay[1][:], stay[2]]
 
         def weigh_y(out, keeps, neg_part):
             nc.vector.scalar_tensor_tensor(out, keeps, 1.0, neg_part, ALU.subtract, ALU.mult)
 
-        def weigh_states(t, h):
-            nc.vector.tensor_tensor(two(kept[t])[h], state[t][:].indirect(trk_half[h]), two(stay[t])[h], ALU.mult)
+        def weigh_states(t):
+            for h in range(2):
+                window = state[t][:].indirect(trk_half[h])
+                nc.vector.tensor_tensor(kept[t][h], window, two(stay[t])[h], ALU.mult)
 
         def add(t, h):
-            nc.vector.tensor_tensor(two(kept[t])[h], two(kept[t])[h], two(fresh[t])[h], ALU.add)
+            nc.vector.tensor_tensor(two(new[t])[h], kept[t][h], two(fresh[t])[h], ALU.add)
+
+        def scatter(t):
+            nc.scalar.activation(state[t][:].indirect(trk_sb[:]), new[t], ACT.Copy)
 
         def store(t):
             nc.sync.dma_start(out_rows[:, t, :], state[t][:])
 
-        planes = keep.tile([P, PACK * U], F32, name="planes")
-        by_tile = planes[:].rearrange("p (q t c) -> p t q c", q=4, t=PACK)
-
-        def quarters(t):
-            return state[t][:].rearrange("p (q c) -> p q c", q=4)
+        def halves(t):
+            return state[t][:].rearrange("p (h c) -> p h c", h=2)
 
         for h in range(2):
             for t in range(2):
                 weigh_y(two(fresh[t])[h], two(stay[t])[h], neg_y[t][h])
-        for h in range(2):
-            weigh_states(0, h)
-        for h in range(2):
-            add(0, h)
-        nc.scalar.activation(state[0][:].indirect(trk_sb[:]), kept[0][:], ACT.Copy)
-        store(0)
-        nc.sync.dma_start(by_tile[:, 0, :, :], quarters(0))
-        weigh_y(fresh[2][:], stay[2][:], whole_y[2])
-        weigh_states(1, 1)
-        weigh_states(1, 0)
-        add(1, 1)
-        nc.vector.tensor_tensor(state[1][:].indirect(trk_half[0]), two(kept[1])[0], two(fresh[1])[0], ALU.add)
-        nc.scalar.activation(state[1][:].indirect(trk_half[1]), two(kept[1])[1], ACT.Copy)
-        nc.sync.dma_start(by_tile[:, 1, :, :], quarters(1))
-        store(1)
-        for h in range(2):
-            weigh_states(2, h)
+        for t in range(2):
+            weigh_states(t)
+            for h in range(2):
+                add(t, h)
+            scatter(t)
+            nc.sync.dma_start(by_tile[:, t, :, :], halves(t))
+            store(t)
+        weigh_y(fresh[2], stay[2], neg_y[2])
+        weigh_states(2)
         add(2, 0)
+        weigh_y(fresh[3], stay[3], neg_y[3])
+        weigh_states(3)
         add(2, 1)
-        for h in range(2):
-            weigh_y(two(fresh[3])[h], two(stay[3])[h], neg_y[3][h])
-        nc.scalar.activation(state[2][:].indirect(trk_sb[:]), kept[2][:], ACT.Copy)
-        store(2)
-        nc.vector.tensor_tensor(kept[3][:], state[3][:].indirect(trk_sb[:]), stay[3][:], ALU.mult)
-        nc.vector.tensor_tensor(state[3][:].indirect(trk_sb[:]), kept[3][:], fresh[3][:], ALU.add)
+        scatter(2)
+        nc.vector.tensor_tensor(state[3][:].indirect(trk_sb[:]), kept3, fresh[3], ALU.add)
         store(3)
+        store(2)
 
-        nc.scalar.copy(by_tile[:, 2, 2:4, :], quarters(2)[:, 2:4, :])
-        nc.scalar.copy(by_tile[:, 2, 0:2, :], quarters(2)[:, 0:2, :])
-        nc.vector.tensor_copy(by_tile[:, 3, 2, :], quarters(3)[:, 2, :])
-        nc.vector.tensor_copy(by_tile[:, 3, 0:2, :], quarters(3)[:, 0:2, :])
-        nc.vector.tensor_copy(by_tile[:, 3, 3, :], quarters(3)[:, 3, :])
+        nc.vector.tensor_copy(by_tile[:, 3, :, :], halves(3))
+        nc.vector.tensor_copy(by_tile[:, 2, 1, :QUARTER], halves(2)[:, 1, :QUARTER])
+        nc.vector.tensor_copy(by_tile[:, 2, 0, :], halves(2)[:, 0, :])
+        nc.vector.tensor_copy(by_tile[:, 2, 1, QUARTER:], halves(2)[:, 1, QUARTER:])
 
         woven = keep.tile([P, U, PACK], BF16, name="woven", align_bytes=64)
-        across = planes[:].rearrange("p (q t c) -> p q c t", q=4, t=PACK)
+        across = planes[:].rearrange("p (h t c i) -> p h c t i", h=2, t=PACK, i=WALK)
 
         def piece(lo, hi):
-            q = lo // QUARTER
-            return woven[:, lo:hi, :], across[:, q, lo - q * QUARTER : hi - q * QUARTER, :]
+            h = lo // (U // 2)
+            lines = slice((lo - h * U // 2) // WALK, (hi - h * U // 2) // WALK)
+            return woven[:, lo:hi, :].rearrange("p (c i) t -> p c t i", i=WALK), across[:, h, lines, :, :]
 
         nc.vector.tensor_copy(*piece(0, QUARTER))
         nc.vector.tensor_copy(*piece(QUARTER, 2 * QUARTER))

@@ -26,6 +26,7 @@ ROW_BYTES = 4 * U
 HALF = S // 2
 QUARTER = U // 4
 EIGHTH = U // 8
+ALIGN = 256
 WALK = 4
 
 
@@ -49,16 +50,16 @@ def tile_picked_kalman8_none_po_kernel(
 
         def placed(shape, dtype, name, place, across=0):
             offset = place * ROW_BYTES + across * ROW_BYTES // 2
-            return shared.tile(shape, dtype, name=name, offset=offset, align_bytes=64)
+            return shared.tile(shape, dtype, name=name, offset=offset, align_bytes=ALIGN)
 
         trk_sb = keep.tile([P, S // GROUP], U16, name="trk_sb")
         offs_sb = keep.tile([P, S // GROUP], U16, name="offs_sb")
-        x_table = keep.tile([P, T], I32, name="x_table", align_bytes=64)
-        scale_table = keep.tile([P, T], U8, name="scale_table", align_bytes=64)
+        x_table = keep.tile([P, T], I32, name="x_table", align_bytes=ALIGN)
+        scale_table = keep.tile([P, T], U8, name="scale_table", align_bytes=ALIGN)
         w_raw = [placed([P, 2, N], F32, f"w_raw{h}", 2 * h, across=1) for h in range(2)]
         w_bf = placed([P, N * PACK], BF16, "w_bf", 4, across=1)
-        var = {0: keep.tile([P, U], F32, name="var0", tag="var0", align_bytes=64)}
-        var[1] = keep.tile([P, U], F32, name="var1")
+        var = {0: keep.tile([P, U], F32, name="var0", tag="var0", align_bytes=ALIGN)}
+        var[1] = keep.tile([P, U], F32, name="var1", align_bytes=ALIGN)
 
         nc.vector.memset(scale_table[:].bitcast(I32), 0)
         nc.sync.dma_start(var[0][:], va_rows[:, 0, :])
@@ -79,9 +80,9 @@ def tile_picked_kalman8_none_po_kernel(
         root0 = keep.tile([P, U], F32, name="root0")
         root(root0[:], var[0][:])
 
-        picked_scale = keep.tile([P, S], U8, name="picked_scale", align_bytes=64)
+        picked_scale = keep.tile([P, S], U8, name="picked_scale", align_bytes=ALIGN)
         nc.vector.tensor_copy(picked_scale[:], scale_table[:].indirect(offs_sb[:]))
-        x_scale = keep.tile([P, S], U8, name="x_scale", tag="var0", align_bytes=64)
+        x_scale = keep.tile([P, S], U8, name="x_scale", tag="var0", align_bytes=ALIGN)
         nc.vector.memset(x_scale[:].bitcast(I32), 0)
         for r in range(RUN):
             nc.scalar.dma_start(
@@ -92,8 +93,8 @@ def tile_picked_kalman8_none_po_kernel(
         for h in range(2):
             w_half = w_raw[h][:].rearrange("p j (m t) -> p m t j", t=PACK)
             nc.vector.tensor_scalar(w_dealt[:, :, :, 2 * h : 2 * h + 2], w_half, -1.0, None, ALU.mult)
-        w_codes = keep.tile([P, N], U32, name="w_codes", align_bytes=64)
-        w_scale = keep.tile([P, N], U8, name="w_scale", align_bytes=64)
+        w_codes = keep.tile([P, N], U32, name="w_codes", align_bytes=ALIGN)
+        w_scale = keep.tile([P, N], U8, name="w_scale", align_bytes=ALIGN)
         nc.vector.quantize_mx(out=w_codes[:].bitcast(FP8X4), scales=w_scale[:], in_=w_bf[:])
 
         state = {}
@@ -102,7 +103,7 @@ def tile_picked_kalman8_none_po_kernel(
             tiles[t] = placed([P, U], F32, f"later{place}", place)
             nc.sync.dma_start(tiles[t][:], (st_rows if tiles is state else va_rows)[:, t, :])
 
-        x_codes = keep.tile([P, S], U32, name="x_codes", align_bytes=64)
+        x_codes = keep.tile([P, S], U32, name="x_codes", align_bytes=ALIGN)
         for out, columns in zip(two(x_codes), half_columns):
             nc.vector.tensor_copy(out, x_table[:].bitcast(U32).indirect(offs_sb[:, columns]))
 
@@ -127,7 +128,7 @@ def tile_picked_kalman8_none_po_kernel(
         for t in (2, 3):
             neg_y[t] = project(t, slice(0, S), f"neg_y{t}")
 
-        planes = keep.tile([P, PACK * U], F32, name="planes")
+        planes = keep.tile([P, PACK * U], F32, name="planes", align_bytes=ALIGN)
         by_tile = planes[:].rearrange("p (h t c) -> p t h c", h=2, t=PACK)
         stay = {t: keep.tile([P, S], F32, name=f"stay{t}") for t in (0, 1)}
         strip = keep.tile([P, HALF + S], F32, name="strip")
@@ -212,7 +213,7 @@ def tile_picked_kalman8_none_po_kernel(
         nc.vector.tensor_copy(by_tile[:, 2, 0, :], halves(2)[:, 0, :])
         nc.vector.tensor_copy(by_tile[:, 2, 1, QUARTER:], halves(2)[:, 1, QUARTER:])
 
-        woven = keep.tile([P, U, PACK], BF16, name="woven", align_bytes=64)
+        woven = keep.tile([P, U, PACK], BF16, name="woven", align_bytes=ALIGN)
         across = planes[:].rearrange("p (h t c i) -> p h c t i", h=2, t=PACK, i=WALK)
 
         def piece(lo, hi):
@@ -226,8 +227,8 @@ def tile_picked_kalman8_none_po_kernel(
         nc.scalar.copy(*piece(3 * QUARTER, 7 * EIGHTH))
         nc.scalar.copy(*piece(7 * EIGHTH, U))
 
-        out_scale = keep.tile([P, U], U8, name="out_scale", align_bytes=64)
-        out_codes = keep.tile([P, U], I32, name="out_codes", align_bytes=64)
+        out_scale = keep.tile([P, U], U8, name="out_scale", align_bytes=ALIGN)
+        out_codes = keep.tile([P, U], I32, name="out_codes", align_bytes=ALIGN)
         out_words = out_1[0].rearrange("p c r -> p (c r)").bitcast(I32)
         edges = (0, QUARTER, 2 * QUARTER, 3 * QUARTER, 7 * EIGHTH, U)
         stores = {2 * QUARTER: 0, 3 * QUARTER: 2 * QUARTER, U: 3 * QUARTER}

@@ -231,7 +231,7 @@ def tile_picked_kalman8_none_po_kernel(
         out_codes = keep.tile([P, U], I32, name="out_codes", align_bytes=ALIGN)
         out_words = out_1[0].rearrange("p c r -> p (c r)").bitcast(I32)
         edges = (0, QUARTER, 2 * QUARTER, 3 * QUARTER, 7 * EIGHTH, U)
-        stores = {2 * QUARTER: 0, 3 * QUARTER: 2 * QUARTER, U: 3 * QUARTER}
+        stores = {hi: hi - QUARTER for hi in range(QUARTER, U + 1, QUARTER)}
         for lo, hi in zip(edges, edges[1:]):
             nc.vector.quantize_mx(
                 out=out_codes[:, lo:hi].bitcast(FP8X4),

@@ -27,7 +27,7 @@ HALF = S // 2
 QUARTER = U // 4
 EIGHTH = U // 8
 ALIGN = 256
-WALK = 4
+WALK = 2
 
 
 def two(ap):

@@ -26,6 +26,7 @@ ROW_BYTES = 4 * U
 HALF = S // 2
 QUARTER = U // 4
 EIGHTH = U // 8
+ON_VECTOR = 544
 ALIGN = 256
 WALK = 2
 
@@ -129,11 +130,11 @@ def tile_picked_kalman8_none_po_kernel(
             neg_y[t] = project(t, slice(0, S), f"neg_y{t}")
 
         planes = keep.tile([P, PACK * U], F32, name="planes", align_bytes=ALIGN)
-        by_tile = planes[:].rearrange("p (h t c) -> p t h c", h=2, t=PACK)
+        by_tile = planes[:].rearrange("p (q t c) -> p t q c", q=4, t=PACK)
         stay = {t: keep.tile([P, S], F32, name=f"stay{t}") for t in (0, 1)}
         strip = keep.tile([P, HALF + S], F32, name="strip")
         stay[3] = strip[:, HALF:]
-        stay[2] = by_tile[:, 2, 0, :]
+        stay[2] = planes[:, 2 * QUARTER : U]
         picked = keep.tile([P, S], F32, name="picked")
         roots = keep.tile([P, S], F32, name="roots")
         nc.scalar.activation(picked[:], root0[:].indirect(trk_sb[:]), ACT.Copy)
@@ -148,8 +149,7 @@ def tile_picked_kalman8_none_po_kernel(
             for h in range(2):
                 nc.scalar.square(two(stay[t])[h], two(roots)[h])
 
-        for h in range(2):
-            look_up(1, h)
+        nc.scalar.activation(picked[:], var[1][:].indirect(trk_sb[:]), ACT.Copy)
         gain(1)
         look_up(2, 0)
         nc.vector.tensor_copy(two(picked)[1], var[2][:].indirect(trk_half[1]))
@@ -162,7 +162,7 @@ def tile_picked_kalman8_none_po_kernel(
         new = {t: keep.tile([P, S], F32, name=f"new{t}")[:] for t in range(2)}
         kept[2] = [strip[:, :HALF], keep.tile([P, HALF], F32, name="kept2")[:]]
         new[2] = strip[:, :S]
-        kept3 = by_tile[:, 2, 1, :]
+        kept3 = planes[:, 2 * U + 2 * QUARTER : 3 * U]
         kept[3] = two(kept3)
         fresh = [placed([P, S], F32, f"fresh{t}", later.index((var, 2)), across=t)[:] for t in range(2)]
         fresh = fresh + [stay[1][:], stay[2]]
@@ -184,8 +184,8 @@ def tile_picked_kalman8_none_po_kernel(
         def store(t):
             nc.sync.dma_start(out_rows[:, t, :], state[t][:])
 
-        def halves(t):
-            return state[t][:].rearrange("p (h c) -> p h c", h=2)
+        def quarters(t):
+            return state[t][:].rearrange("p (q c) -> p q c", q=4)
 
         for h in range(2):
             for t in range(2):
@@ -195,7 +195,7 @@ def tile_picked_kalman8_none_po_kernel(
             for h in range(2):
                 add(t, h)
             scatter(t)
-            nc.sync.dma_start(by_tile[:, t, :, :], halves(t))
+            nc.sync.dma_start(by_tile[:, t, :, :], quarters(t))
             store(t)
         weigh_y(fresh[2], stay[2], neg_y[2])
         weigh_states(2)
@@ -208,22 +208,24 @@ def tile_picked_kalman8_none_po_kernel(
         store(3)
         store(2)
 
-        nc.vector.tensor_copy(by_tile[:, 3, :, :], halves(3))
-        nc.vector.tensor_copy(by_tile[:, 2, 1, :QUARTER], halves(2)[:, 1, :QUARTER])
-        nc.vector.tensor_copy(by_tile[:, 2, 0, :], halves(2)[:, 0, :])
-        nc.vector.tensor_copy(by_tile[:, 2, 1, QUARTER:], halves(2)[:, 1, QUARTER:])
+        nc.vector.tensor_copy(by_tile[:, 3, :, :], quarters(3))
+        nc.vector.tensor_copy(by_tile[:, 2, 2, :], quarters(2)[:, 2, :])
+        for q in range(2):
+            nc.vector.tensor_copy(by_tile[:, 2, q, :], quarters(2)[:, q, :])
+        nc.scalar.copy(by_tile[:, 2, 3, :], quarters(2)[:, 3, :])
 
         woven = keep.tile([P, U, PACK], BF16, name="woven", align_bytes=ALIGN)
-        across = planes[:].rearrange("p (h t c i) -> p h c t i", h=2, t=PACK, i=WALK)
+        across = planes[:].rearrange("p (q t c i) -> p q c t i", q=4, t=PACK, i=WALK)
 
         def piece(lo, hi):
-            h = lo // (U // 2)
-            lines = slice((lo - h * U // 2) // WALK, (hi - h * U // 2) // WALK)
-            return woven[:, lo:hi, :].rearrange("p (c i) t -> p c t i", i=WALK), across[:, h, lines, :, :]
+            q = lo // QUARTER
+            lines = slice((lo - q * QUARTER) // WALK, (hi - q * QUARTER) // WALK)
+            return woven[:, lo:hi, :].rearrange("p (c i) t -> p c t i", i=WALK), across[:, q, lines, :, :]
 
         nc.vector.tensor_copy(*piece(0, QUARTER))
         nc.vector.tensor_copy(*piece(QUARTER, 2 * QUARTER))
-        nc.scalar.copy(*piece(2 * QUARTER, 3 * QUARTER))
+        nc.vector.tensor_copy(*piece(2 * QUARTER, ON_VECTOR))
+        nc.scalar.copy(*piece(ON_VECTOR, 3 * QUARTER))
         nc.scalar.copy(*piece(3 * QUARTER, 7 * EIGHTH))
         nc.scalar.copy(*piece(7 * EIGHTH, U))
 

from contextlib import ExitStack

import concourse.mybir as mybir

K, T, S, N, U = 512, 2048, 512, 512, 1024
FLOPS = 2 * K * S * N

F32 = mybir.dt.float32
BF16 = mybir.dt.bfloat16
I32 = mybir.dt.int32
U32 = mybir.dt.uint32
U16 = mybir.dt.uint16
U8 = mybir.dt.uint8
FP8X4 = mybir.dt.float8_e4m3fn_x4
ALU = mybir.AluOpType
ACT = mybir.ActivationFunctionType

P = 128
PACK = 4
GROUP = 16
QUADRANT = 32
SCALE_ROWS = 16
RUN = SCALE_ROWS * QUADRANT // P
SPREAD = P // SCALE_ROWS
ROW_BYTES = 4 * U
HALF = S // 2
QUARTER = U // 4
EIGHTH = U // 8
ON_VECTOR = 544
ALIGN = 256
WALK = 2


def two(ap):
    return [ap[:, :HALF], ap[:, HALF:S]]


def tile_picked_kalman8_none_po_kernel(
    tc, x_words, x_scales, w1, st, va, offs, trk, out_0, out_1, out_2
):
    nc = tc.nc
    st_rows = st.rearrange("(p t) u -> p t u", t=PACK)
    va_rows = va.rearrange("(p t) u -> p t u", t=PACK)
    w_rows = w1.rearrange("(p j) c -> p j c", j=PACK)
    out_rows = out_0.rearrange("(p t) u -> p t u", t=PACK)

    with ExitStack() as ctx:
        keep = ctx.enter_context(tc.tile_pool(name="keep", bufs=1))
        shared = ctx.enter_context(tc.tile_pool(name="shared", bufs=1))
        psum = ctx.enter_context(tc.psum_pool(name="psum", bufs=1))

        def placed(shape, dtype, name, place, across=0):
            offset = place * ROW_BYTES + across * ROW_BYTES // 2
            return shared.tile(shape, dtype, name=name, offset=offset, align_bytes=ALIGN)

        trk_sb = keep.tile([P, S // GROUP], U16, name="trk_sb")
        offs_sb = keep.tile([P, S // GROUP], U16, name="offs_sb")
        x_table = keep.tile([P, T], I32, name="x_table", align_bytes=ALIGN)
        scale_table = keep.tile([P, T], U8, name="scale_table", align_bytes=ALIGN)
        w_raw = [placed([P, 2, N], F32, f"w_raw{h}", 2 * h, across=1) for h in range(2)]
        w_bf = placed([P, N * PACK], BF16, "w_bf", 4, across=1)
        var = {0: keep.tile([P, U], F32, name="var0", tag="var0", align_bytes=ALIGN)}
        var[1] = keep.tile([P, U], F32, name="var1", align_bytes=ALIGN)

        nc.vector.memset(scale_table[:].bitcast(I32), 0)
        nc.sync.dma_start(var[0][:], va_rows[:, 0, :])
        nc.sync.dma_start(offs_sb[:], offs)
        nc.sync.dma_start(trk_sb[:], trk)
        nc.sync.dma_start(scale_table[0:P:SPREAD, :].bitcast(I32), x_scales[0].bitcast(I32))
        for h in range(2):
            nc.sync.dma_start(w_raw[h][:], w_rows[:, 2 * h : 2 * h + 2, :])
        nc.sync.dma_start(var[1][:], va_rows[:, 1, :])
        nc.sync.dma_start(x_table[:], x_words[0].rearrange("p c r -> p (c r)").bitcast(I32))

        half_columns = [slice(h * HALF // GROUP, (h + 1) * HALF // GROUP) for h in range(2)]
        trk_half = [trk_sb[:, cols] for cols in half_columns]

        def root(out, in_):
            nc.scalar.activation(out, in_, ACT.Abs_reciprocal_sqrt, bias=1.0, scale=2.0)

        root0 = keep.tile([P, U], F32, name="root0")
        root(root0[:], var[0][:])

        picked_scale = keep.tile([P, S], U8, name="picked_scale", align_bytes=ALIGN)
        nc.vector.tensor_copy(picked_scale[:], scale_table[:].indirect(offs_sb[:]))
        x_scale = keep.tile([P, S], U8, name="x_scale", tag="var0", align_bytes=ALIGN)
        nc.vector.memset(x_scale[:].bitcast(I32), 0)
        for r in range(RUN):
            nc.scalar.dma_start(
                x_scale[r:P:QUADRANT, :].bitcast(I32), picked_scale[SPREAD * r : P : QUADRANT, :].bitcast(I32)
            )

        w_dealt = w_bf[:].rearrange("p (t m j) -> p m t j", t=PACK, j=PACK)
        for h in range(2):
            w_half = w_raw[h][:].rearrange("p j (m t) -> p m t j", t=PACK)
            nc.vector.tensor_scalar(w_dealt[:, :, :, 2 * h : 2 * h + 2], w_half, -1.0, None, ALU.mult)
        w_codes = keep.tile([P, N], U32, name="w_codes", align_bytes=ALIGN)
        w_scale = keep.tile([P, N], U8, name="w_scale", align_bytes=ALIGN)
        nc.vector.quantize_mx(out=w_codes[:].bitcast(FP8X4), scales=w_scale[:], in_=w_bf[:])

        state = {}
        later = [(var, 2), (var, 3), (state, 0), (state, 1), (state, 2), (state, 3)]
        for place, (tiles, t) in enumerate(later):
            tiles[t] = placed([P, U], F32, f"later{place}", place)
            nc.sync.dma_start(tiles[t][:], (st_rows if tiles is state else va_rows)[:, t, :])

        x_codes = keep.tile([P, S], U32, name="x_codes", align_bytes=ALIGN)
        for out, columns in zip(two(x_codes), half_columns):
            nc.vector.tensor_copy(out, x_table[:].bitcast(U32).indirect(offs_sb[:, columns]))

        def project(t, entries, name):
            bank = psum.tile([P, entries.stop - entries.start], F32, name=name)
            cols = slice(t * P, (t + 1) * P)
            nc.tensor.matmul_mx(
                out=bank[:],
                lhsT=w_codes[:, cols].bitcast(FP8X4),
                lhsT_scale=w_scale[:, cols],
                rhs=x_codes[:, entries].bitcast(FP8X4),
                rhs_scale=x_scale[:, entries],
                start=True,
                stop=True,
            )
            return bank[:]

        neg_y = {0: [], 1: []}
        for h in range(2):
            for t in range(2):
                neg_y[t].append(project(t, slice(h * HALF, (h + 1) * HALF), f"neg_y{t}_{h}"))
        for t in (2, 3):
            neg_y[t] = project(t, slice(0, S), f"neg_y{t}")

        planes = keep.tile([P, PACK * U], F32, name="planes", align_bytes=ALIGN)
        by_tile = planes[:].rearrange("p (q t c) -> p t q c", q=4, t=PACK)
        stay = {t: keep.tile([P, S], F32, name=f"stay{t}") for t in (0, 1)}
        strip = keep.tile([P, HALF + S], F32, name="strip")
        stay[3] = strip[:, HALF:]
        stay[2] = planes[:, 2 * QUARTER : U]
        picked = keep.tile([P, S], F32, name="picked")
        roots = keep.tile([P, S], F32, name="roots")
        nc.scalar.activation(picked[:], root0[:].indirect(trk_sb[:]), ACT.Copy)
        nc.scalar.square(stay[0][:], picked[:])

        def look_up(t, h):
            nc.scalar.activation(two(picked)[h], var[t][:].indirect(trk_half[h]), ACT.Copy)

        def gain(t):
            for h in range(2):
                root(two(roots)[h], two(picked)[h])
            for h in range(2):
                nc.scalar.square(two(stay[t])[h], two(roots)[h])

        nc.scalar.activation(picked[:], var[1][:].indirect(trk_sb[:]), ACT.Copy)
        gain(1)
        look_up(2, 0)
        nc.vector.tensor_copy(two(picked)[1], var[2][:].indirect(trk_half[1]))
        gain(2)
        for h in range(2):
            look_up(3, h)
        gain(3)

        kept = {t: two(keep.tile([P, S], F32, name=f"kept{t}")) for t in range(2)}
        new = {t: keep.tile([P, S], F32, name=f"new{t}")[:] for t in range(2)}
        kept[2] = [strip[:, :HALF], keep.tile([P, HALF], F32, name="kept2")[:]]
        new[2] = strip[:, :S]
        kept3 = planes[:, 2 * U + 2 * QUARTER : 3 * U]
        kept[3] = two(kept3)
        fresh = [placed([P, S], F32, f"fresh{t}", later.index((var, 2)), across=t)[:] for t in range(2)]
        fresh = fresh + [stay[1][:], stay[2]]

        def weigh_y(out, keeps, neg_part):
            nc.vector.scalar_tensor_tensor(out, keeps, 1.0, neg_part, ALU.subtract, ALU.mult)

        def weigh_states(t):
            for h in range(2):
                window = state[t][:].indirect(trk_half[h])
                nc.vector.tensor_tensor(kept[t][h], window, two(stay[t])[h], ALU.mult)

        def add(t, h):
            nc.vector.tensor_tensor(two(new[t])[h], kept[t][h], two(fresh[t])[h], ALU.add)

        def scatter(t):
            nc.scalar.activation(state[t][:].indirect(trk_sb[:]), new[t], ACT.Copy)

        def store(t):
            nc.sync.dma_start(out_rows[:, t, :], state[t][:])

        def quarters(t):
            return state[t][:].rearrange("p (q c) -> p q c", q=4)

        for h in range(2):
            for t in range(2):
                weigh_y(two(fresh[t])[h], two(stay[t])[h], neg_y[t][h])
        for t in range(2):
            weigh_states(t)
            for h in range(2):
                add(t, h)
            scatter(t)
            nc.sync.dma_start(by_tile[:, t, :, :], quarters(t))
            store(t)
        weigh_y(fresh[2], stay[2], neg_y[2])
        weigh_states(2)
        add(2, 0)
        weigh_y(fresh[3], stay[3], neg_y[3])
        weigh_states(3)
        add(2, 1)
        scatter(2)
        nc.vector.tensor_tensor(state[3][:].indirect(trk_sb[:]), kept3, fresh[3], ALU.add)
        store(3)
        store(2)

        nc.vector.tensor_copy(by_tile[:, 3, :, :], quarters(3))
        nc.vector.tensor_copy(by_tile[:, 2, 2, :], quarters(2)[:, 2, :])
        for q in range(2):
            nc.vector.tensor_copy(by_tile[:, 2, q, :], quarters(2)[:, q, :])
        nc.scalar.copy(by_tile[:, 2, 3, :], quarters(2)[:, 3, :])

        woven = keep.tile([P, U, PACK], BF16, name="woven", align_bytes=ALIGN)
        across = planes[:].rearrange("p (q t c i) -> p q c t i", q=4, t=PACK, i=WALK)

        def piece(lo, hi):
            q = lo // QUARTER
            lines = slice((lo - q * QUARTER) // WALK, (hi - q * QUARTER) // WALK)
            return woven[:, lo:hi, :].rearrange("p (c i) t -> p c t i", i=WALK), across[:, q, lines, :, :]

        nc.vector.tensor_copy(*piece(0, QUARTER))
        nc.vector.tensor_copy(*piece(QUARTER, 2 * QUARTER))
        nc.vector.tensor_copy(*piece(2 * QUARTER, ON_VECTOR))
        nc.scalar.copy(*piece(ON_VECTOR, 3 * QUARTER))
        nc.scalar.copy(*piece(3 * QUARTER, 7 * EIGHTH))
        nc.scalar.copy(*piece(7 * EIGHTH, U))

        out_scale = keep.tile([P, U], U8, name="out_scale", align_bytes=ALIGN)
        out_codes = keep.tile([P, U], I32, name="out_codes", align_bytes=ALIGN)
        out_words = out_1[0].rearrange("p c r -> p (c r)").bitcast(I32)
        edges = (0, QUARTER, 2 * QUARTER, 3 * QUARTER, 7 * EIGHTH, U)
        stores = {hi: hi - QUARTER for hi in range(QUARTER, U + 1, QUARTER)}
        for lo, hi in zip(edges, edges[1:]):
            nc.vector.quantize_mx(
                out=out_codes[:, lo:hi].bitcast(FP8X4),
                scales=out_scale[:, lo:hi],
                in_=woven[:, lo:hi, :].rearrange("p c t -> p (c t)"),
            )
            if hi in stores:
                nc.sync.dma_start(out_words[:, stores[hi] : hi], out_codes[:, stores[hi] : hi])
        for r in range(RUN):
            queue = nc.sync if r % 2 == 0 else nc.scalar
            queue.dma_start(out_2[0, r:SCALE_ROWS:RUN, :].bitcast(I32), out_scale[r:P:QUADRANT, :].bitcast(I32))
